import numpy as np
import ml_dtypes


def mxq(x, axis, fmt="e4m3"):
    dtype, down = {"e4m3": (ml_dtypes.float8_e4m3fn, 7), "e5m2": (ml_dtypes.float8_e5m2, 14)}[fmt]
    v = np.moveaxis(np.asarray(x, np.float32).astype(ml_dtypes.bfloat16).astype(np.float64), axis, -1)
    blocks = v.reshape(v.shape[:-1] + (-1, 32))
    amax = np.abs(blocks).max(-1, keepdims=True)
    byte = np.maximum(np.where(amax > 0, np.frexp(amax)[1] - 1 + 127, 0) - down, 1)
    scale = np.exp2(byte - 127.0)
    codes = (blocks / scale).astype(np.float32).astype(dtype).astype(np.float64)
    return np.moveaxis((codes * scale).reshape(v.shape), -1, axis)


WIDE = False


def mx_kscale(k):
    if not WIDE:
        return np.ones(k)
    levels = np.array([10, -10, 5, -5, 0])
    if k % 512:
        return np.exp2(np.random.permutation(np.resize(levels, k // 32))).repeat(32)
    a = np.empty((k // 512, 16))
    for p in range(k // 512):
        a[p, :8] = np.random.permutation(np.resize(levels, 8))
        for g in range(8):
            far = levels[np.abs(levels - a[p, g]) >= 10]
            a[p, g + 8] = far[np.random.randint(len(far))]
    return np.exp2(a.ravel()).repeat(32)


def f64(x):
    return np.asarray(x).astype(np.float64)


def striped(idx):
    return np.tile(idx.reshape(-1, 16).T, (8, 1)).astype(np.uint16)


def unstriped(offs):
    return offs[:16].T.reshape(-1).astype(np.int64)


E2M1 = np.array([0.0, 0.5, 1.0, 1.5, 2.0, 3.0, 4.0, 6.0, -0.0, -0.5, -1.0, -1.5, -2.0, -3.0, -4.0, -6.0])


def pack_weight(w, fmt):
    k, n = w.shape
    w = f64(np.asarray(w, np.float32).astype(ml_dtypes.bfloat16)).reshape(k // 32, 32, n)
    amax = np.abs(w).max(1)
    if fmt == "e4m3":
        byte = np.frexp(amax)[1] - 1 + 127 - 7
    else:
        mant, ex = np.frexp(amax / 6.0)
        byte = np.where(mant > 0.5, ex, ex - 1) + 127
    byte = np.clip(np.where(amax > 0, byte, 1), 1, 254)
    scaled = (w * np.exp2(127.0 - byte)[:, None, :]).reshape(k, n).astype(np.float32)
    by_word = np.ascontiguousarray(scaled.reshape(k // 512, 128, 4, n).transpose(0, 1, 3, 2))
    if fmt == "e4m3":
        words = by_word.astype(ml_dtypes.float8_e4m3fn).view(np.uint8)
    else:
        c = by_word.astype(ml_dtypes.float4_e2m1fn).view(np.uint8) & 0xF
        words = (c[..., 0::2] | (c[..., 1::2] << 4)).reshape(k // 512, 128, 2 * n)
    return np.ascontiguousarray(words), np.ascontiguousarray(byte.astype(np.uint8).reshape(k // 512, 16, n))


def unpack_weight(words, scales, fmt):
    g, _, n = scales.shape
    words = np.ascontiguousarray(words).reshape(g, 128, n, -1)
    if fmt == "e4m3":
        vals = words.view(ml_dtypes.float8_e4m3fn).astype(np.float64)
    else:
        nib = np.empty((g, 128, n, 4), np.uint8)
        nib[..., 0::2] = words & 0xF
        nib[..., 1::2] = words >> 4
        vals = E2M1[nib]
    vals = vals * np.repeat(np.exp2(scales.astype(np.float64) - 127.0), 8, axis=1)[..., None]
    return vals.transpose(0, 1, 3, 2).reshape(g * 512, n)


def gelu(v):
    return 0.5 * v * (1.0 + np.tanh(np.sqrt(2.0 / np.pi) * (v + 0.044715 * v**3)))


def striped8(idx):
    return np.concatenate([v.reshape(-1, 16).T for v in idx]).astype(np.uint16)


def unstriped8(offs):
    return np.stack([offs[16 * g:16 * g + 16].T.reshape(-1) for g in range(8)]).astype(np.int64)


def heads(h, wgt, idx8):
    r = np.arange(h.shape[0])
    return wgt[r // 4 % 128] * h[r[:, None], idx8[r % 512 // 64]]


def bf(x):
    return np.asarray(x, np.float32).astype(ml_dtypes.bfloat16)


def planes(Y):
    n, m = Y.shape
    b = f64(bf(Y)).reshape(n // 32, 32, m)
    amax = np.abs(b).max(1)
    byte = np.clip(np.where(amax > 0, np.frexp(amax)[1] - 1 + 127 - 7, 1), 1, 254)
    codes = (b * np.exp2(127.0 - byte)[:, None, :]).reshape(n, m).astype(np.float32).astype(ml_dtypes.float8_e4m3fn).view(np.uint8)
    words = codes.reshape(n // 512, 128, 4, m).transpose(0, 1, 3, 2)
    return np.ascontiguousarray(words), np.ascontiguousarray(byte.astype(np.uint8).reshape(n // 512, 16, m))


K, H, N, T, S, P = 1024, 1024, 1024, 2048, 1024, 512

def setup_inputs():
    n = np.random.standard_normal
    s = mx_kscale(K)[:, None]
    u = mx_kscale(H)[:, None]
    tab_words, tab_scales = pack_weight(n((K, T)) * s, "e4m3")
    w4_words, w4_scales = pack_weight(n((K, H)) / np.sqrt(K) / s, "e2m1")
    ws = 1.5 * n((H, N)) / np.sqrt(H) * np.exp(0.8 * n(N)) / u
    ws_words, ws_scales = pack_weight(ws, "e4m3")
    lists = np.stack([np.random.permutation(S)[:P] for _ in range(8)])
    wgt = np.repeat(np.random.uniform(0.5, 2.0, (8, P)), 16, axis=0)
    return {
        "tab_words": tab_words, "tab_scales": tab_scales,
        "offs": striped(np.random.permutation(T)[:S]),
        "w4_words": w4_words, "w4_scales": w4_scales,
        "offs2": striped8(lists),
        "wgt": wgt.astype(np.float32),
        "noise": (n((K, P)) * s).astype(np.float32),
        "wn": (n((K, H)) / np.sqrt(K) / s).astype(np.float32),
        "mix": (n((H, P)) * u).astype(np.float32),
        "ws_words": ws_words, "ws_scales": ws_scales,
    }

def reference(tab_words, tab_scales, offs, w4_words, w4_scales, offs2, wgt, noise, wn, mix, ws_words, ws_scales):
    v = unpack_weight(tab_words, tab_scales, "e4m3")[:, unstriped(offs)]
    w4 = unpack_weight(w4_words, w4_scales, "e2m1")
    h = w4.T @ v
    x = heads(h, f64(wgt), unstriped8(offs2))
    d = mxq(f64(wn), 0, "e4m3").T @ mxq(f64(noise), 0, "e4m3")
    x2 = np.square(x)
    mask = x2 / (x2 + np.square(d) + 0.2)
    z = mask * f64(mix)
    ws = unpack_weight(ws_words, ws_scales, "e4m3")
    y = ws.T @ mxq(z, 0, "e4m3")
    words, scales = planes(y)
    return y, words, scales

@@ -1,0 +1,344 @@
+from contextlib import ExitStack
+
+import concourse.mybir as mybir
+
+K, H, N, T, S, M = 1024, 1024, 1024, 2048, 1024, 512
+P = 128
+FLOPS = 2 * K * H * S + 2 * K * H * M + 2 * H * N * M
+
+F32 = mybir.dt.float32
+BF16 = mybir.dt.bfloat16
+I32 = mybir.dt.int32
+U32 = mybir.dt.uint32
+U16 = mybir.dt.uint16
+U8 = mybir.dt.uint8
+E4M3 = mybir.dt.float8_e4m3fn_x4
+E2M1 = mybir.dt.float4_e2m1fn_x4
+ACT = mybir.ActivationFunctionType
+ALU = mybir.AluOpType
+
+CHUNKS = [256,256]
+
+
+def tile_list_ratio_mask_synthesis_kernel(
+    tc, tab_words, tab_scales, offs, w4_words, w4_scales, offs2, wgt, noise, wn, mix, ws_words, ws_scales,
+    out_0, out_1, out_2,
+):
+    nc = tc.nc
+    starts = [sum(CHUNKS[:c]) for c in range(len(CHUNKS))]
+    units = [(c, b) for c in range(len(CHUNKS)) for b in range(2)]
+
+    with ExitStack() as ctx:
+        keep = ctx.enter_context(tc.tile_pool(name="keep", bufs=1))
+        raw = ctx.enter_context(tc.tile_pool(name="raw", bufs=6))
+        grp = ctx.enter_context(tc.tile_pool(name="grp", bufs=4))
+        psum_h = ctx.enter_context(tc.psum_pool(name="psum_h", bufs=4))
+        psum_d = ctx.enter_context(tc.psum_pool(name="psum_d", bufs=4))
+
+        def kept(name, shape, dtype):
+            return keep.tile(shape, dtype, name=name, align_bytes=64)
+
+        idx = keep.tile([P, S // 16], U16, name="idx")
+        idx2 = keep.tile([P, M // 16], U16, name="idx2")
+        tab_s = kept("tab_s", [P, T], U8)
+        tab_w = [kept(f"tab_w{a}", [P, T], I32) for a in range(2)]
+        w4_raw = kept("w4_raw", [P, 2, 2 * H], U8)
+        w4 = kept("w4", [P, 2, 2 * H], U8)
+        wsc_raw = kept("wsc_raw", [P, 2, H], U8)
+        wsc = kept("wsc", [P, 2, H], U8)
+        v_s = [kept(f"v_s{a}", [P, S], U8) for a in range(2)]
+        v_w = [[kept(f"v_w{a}_{j}", [P, 512], U32) for j in range(2)] for a in range(2)]
+        warm = kept("warm", [P, 16], F32)
+
+        wss_raw = kept("wss_raw", [P, N], U8)
+        wss = kept("wss", [P, N], U8)
+        wgt_sb = kept("wgt_sb", [P, M], F32)
+        ws_raw = kept("ws_raw", [P, 2, N], I32)
+        nc.gpsimd.memset(tab_s[:].bitcast(I32), 0)
+        nc.vector.memset(wsc_raw[:].rearrange("p a c -> p (a c)").bitcast(I32), 0)
+        nc.vector.memset(warm[:], 1.0)
+        nc.gpsimd.memset(v_s[1][:].bitcast(I32), 0)
+        nc.gpsimd.memset(wss_raw[:].bitcast(I32), 0)
+        nc.scalar.activation(out=warm[:, 8:9], in_=warm[:, 0:1], func=ACT.Abs_reciprocal_sqrt)
+        noise_raw, wn_raw, mix_sb = {}, {}, {}
+
+        def load_noise(a):
+            noise_raw[a] = raw.tile([P, 4, M], F32, name="raw", tag="raw")
+            nc.sync.dma_start(noise_raw[a][:], noise[512 * a : 512 * (a + 1), :].rearrange("(p j) m -> p j m", j=4))
+
+        def load_wn(a, b):
+            wn_raw[a, b] = raw.tile([P, 4, 512], F32, name="raw", tag="raw")
+            nc.sync.dma_start(
+                wn_raw[a, b][:], wn[512 * a : 512 * (a + 1), 512 * b : 512 * (b + 1)].rearrange("(p j) c -> p j c", j=4)
+            )
+
+        def load_mix(b):
+            mix_sb[b] = kept(f"mix{b}", [P, 4, M], F32)
+            nc.sync.dma_start(mix_sb[b][:], mix[512 * b : 512 * (b + 1), :].rearrange("(p i) m -> p i m", i=4))
+
+        nc.sync.dma_start(idx[:], offs)
+        nc.sync.dma_start(w4_raw[:].bitcast(I32), w4_words.rearrange("a p c -> p a c").bitcast(I32))
+        for q in range(4):
+            nc.sync.dma_start(tab_s[32 * q : 32 * q + 8, :].bitcast(I32), tab_scales[:, 4 * q : 4 * q + 4, :].bitcast(I32))
+        nc.sync.dma_start(tab_w[0][:], tab_words[0].rearrange("p t i -> p (t i)").bitcast(I32))
+        for q in range(4):
+            nc.sync.dma_start(
+                wsc_raw[32 * q : 32 * q + 4, :, :].bitcast(I32),
+                w4_scales[:, 4 * q : 4 * q + 4, :].rearrange("a r c -> r a c").bitcast(I32),
+            )
+        load_noise(0)
+        nc.sync.dma_start(tab_w[1][:], tab_words[1].rearrange("p t i -> p (t i)").bitcast(I32))
+        nc.sync.dma_start(idx2[:], offs2)
+        nc.sync.dma_start(wgt_sb[:], wgt)
+        load_noise(1)
+        load_wn(0, 0)
+        load_wn(1, 0)
+        load_mix(0)
+        load_wn(0, 1)
+        load_wn(1, 1)
+        for q in range(4):
+            nc.sync.dma_start(wss_raw[32 * q : 32 * q + 8, :].bitcast(I32), ws_scales[:, 4 * q : 4 * q + 4, :].bitcast(I32))
+        nc.sync.dma_start(ws_raw[:], ws_words.rearrange("a p c i -> p a (c i)").bitcast(I32))
+        load_mix(1)
+
+        nc.vector.tensor_copy(
+            out=w4[:].bitcast(U16).rearrange("p a (b t m) -> p (a b) m t", b=2, t=4),
+            in_=w4_raw[:].bitcast(U16).rearrange("p a (b m t) -> p (a b) m t", b=2, t=4),
+        )
+        nc.vector.tensor_copy(out=v_s[0][:], in_=tab_s[:].indirect(idx[:]))
+        nc.scalar.dma_start(v_s[1][0:100, :].bitcast(I32), v_s[0][4:104, :].bitcast(I32))
+        for j in range(2):
+            nc.vector.tensor_copy(out=v_w[0][j][:], in_=tab_w[0][:].bitcast(U32).indirect(idx[:, 32 * j : 32 * (j + 1)]))
+        nc.vector.tensor_copy(
+            out=wsc[:].rearrange("p a (b t m) -> p (a b) m t", b=2, t=4),
+            in_=wsc_raw[:].rearrange("p a (b m t) -> p (a b) m t", b=2, t=4),
+        )
+        for j in range(2):
+            nc.vector.tensor_copy(out=v_w[1][j][:], in_=tab_w[1][:].bitcast(U32).indirect(idx[:, 32 * j : 32 * (j + 1)]))
+
+        h = {(b, i): kept(f"h{b}_{i}", [P, S], F32) for b in range(2) for i in range(4)}
+        x = {(c, b): kept(f"x{c}_{b}", [P, 4, CHUNKS[c]], F32) for c, b in units}
+        den = {(c, b): kept(f"den{c}_{b}", [P, 4, CHUNKS[c]], F32) for c, b in units}
+
+        def speech(b, i):
+            col = 512 * b + 128 * i
+            for j in range(2):
+                bank = psum_h.tile([P, 512], F32, name="bank_h", tag="bank_h")
+                for a in range(2):
+                    nc.tensor.matmul_mx(
+                        out=bank[:],
+                        lhsT=w4[:, a, 2 * col : 2 * col + 256].bitcast(E2M1),
+                        lhsT_scale=wsc[:, a, col : col + 128],
+                        rhs=v_w[a][j][:].bitcast(E4M3),
+                        rhs_scale=v_s[a][:, 512 * j : 512 * (j + 1)],
+                        start=(a == 0),
+                        stop=(a == 1),
+                    )
+                nc.scalar.copy(out=h[b, i][:, 512 * j : 512 * (j + 1)], in_=bank[:])
+
+        def pick(c, b, i):
+            m0, width = starts[c], CHUNKS[c]
+            nc.vector.tensor_tensor(
+                out=x[c, b][:, i, :],
+                in0=h[b, i][:].indirect(idx2[:, m0 // 16 : (m0 + width) // 16]),
+                in1=wgt_sb[:, m0 : m0 + width],
+                op=ALU.mult,
+            )
+
+        def cast(on_vector, out, in_):
+            if on_vector:
+                nc.vector.tensor_copy(out=out, in_=in_)
+            else:
+                nc.scalar.copy(out=out, in_=in_)
+
+        noise_q = [kept(f"noise_q{a}", [P, M], U32) for a in range(2)]
+        noise_s = [kept(f"noise_s{a}", [P, M], U8) for a in range(2)]
+        wn_q = {(a, b): kept(f"wn_q{a}_{b}", [P, 512], U32) for a in range(2) for b in range(2)}
+        wn_s = {(a, b): kept(f"wn_s{a}_{b}", [P, 512], U8) for a in range(2) for b in range(2)}
+
+        def quantise_noise(a, engines):
+            g = grp.tile([P, M, 4], BF16, name="grouped", tag="grouped", align_bytes=64)
+            for half, engine in enumerate(engines):
+                cols = slice(256 * half, 256 * (half + 1))
+                cast(
+                    engine == "V",
+                    g[:, cols, :].rearrange("p (c e) j -> p c j e", e=4),
+                    noise_raw[a][:, :, cols].rearrange("p j (c e) -> p c j e", e=4),
+                )
+            nc.vector.quantize_mx(out=noise_q[a][:].bitcast(E4M3), scales=noise_s[a][:], in_=g[:].rearrange("p m j -> p (m j)"))
+
+        def quantise_wn(a, b, engines):
+            g = grp.tile([P, 4, P, 4], BF16, name="grouped", tag="grouped", align_bytes=64)
+            n = len(engines)
+            for part, engine in enumerate(engines):
+                cast(
+                    engine == "V",
+                    g[:, :, part * P // n : (part + 1) * P // n, :].rearrange("p t m j -> p m j t"),
+                    wn_raw[a, b][:, :, part * 512 // n : (part + 1) * 512 // n].rearrange("p j (m t) -> p m j t", t=4),
+                )
+            nc.vector.quantize_mx(
+                out=wn_q[a, b][:].bitcast(E4M3), scales=wn_s[a, b][:], in_=g[:].rearrange("p t m j -> p (t m j)")
+            )
+
+        def product(c, lhs, lhs_scale, rhs, rhs_scale, empty):
+            width = CHUNKS[c]
+            per_bank = 512 // width
+            for i0 in range(0, 4, per_bank):
+                bank = psum_d.tile([P, per_bank, width], F32, name="bank_d", tag="bank_d")
+                for i in range(i0, i0 + per_bank):
+                    for a in range(2):
+                        nc.tensor.matmul_mx(
+                            out=bank[:, i - i0, :],
+                            lhsT=lhs(a, i).bitcast(E4M3),
+                            lhsT_scale=lhs_scale(a, i),
+                            rhs=rhs(a).bitcast(E4M3),
+                            rhs_scale=rhs_scale(a),
+                            start=(a == 0),
+                            stop=(a == 1),
+                        )
+                empty(slice(i0, i0 + per_bank), bank)
+
+        def noise_power(c, b):
+            cols = slice(starts[c], starts[c] + CHUNKS[c])
+            product(
+                c,
+                lambda a, i: wn_q[a, b][:, 128 * i : 128 * (i + 1)],
+                lambda a, i: wn_s[a, b][:, 128 * i : 128 * (i + 1)],
+                lambda a: noise_q[a][:, cols],
+                lambda a: noise_s[a][:, cols],
+                lambda rows, bank: nc.scalar.activation(out=den[c, b][:, rows, :], in_=bank[:], func=ACT.Square),
+            )
+
+        z_q = {(c, b): kept(f"z_q{c}_{b}", [P, CHUNKS[c]], U32) for c, b in units}
+        z_s = {(c, b): kept(f"z_s{c}_{b}", [P, CHUNKS[c]], U8) for c, b in units}
+        z_g = {}
+
+        def square_x(c, b):
+            nc.scalar.activation(out=x[c, b][:], in_=x[c, b][:], func=ACT.Square)
+
+        def denominator(c, b):
+            nc.vector.scalar_tensor_tensor(
+                out=den[c, b][:].rearrange("p i m -> p (i m)"),
+                in0=x[c, b][:].rearrange("p i m -> p (i m)"),
+                scalar=0.2,
+                in1=den[c, b][:].rearrange("p i m -> p (i m)"),
+                op0=ALU.add,
+                op1=ALU.add,
+            )
+
+        def invert(c, b):
+            nc.scalar.activation(out=den[c, b][:], in_=den[c, b][:], func=ACT.Abs_reciprocal_sqrt)
+            nc.scalar.activation(out=den[c, b][:], in_=den[c, b][:], func=ACT.Square)
+
+        def numerator(c, b):
+            cols = slice(starts[c], starts[c] + CHUNKS[c])
+            nc.vector.tensor_tensor(out=x[c, b][:], in0=x[c, b][:], in1=mix_sb[b][:, :, cols], op=ALU.mult)
+
+        def mask_b(c, b):
+            g = grp.tile([P, CHUNKS[c], 4], BF16, name="grouped", tag="grouped", align_bytes=64)
+            nc.vector.tensor_tensor(
+                out=g[:].rearrange("p (c e) i -> p c i e", e=4),
+                in0=x[c, b][:].rearrange("p i (c e) -> p c i e", e=4),
+                in1=den[c, b][:].rearrange("p i (c e) -> p c i e", e=4),
+                op=ALU.mult,
+            )
+            z_g[c, b] = g
+
+        def mask_c(c, b):
+            nc.vector.quantize_mx(
+                out=z_q[c, b][:].bitcast(E4M3), scales=z_s[c, b][:], in_=z_g[c, b][:].rearrange("p m i -> p (m i)")
+            )
+
+        ws = kept("ws", [P, 2, N], I32)
+        y_s = kept("y_s", [P, M], U8)
+
+        y_banks = {}
+
+        def synth_pass(c, a):
+            width = CHUNKS[c]
+            per_bank = 512 // width
+            for g in range(2):
+                for t0 in range(0, 4, per_bank):
+                    if a == 0:
+                        y_banks[c, g, t0] = psum_h.tile([P, per_bank, width], F32, name="bank_h", tag="bank_h")
+                    for t in range(t0, t0 + per_bank):
+                        col = 512 * g + 128 * t
+                        nc.tensor.matmul_mx(
+                            out=y_banks[c, g, t0][:, t - t0, :],
+                            lhsT=ws[:, a, col : col + 128].bitcast(E4M3),
+                            lhsT_scale=wss[4 * a : P, col : col + 128],
+                            rhs=z_q[c, a][:].bitcast(E4M3),
+                            rhs_scale=z_s[c, a][:],
+                            start=(a == 0 and t == t0),
+                            stop=(a == 1 and t == t0 + per_bank - 1),
+                        )
+
+        def synthesis(c, g):
+            width = CHUNKS[c]
+            per_bank = 512 // width
+            cols = slice(starts[c], starts[c] + width)
+            y = raw.tile([P, 4, width], F32, name="raw", tag="raw")
+            for t0 in range(0, 4, per_bank):
+                nc.scalar.copy(out=y[:, t0 : t0 + per_bank, :], in_=y_banks[c, g, t0][:])
+            nc.sync.dma_start(out_0[512 * g : 512 * (g + 1), cols].rearrange("(p t) m -> p t m", t=4), y[:])
+            yg = grp.tile([P, width, 4], BF16, name="grouped", tag="grouped", align_bytes=64)
+            nc.vector.tensor_copy(
+                out=yg[:].rearrange("p (c e) t -> p c t e", e=4), in_=y[:].rearrange("p t (c e) -> p c t e", e=4)
+            )
+            y_q = kept(f"y_q{c}_{g}", [P, width], I32)
+            nc.vector.quantize_mx(
+                out=y_q[:].bitcast(E4M3), scales=y_s[4 * g : P, cols], in_=yg[:].rearrange("p m t -> p (m t)")
+            )
+            nc.sync.dma_start(out_1[g, :, cols, :].rearrange("p m t -> p (m t)").bitcast(I32), y_q[:])
+
+        def deal_ws():
+            nc.vector.tensor_copy(
+                out=ws[:].rearrange("p a (g t m) -> p (a g) m t", g=2, t=4),
+                in_=ws_raw[:].rearrange("p a (g m t) -> p (a g) m t", g=2, t=4),
+            )
+            nc.vector.tensor_copy(
+                out=wss[:].rearrange("p (g t m) -> p g m t", g=2, t=4),
+                in_=wss_raw[:].rearrange("p (g m t) -> p g m t", g=2, t=4),
+            )
+
+        nc_ = len(CHUNKS)
+        def unit(c, b):
+            square_x(c, b)
+            denominator(c, b)
+            invert(c, b)
+            numerator(c, b)
+            mask_b(c, b)
+            mask_c(c, b)
+        quantise_noise(0, "SS")
+        for i in range(4):
+            speech(0, i)
+        quantise_noise(1, "VV")
+        quantise_wn(0, 0, "VV")
+        quantise_wn(1, 0, "VV")
+        for c in range(nc_):
+            noise_power(c, 0)
+        for i in range(4):
+            for c in range(nc_):
+                pick(c, 0, i)
+        for i in range(4):
+            speech(1, i)
+        for c in range(1):
+            unit(c, 0)
+        quantise_wn(0, 1, "SS")
+        quantise_wn(1, 1, "SS")
+        for c in range(nc_):
+            noise_power(c, 1)
+        for c in range(nc_):
+            for i in range(4):
+                pick(c, 1, i)
+        deal_ws()
+        for c in range(nc_):
+            if c >= 1:
+                unit(c, 0)
+            synth_pass(c, 0)
+            unit(c, 1)
+            synth_pass(c, 1)
+            for g in range(2):
+                synthesis(c, g)
+        for q in range(4):
+            nc.scalar.dma_start(out_2[:, 4 * q : 4 * q + 4, :].bitcast(I32), y_s[32 * q : 32 * q + 8, :].bitcast(I32))

@@ -17,7 +17,7 @@ E2M1 = mybir.dt.float4_e2m1fn_x4
 ACT = mybir.ActivationFunctionType
 ALU = mybir.AluOpType
 
-CHUNKS = [256,256]
+CHUNKS = [256,128,128]
 
 
 def tile_list_ratio_mask_synthesis_kernel(
@@ -72,52 +72,57 @@ def tile_list_ratio_mask_synthesis_kernel(
                 wn_raw[a, b][:], wn[512 * a : 512 * (a + 1), 512 * b : 512 * (b + 1)].rearrange("(p j) c -> p j c", j=4)
             )
 
-        def load_mix(b):
-            mix_sb[b] = kept(f"mix{b}", [P, 4, M], F32)
-            nc.sync.dma_start(mix_sb[b][:], mix[512 * b : 512 * (b + 1), :].rearrange("(p i) m -> p i m", i=4))
+        def load_mix(c, b):
+            cols = slice(starts[c], starts[c] + CHUNKS[c])
+            mix_sb[c, b] = kept(f"mix{c}_{b}", [P, 4, CHUNKS[c]], F32)
+            nc.sync.dma_start(mix_sb[c, b][:], mix[512 * b : 512 * (b + 1), cols].rearrange("(p i) m -> p i m", i=4))
 
         nc.sync.dma_start(idx[:], offs)
         nc.sync.dma_start(w4_raw[:].bitcast(I32), w4_words.rearrange("a p c -> p a c").bitcast(I32))
         for q in range(4):
             nc.sync.dma_start(tab_s[32 * q : 32 * q + 8, :].bitcast(I32), tab_scales[:, 4 * q : 4 * q + 4, :].bitcast(I32))
         nc.sync.dma_start(tab_w[0][:], tab_words[0].rearrange("p t i -> p (t i)").bitcast(I32))
+        nc.sync.dma_start(tab_w[1][:], tab_words[1].rearrange("p t i -> p (t i)").bitcast(I32))
         for q in range(4):
             nc.sync.dma_start(
                 wsc_raw[32 * q : 32 * q + 4, :, :].bitcast(I32),
                 w4_scales[:, 4 * q : 4 * q + 4, :].rearrange("a r c -> r a c").bitcast(I32),
             )
         load_noise(0)
-        nc.sync.dma_start(tab_w[1][:], tab_words[1].rearrange("p t i -> p (t i)").bitcast(I32))
         nc.sync.dma_start(idx2[:], offs2)
         nc.sync.dma_start(wgt_sb[:], wgt)
         load_noise(1)
         load_wn(0, 0)
         load_wn(1, 0)
-        load_mix(0)
         load_wn(0, 1)
         load_wn(1, 1)
+        load_mix(0, 0)
+        load_mix(0, 1)
         for q in range(4):
             nc.sync.dma_start(wss_raw[32 * q : 32 * q + 8, :].bitcast(I32), ws_scales[:, 4 * q : 4 * q + 4, :].bitcast(I32))
         nc.sync.dma_start(ws_raw[:], ws_words.rearrange("a p c i -> p a (c i)").bitcast(I32))
-        load_mix(1)
+        for c in range(1, 3):
+            load_mix(c, 0)
+            load_mix(c, 1)
 
         nc.vector.tensor_copy(
-            out=w4[:].bitcast(U16).rearrange("p a (b t m) -> p (a b) m t", b=2, t=4),
-            in_=w4_raw[:].bitcast(U16).rearrange("p a (b m t) -> p (a b) m t", b=2, t=4),
+            out=w4[:].bitcast(U16).rearrange("p a (b t m) -> p (a b) t m", b=2, t=4),
+            in_=w4_raw[:].bitcast(U16).rearrange("p a (b m t) -> p (a b) t m", b=2, t=4),
         )
         nc.vector.tensor_copy(out=v_s[0][:], in_=tab_s[:].indirect(idx[:]))
         nc.scalar.dma_start(v_s[1][0:100, :].bitcast(I32), v_s[0][4:104, :].bitcast(I32))
-        for j in range(2):
-            nc.vector.tensor_copy(out=v_w[0][j][:], in_=tab_w[0][:].bitcast(U32).indirect(idx[:, 32 * j : 32 * (j + 1)]))
+        nc.vector.tensor_copy(out=v_w[0][0][:], in_=tab_w[0][:].bitcast(U32).indirect(idx[:, 0 : 32]))
+        nc.vector.tensor_copy(out=v_w[0][1][:], in_=tab_w[0][:].bitcast(U32).indirect(idx[:, 32 : 64]))
+        nc.vector.tensor_copy(out=v_w[1][0][:], in_=tab_w[1][:].bitcast(U32).indirect(idx[:, 0 : 32]))
         nc.vector.tensor_copy(
-            out=wsc[:].rearrange("p a (b t m) -> p (a b) m t", b=2, t=4),
-            in_=wsc_raw[:].rearrange("p a (b m t) -> p (a b) m t", b=2, t=4),
+            out=wsc[:].rearrange("p a (b t m) -> p (a b) t m", b=2, t=4),
+            in_=wsc_raw[:].rearrange("p a (b m t) -> p (a b) t m", b=2, t=4),
         )
-        for j in range(2):
-            nc.vector.tensor_copy(out=v_w[1][j][:], in_=tab_w[1][:].bitcast(U32).indirect(idx[:, 32 * j : 32 * (j + 1)]))
+        nc.vector.tensor_copy(out=v_w[1][1][:], in_=tab_w[1][:].bitcast(U32).indirect(idx[:, 32 : 64]))
 
         h = {(b, i): kept(f"h{b}_{i}", [P, S], F32) for b in range(2) for i in range(4)}
-        x = {(c, b): kept(f"x{c}_{b}", [P, 4, CHUNKS[c]], F32) for c, b in units}
+        x = {}
+        x_tag = [0,1,2,0,1,2]
         den = {(c, b): kept(f"den{c}_{b}", [P, 4, CHUNKS[c]], F32) for c, b in units}
 
         def speech(b, i):
@@ -138,6 +143,8 @@ def tile_list_ratio_mask_synthesis_kernel(
 
         def pick(c, b, i):
             m0, width = starts[c], CHUNKS[c]
+            if i == 0:
+                x[c, b] = keep.tile([P, 4, width], F32, name="x", tag=f"x{x_tag[2 * c + b]}")
             nc.vector.tensor_tensor(
                 out=x[c, b][:, i, :],
                 in0=h[b, i][:].indirect(idx2[:, m0 // 16 : (m0 + width) // 16]),
@@ -169,12 +176,12 @@ def tile_list_ratio_mask_synthesis_kernel(
 
         def quantise_wn(a, b, engines):
             g = grp.tile([P, 4, P, 4], BF16, name="grouped", tag="grouped", align_bytes=64)
-            n = len(engines)
-            for part, engine in enumerate(engines):
+            for pair, engine in enumerate(engines):
+                slots = slice(2 * pair, 2 * pair + 2)
                 cast(
                     engine == "V",
-                    g[:, :, part * P // n : (part + 1) * P // n, :].rearrange("p t m j -> p m j t"),
-                    wn_raw[a, b][:, :, part * 512 // n : (part + 1) * 512 // n].rearrange("p j (m t) -> p m j t", t=4),
+                    g[:, slots, :, :].rearrange("p t m j -> p m j t"),
+                    wn_raw[a, b][:].rearrange("p j (m t) -> p m j t", t=4)[:, :, :, slots],
                 )
             nc.vector.quantize_mx(
                 out=wn_q[a, b][:].bitcast(E4M3), scales=wn_s[a, b][:], in_=g[:].rearrange("p t m j -> p (t m j)")
@@ -231,14 +238,13 @@ def tile_list_ratio_mask_synthesis_kernel(
             nc.scalar.activation(out=den[c, b][:], in_=den[c, b][:], func=ACT.Square)
 
         def numerator(c, b):
-            cols = slice(starts[c], starts[c] + CHUNKS[c])
-            nc.vector.tensor_tensor(out=x[c, b][:], in0=x[c, b][:], in1=mix_sb[b][:, :, cols], op=ALU.mult)
+            nc.vector.tensor_tensor(out=mix_sb[c, b][:], in0=x[c, b][:], in1=mix_sb[c, b][:], op=ALU.mult)
 
         def mask_b(c, b):
             g = grp.tile([P, CHUNKS[c], 4], BF16, name="grouped", tag="grouped", align_bytes=64)
             nc.vector.tensor_tensor(
                 out=g[:].rearrange("p (c e) i -> p c i e", e=4),
-                in0=x[c, b][:].rearrange("p i (c e) -> p c i e", e=4),
+                in0=mix_sb[c, b][:].rearrange("p i (c e) -> p c i e", e=4),
                 in1=den[c, b][:].rearrange("p i (c e) -> p c i e", e=4),
                 op=ALU.mult,
             )
@@ -279,7 +285,7 @@ def tile_list_ratio_mask_synthesis_kernel(
             cols = slice(starts[c], starts[c] + width)
             y = raw.tile([P, 4, width], F32, name="raw", tag="raw")
             for t0 in range(0, 4, per_bank):
-                nc.scalar.copy(out=y[:, t0 : t0 + per_bank, :], in_=y_banks[c, g, t0][:])
+                cast(c == len(CHUNKS) - 1 and g == 1, y[:, t0 : t0 + per_bank, :], y_banks[c, g, t0][:])
             nc.sync.dma_start(out_0[512 * g : 512 * (g + 1), cols].rearrange("(p t) m -> p t m", t=4), y[:])
             yg = grp.tile([P, width, 4], BF16, name="grouped", tag="grouped", align_bytes=64)
             nc.vector.tensor_copy(
@@ -297,48 +303,46 @@ def tile_list_ratio_mask_synthesis_kernel(
                 in_=ws_raw[:].rearrange("p a (g m t) -> p (a g) m t", g=2, t=4),
             )
             nc.vector.tensor_copy(
-                out=wss[:].rearrange("p (g t m) -> p g m t", g=2, t=4),
-                in_=wss_raw[:].rearrange("p (g m t) -> p g m t", g=2, t=4),
+                out=wss[:].rearrange("p (g t m) -> p g t m", g=2, t=4),
+                in_=wss_raw[:].rearrange("p (g m t) -> p g t m", g=2, t=4),
             )
 
         nc_ = len(CHUNKS)
-        def unit(c, b):
+        def front(c, b):
+            noise_power(c, b)
             square_x(c, b)
             denominator(c, b)
             invert(c, b)
             numerator(c, b)
+        def back(c, b):
             mask_b(c, b)
             mask_c(c, b)
-        quantise_noise(0, "SS")
-        for i in range(4):
-            speech(0, i)
+            synth_pass(c, b)
+            if b == 1:
+                for g in range(2):
+                    synthesis(c, g)
+        def picks_of(c, b):
+            for i in range(4):
+                pick(c, b, i)
+        for b in range(2):
+            for i in range(4):
+                speech(b, i)
+                pick(0, b, i)
+        quantise_noise(0, "VV")
         quantise_noise(1, "VV")
         quantise_wn(0, 0, "VV")
         quantise_wn(1, 0, "VV")
-        for c in range(nc_):
-            noise_power(c, 0)
-        for i in range(4):
-            for c in range(nc_):
-                pick(c, 0, i)
-        for i in range(4):
-            speech(1, i)
-        for c in range(1):
-            unit(c, 0)
+
         quantise_wn(0, 1, "SS")
         quantise_wn(1, 1, "SS")
-        for c in range(nc_):
-            noise_power(c, 1)
-        for c in range(nc_):
-            for i in range(4):
-                pick(c, 1, i)
+        front(0, 0)
         deal_ws()
-        for c in range(nc_):
-            if c >= 1:
-                unit(c, 0)
-            synth_pass(c, 0)
-            unit(c, 1)
-            synth_pass(c, 1)
-            for g in range(2):
-                synthesis(c, g)
+        order = units
+        for u, (c, b) in enumerate(order):
+            if u + 2 < len(order) and order[u + 2][0] > 0:
+                picks_of(*order[u + 2])
+            if u + 1 < len(order):
+                front(*order[u + 1])
+            back(c, b)
         for q in range(4):
             nc.scalar.dma_start(out_2[:, 4 * q : 4 * q + 4, :].bitcast(I32), y_s[32 * q : 32 * q + 8, :].bitcast(I32))

@@ -30,10 +30,9 @@ def tile_list_ratio_mask_synthesis_kernel(
 
     with ExitStack() as ctx:
         keep = ctx.enter_context(tc.tile_pool(name="keep", bufs=1))
-        raw = ctx.enter_context(tc.tile_pool(name="raw", bufs=6))
+        raw = ctx.enter_context(tc.tile_pool(name="raw", bufs=4))
         grp = ctx.enter_context(tc.tile_pool(name="grp", bufs=4))
-        psum_h = ctx.enter_context(tc.psum_pool(name="psum_h", bufs=4))
-        psum_d = ctx.enter_context(tc.psum_pool(name="psum_d", bufs=4))
+        psum = ctx.enter_context(tc.psum_pool(name="psum", bufs=1))
 
         def kept(name, shape, dtype):
             return keep.tile(shape, dtype, name=name, align_bytes=64)
@@ -45,7 +44,7 @@ def tile_list_ratio_mask_synthesis_kernel(
         w4_raw = kept("w4_raw", [P, 2, 2 * H], U8)
         w4 = kept("w4", [P, 2, 2 * H], U8)
         wsc_raw = kept("wsc_raw", [P, 2, H], U8)
-        wsc = kept("wsc", [P, 2, H], U8)
+        wsc = [kept(f"wsc{a}", [P, H], U8) for a in range(2)]
         v_s = [kept(f"v_s{a}", [P, S], U8) for a in range(2)]
         v_w = [[kept(f"v_w{a}_{j}", [P, 512], U32) for j in range(2)] for a in range(2)]
         warm = kept("warm", [P, 16], F32)
@@ -62,9 +61,12 @@ def tile_list_ratio_mask_synthesis_kernel(
         nc.scalar.activation(out=warm[:, 8:9], in_=warm[:, 0:1], func=ACT.Abs_reciprocal_sqrt)
         noise_raw, wn_raw, mix_sb = {}, {}, {}
 
-        def load_noise(a):
-            noise_raw[a] = raw.tile([P, 4, M], F32, name="raw", tag="raw")
-            nc.sync.dma_start(noise_raw[a][:], noise[512 * a : 512 * (a + 1), :].rearrange("(p j) m -> p j m", j=4))
+        def load_noise(a, half):
+            noise_raw[a, half] = kept(f"noise_raw{a}_{half}", [P, 4, 256], F32)
+            nc.sync.dma_start(
+                noise_raw[a, half][:],
+                noise[512 * a : 512 * (a + 1), 256 * half : 256 * (half + 1)].rearrange("(p j) m -> p j m", j=4),
+            )
 
         def load_wn(a, b):
             wn_raw[a, b] = raw.tile([P, 4, 512], F32, name="raw", tag="raw")
@@ -88,14 +90,16 @@ def tile_list_ratio_mask_synthesis_kernel(
                 wsc_raw[32 * q : 32 * q + 4, :, :].bitcast(I32),
                 w4_scales[:, 4 * q : 4 * q + 4, :].rearrange("a r c -> r a c").bitcast(I32),
             )
-        load_noise(0)
+        load_noise(0, 0)
+        load_noise(1, 0)
         nc.sync.dma_start(idx2[:], offs2)
         nc.sync.dma_start(wgt_sb[:], wgt)
-        load_noise(1)
         load_wn(0, 0)
         load_wn(1, 0)
         load_wn(0, 1)
         load_wn(1, 1)
+        load_noise(0, 1)
+        load_noise(1, 1)
         load_mix(0, 0)
         load_mix(0, 1)
         for q in range(4):
@@ -113,33 +117,37 @@ def tile_list_ratio_mask_synthesis_kernel(
         nc.scalar.dma_start(v_s[1][0:100, :].bitcast(I32), v_s[0][4:104, :].bitcast(I32))
         nc.vector.tensor_copy(out=v_w[0][0][:], in_=tab_w[0][:].bitcast(U32).indirect(idx[:, 0 : 32]))
         nc.vector.tensor_copy(out=v_w[0][1][:], in_=tab_w[0][:].bitcast(U32).indirect(idx[:, 32 : 64]))
+        nc.vector.tensor_copy(
+            out=wsc[0][:].rearrange("p (b t m) -> p b t m", b=2, t=4),
+            in_=wsc_raw[:, 0, :].rearrange("p (b m t) -> p b t m", b=2, t=4),
+        )
         nc.vector.tensor_copy(out=v_w[1][0][:], in_=tab_w[1][:].bitcast(U32).indirect(idx[:, 0 : 32]))
         nc.vector.tensor_copy(
-            out=wsc[:].rearrange("p a (b t m) -> p (a b) t m", b=2, t=4),
-            in_=wsc_raw[:].rearrange("p a (b m t) -> p (a b) t m", b=2, t=4),
+            out=wsc[1][:].rearrange("p (b t m) -> p b t m", b=2, t=4),
+            in_=wsc_raw[:, 1, :].rearrange("p (b m t) -> p b t m", b=2, t=4),
         )
         nc.vector.tensor_copy(out=v_w[1][1][:], in_=tab_w[1][:].bitcast(U32).indirect(idx[:, 32 : 64]))
 
         h = {(b, i): kept(f"h{b}_{i}", [P, S], F32) for b in range(2) for i in range(4)}
         x = {}
-        x_tag = [0,1,2,0,1,2]
+        x_tag = [0,1,2,3,0,1]
         den = {(c, b): kept(f"den{c}_{b}", [P, 4, CHUNKS[c]], F32) for c, b in units}
 
         def speech(b, i):
             col = 512 * b + 128 * i
             for j in range(2):
-                bank = psum_h.tile([P, 512], F32, name="bank_h", tag="bank_h")
+                bank = psum.tile([P, 512], F32, name="bank", tag=f"bank{(2 * i + j) % 8}")
                 for a in range(2):
                     nc.tensor.matmul_mx(
                         out=bank[:],
                         lhsT=w4[:, a, 2 * col : 2 * col + 256].bitcast(E2M1),
-                        lhsT_scale=wsc[:, a, col : col + 128],
+                        lhsT_scale=wsc[a][:, col : col + 128],
                         rhs=v_w[a][j][:].bitcast(E4M3),
                         rhs_scale=v_s[a][:, 512 * j : 512 * (j + 1)],
                         start=(a == 0),
                         stop=(a == 1),
                     )
-                nc.scalar.copy(out=h[b, i][:, 512 * j : 512 * (j + 1)], in_=bank[:])
+                cast((b, i, j) in [], h[b, i][:, 512 * j : 512 * (j + 1)], bank[:])
 
         def pick(c, b, i):
             m0, width = starts[c], CHUNKS[c]
@@ -158,21 +166,21 @@ def tile_list_ratio_mask_synthesis_kernel(
             else:
                 nc.scalar.copy(out=out, in_=in_)
 
-        noise_q = [kept(f"noise_q{a}", [P, M], U32) for a in range(2)]
-        noise_s = [kept(f"noise_s{a}", [P, M], U8) for a in range(2)]
+        noise_q = {(a, half): kept(f"noise_q{a}_{half}", [P, 256], U32) for a in range(2) for half in range(2)}
+        noise_s = {(a, half): kept(f"noise_s{a}_{half}", [P, 256], U8) for a in range(2) for half in range(2)}
         wn_q = {(a, b): kept(f"wn_q{a}_{b}", [P, 512], U32) for a in range(2) for b in range(2)}
         wn_s = {(a, b): kept(f"wn_s{a}_{b}", [P, 512], U8) for a in range(2) for b in range(2)}
 
-        def quantise_noise(a, engines):
-            g = grp.tile([P, M, 4], BF16, name="grouped", tag="grouped", align_bytes=64)
-            for half, engine in enumerate(engines):
-                cols = slice(256 * half, 256 * (half + 1))
-                cast(
-                    engine == "V",
-                    g[:, cols, :].rearrange("p (c e) j -> p c j e", e=4),
-                    noise_raw[a][:, :, cols].rearrange("p j (c e) -> p c j e", e=4),
-                )
-            nc.vector.quantize_mx(out=noise_q[a][:].bitcast(E4M3), scales=noise_s[a][:], in_=g[:].rearrange("p m j -> p (m j)"))
+        def quantise_noise(a, half, engine):
+            g = grp.tile([P, 256, 4], BF16, name="grouped", tag="grouped", align_bytes=64)
+            cast(
+                engine == "V",
+                g[:].rearrange("p (c e) j -> p c j e", e=4),
+                noise_raw[a, half][:].rearrange("p j (c e) -> p c j e", e=4),
+            )
+            nc.vector.quantize_mx(
+                out=noise_q[a, half][:].bitcast(E4M3), scales=noise_s[a, half][:], in_=g[:].rearrange("p m j -> p (m j)")
+            )
 
         def quantise_wn(a, b, engines):
             g = grp.tile([P, 4, P, 4], BF16, name="grouped", tag="grouped", align_bytes=64)
@@ -187,11 +195,11 @@ def tile_list_ratio_mask_synthesis_kernel(
                 out=wn_q[a, b][:].bitcast(E4M3), scales=wn_s[a, b][:], in_=g[:].rearrange("p t m j -> p (t m j)")
             )
 
-        def product(c, lhs, lhs_scale, rhs, rhs_scale, empty):
+        def product(c, b, lhs, lhs_scale, rhs, rhs_scale, empty):
             width = CHUNKS[c]
             per_bank = 512 // width
             for i0 in range(0, 4, per_bank):
-                bank = psum_d.tile([P, per_bank, width], F32, name="bank_d", tag="bank_d")
+                bank = psum.tile([P, per_bank, width], F32, name="bank", tag=f"bank{(starts[c] * 8 + (4 * b + i0) * width) // 512}")
                 for i in range(i0, i0 + per_bank):
                     for a in range(2):
                         nc.tensor.matmul_mx(
@@ -206,13 +214,15 @@ def tile_list_ratio_mask_synthesis_kernel(
                 empty(slice(i0, i0 + per_bank), bank)
 
         def noise_power(c, b):
-            cols = slice(starts[c], starts[c] + CHUNKS[c])
+            half = starts[c] // 256
+            cols = slice(starts[c] % 256, starts[c] % 256 + CHUNKS[c])
             product(
                 c,
+                b,
                 lambda a, i: wn_q[a, b][:, 128 * i : 128 * (i + 1)],
                 lambda a, i: wn_s[a, b][:, 128 * i : 128 * (i + 1)],
-                lambda a: noise_q[a][:, cols],
-                lambda a: noise_s[a][:, cols],
+                lambda a: noise_q[a, half][:, cols],
+                lambda a: noise_s[a, half][:, cols],
                 lambda rows, bank: nc.scalar.activation(out=den[c, b][:, rows, :], in_=bank[:], func=ACT.Square),
             )
 
@@ -241,12 +251,12 @@ def tile_list_ratio_mask_synthesis_kernel(
             nc.vector.tensor_tensor(out=mix_sb[c, b][:], in0=x[c, b][:], in1=mix_sb[c, b][:], op=ALU.mult)
 
         def mask_b(c, b):
+            nc.vector.tensor_tensor(out=den[c, b][:], in0=mix_sb[c, b][:], in1=den[c, b][:], op=ALU.mult)
             g = grp.tile([P, CHUNKS[c], 4], BF16, name="grouped", tag="grouped", align_bytes=64)
-            nc.vector.tensor_tensor(
-                out=g[:].rearrange("p (c e) i -> p c i e", e=4),
-                in0=mix_sb[c, b][:].rearrange("p i (c e) -> p c i e", e=4),
-                in1=den[c, b][:].rearrange("p i (c e) -> p c i e", e=4),
-                op=ALU.mult,
+            cast(
+                "VVVVVV"[2 * c + b] == "V",
+                g[:].rearrange("p (c e) i -> p c i e", e=4),
+                den[c, b][:].rearrange("p i (c e) -> p c i e", e=4),
             )
             z_g[c, b] = g
 
@@ -258,7 +268,7 @@ def tile_list_ratio_mask_synthesis_kernel(
         ws = kept("ws", [P, 2, N], I32)
         y_s = kept("y_s", [P, M], U8)
 
-        y_banks = {}
+        y_banks, y_sb = {}, {}
 
         def synth_pass(c, a):
             width = CHUNKS[c]
@@ -266,7 +276,7 @@ def tile_list_ratio_mask_synthesis_kernel(
             for g in range(2):
                 for t0 in range(0, 4, per_bank):
                     if a == 0:
-                        y_banks[c, g, t0] = psum_h.tile([P, per_bank, width], F32, name="bank_h", tag="bank_h")
+                        y_banks[c, g, t0] = psum.tile([P, per_bank, width], F32, name="bank", tag=f"bank{(starts[c] * 8 + (4 * g + t0) * width) // 512}")
                     for t in range(t0, t0 + per_bank):
                         col = 512 * g + 128 * t
                         nc.tensor.matmul_mx(
@@ -287,9 +297,17 @@ def tile_list_ratio_mask_synthesis_kernel(
             for t0 in range(0, 4, per_bank):
                 cast(c == len(CHUNKS) - 1 and g == 1, y[:, t0 : t0 + per_bank, :], y_banks[c, g, t0][:])
             nc.sync.dma_start(out_0[512 * g : 512 * (g + 1), cols].rearrange("(p t) m -> p t m", t=4), y[:])
+            y_sb[c, g] = y
+
+        def planes(c, g):
+            width = CHUNKS[c]
+            cols = slice(starts[c], starts[c] + width)
+            y = y_sb[c, g]
             yg = grp.tile([P, width, 4], BF16, name="grouped", tag="grouped", align_bytes=64)
-            nc.vector.tensor_copy(
-                out=yg[:].rearrange("p (c e) t -> p c t e", e=4), in_=y[:].rearrange("p t (c e) -> p c t e", e=4)
+            cast(
+                "VVVVVV"[2 * c + g] == "V",
+                yg[:].rearrange("p (c e) t -> p c t e", e=4),
+                y[:].rearrange("p t (c e) -> p c t e", e=4),
             )
             y_q = kept(f"y_q{c}_{g}", [P, width], I32)
             nc.vector.quantize_mx(
@@ -319,8 +337,14 @@ def tile_list_ratio_mask_synthesis_kernel(
             mask_c(c, b)
             synth_pass(c, b)
             if b == 1:
+                if c > 0:
+                    for g in range(2):
+                        planes(c - 1, g)
                 for g in range(2):
                     synthesis(c, g)
+                if c == nc_ - 1:
+                    for g in range(2):
+                        planes(c, g)
         def picks_of(c, b):
             for i in range(4):
                 pick(c, b, i)
@@ -328,14 +352,16 @@ def tile_list_ratio_mask_synthesis_kernel(
             for i in range(4):
                 speech(b, i)
                 pick(0, b, i)
-        quantise_noise(0, "VV")
-        quantise_noise(1, "VV")
+        quantise_noise(0, 0, "S")
+        quantise_noise(1, 0, "S")
         quantise_wn(0, 0, "VV")
         quantise_wn(1, 0, "VV")
 
         quantise_wn(0, 1, "SS")
         quantise_wn(1, 1, "SS")
         front(0, 0)
+        quantise_noise(0, 1, "S")
+        quantise_noise(1, 1, "S")
         deal_ws()
         order = units
         for u, (c, b) in enumerate(order):

@@ -4,6 +4,9 @@ import concourse.mybir as mybir
 
 K, H, N, T, S, M = 1024, 1024, 1024, 2048, 1024, 512
 P = 128
+PASS = 512
+BANK = 512
+HALF = M // 2
 FLOPS = 2 * K * H * S + 2 * K * H * M + 2 * H * N * M
 
 F32 = mybir.dt.float32
@@ -17,7 +20,8 @@ E2M1 = mybir.dt.float4_e2m1fn_x4
 ACT = mybir.ActivationFunctionType
 ALU = mybir.AluOpType
 
-CHUNKS = [256,128,128]
+CHUNKS = [256, 128, 128]
+PICK_TILES = 3
 
 
 def tile_list_ratio_mask_synthesis_kernel(
@@ -27,348 +31,307 @@ def tile_list_ratio_mask_synthesis_kernel(
     nc = tc.nc
     starts = [sum(CHUNKS[:c]) for c in range(len(CHUNKS))]
     units = [(c, b) for c in range(len(CHUNKS)) for b in range(2)]
+    last_chunk = len(CHUNKS) - 1
 
     with ExitStack() as ctx:
         keep = ctx.enter_context(tc.tile_pool(name="keep", bufs=1))
-        raw = ctx.enter_context(tc.tile_pool(name="raw", bufs=4))
-        grp = ctx.enter_context(tc.tile_pool(name="grp", bufs=4))
+        staged = ctx.enter_context(tc.tile_pool(name="staged", bufs=4))
+        rounded = ctx.enter_context(tc.tile_pool(name="rounded", bufs=4))
         psum = ctx.enter_context(tc.psum_pool(name="psum", bufs=1))
 
         def kept(name, shape, dtype):
             return keep.tile(shape, dtype, name=name, align_bytes=64)
 
+        def rounded_tile(shape):
+            return rounded.tile(shape, BF16, name="rounded", tag="rounded", align_bytes=64)
+
+        def bank_tile(number, shape):
+            return psum.tile(shape, F32, name="bank", tag=f"bank{number}")
+
+        def chunk_cols(c):
+            return slice(starts[c], starts[c] + CHUNKS[c])
+
+        def chunk_bank(c, row_pass, slot):
+            return (8 * starts[c] + (4 * row_pass + slot) * CHUNKS[c]) // BANK
+
         idx = keep.tile([P, S // 16], U16, name="idx")
         idx2 = keep.tile([P, M // 16], U16, name="idx2")
         tab_s = kept("tab_s", [P, T], U8)
         tab_w = [kept(f"tab_w{a}", [P, T], I32) for a in range(2)]
-        w4_raw = kept("w4_raw", [P, 2, 2 * H], U8)
-        w4 = kept("w4", [P, 2, 2 * H], U8)
-        wsc_raw = kept("wsc_raw", [P, 2, H], U8)
-        wsc = [kept(f"wsc{a}", [P, H], U8) for a in range(2)]
+        w4_raw = [kept(f"w4_raw{a}", [P, 2 * H], U8) for a in range(2)]
+        w4_w = [kept(f"w4_w{a}", [P, 2 * H], U8) for a in range(2)]
+        w4_s_raw = kept("w4_s_raw", [P, 2, H], U8)
+        w4_s = [kept(f"w4_s{a}", [P, H], U8) for a in range(2)]
         v_s = [kept(f"v_s{a}", [P, S], U8) for a in range(2)]
-        v_w = [[kept(f"v_w{a}_{j}", [P, 512], U32) for j in range(2)] for a in range(2)]
-        warm = kept("warm", [P, 16], F32)
-
-        wss_raw = kept("wss_raw", [P, N], U8)
-        wss = kept("wss", [P, N], U8)
+        v_w = [[kept(f"v_w{a}_{j}", [P, BANK], U32) for j in range(2)] for a in range(2)]
+        floor = kept("floor", [P, 16], F32)
+        ws_s_raw = kept("ws_s_raw", [P, N], U8)
+        ws_s = kept("ws_s", [P, N], U8)
         wgt_sb = kept("wgt_sb", [P, M], F32)
         ws_raw = kept("ws_raw", [P, 2, N], I32)
+
         nc.gpsimd.memset(tab_s[:].bitcast(I32), 0)
-        nc.vector.memset(wsc_raw[:].rearrange("p a c -> p (a c)").bitcast(I32), 0)
-        nc.vector.memset(warm[:], 1.0)
+        nc.vector.memset(w4_s_raw[:].rearrange("p a c -> p (a c)").bitcast(I32), 0)
+        nc.vector.memset(floor[:, 0:1], 25.0)
         nc.gpsimd.memset(v_s[1][:].bitcast(I32), 0)
-        nc.gpsimd.memset(wss_raw[:].bitcast(I32), 0)
-        nc.scalar.activation(out=warm[:, 8:9], in_=warm[:, 0:1], func=ACT.Abs_reciprocal_sqrt)
+        nc.gpsimd.memset(ws_s_raw[:].bitcast(I32), 0)
+        mask_floor = floor[:, 8:9]
+        nc.scalar.activation(out=mask_floor, in_=floor[:, 0:1], func=ACT.Abs_reciprocal_sqrt)
+
         noise_raw, wn_raw, mix_sb = {}, {}, {}
 
         def load_noise(a, half):
-            noise_raw[a, half] = kept(f"noise_raw{a}_{half}", [P, 4, 256], F32)
+            noise_raw[a, half] = kept(f"noise_raw{a}_{half}", [P, 4, HALF], F32)
             nc.sync.dma_start(
                 noise_raw[a, half][:],
-                noise[512 * a : 512 * (a + 1), 256 * half : 256 * (half + 1)].rearrange("(p j) m -> p j m", j=4),
+                noise[PASS * a : PASS * (a + 1), HALF * half : HALF * (half + 1)].rearrange("(p j) m -> p j m", j=4),
             )
 
         def load_wn(a, b):
-            wn_raw[a, b] = raw.tile([P, 4, 512], F32, name="raw", tag="raw")
+            wn_raw[a, b] = staged.tile([P, 4, PASS], F32, name="staged", tag="staged")
             nc.sync.dma_start(
-                wn_raw[a, b][:], wn[512 * a : 512 * (a + 1), 512 * b : 512 * (b + 1)].rearrange("(p j) c -> p j c", j=4)
+                wn_raw[a, b][:],
+                wn[PASS * a : PASS * (a + 1), PASS * b : PASS * (b + 1)].rearrange("(p j) c -> p j c", j=4),
             )
 
         def load_mix(c, b):
-            cols = slice(starts[c], starts[c] + CHUNKS[c])
             mix_sb[c, b] = kept(f"mix{c}_{b}", [P, 4, CHUNKS[c]], F32)
-            nc.sync.dma_start(mix_sb[c, b][:], mix[512 * b : 512 * (b + 1), cols].rearrange("(p i) m -> p i m", i=4))
+            nc.sync.dma_start(
+                mix_sb[c, b][:], mix[PASS * b : PASS * (b + 1), chunk_cols(c)].rearrange("(p i) m -> p i m", i=4)
+            )
 
         nc.sync.dma_start(idx[:], offs)
-        nc.sync.dma_start(w4_raw[:].bitcast(I32), w4_words.rearrange("a p c -> p a c").bitcast(I32))
+        nc.sync.dma_start(w4_raw[0][:].bitcast(I32), w4_words[0].bitcast(I32))
         for q in range(4):
             nc.sync.dma_start(tab_s[32 * q : 32 * q + 8, :].bitcast(I32), tab_scales[:, 4 * q : 4 * q + 4, :].bitcast(I32))
-        nc.sync.dma_start(tab_w[0][:], tab_words[0].rearrange("p t i -> p (t i)").bitcast(I32))
-        nc.sync.dma_start(tab_w[1][:], tab_words[1].rearrange("p t i -> p (t i)").bitcast(I32))
+        nc.sync.dma_start(w4_raw[1][:].bitcast(I32), w4_words[1].bitcast(I32))
+        for a in range(2):
+            nc.sync.dma_start(tab_w[a][:], tab_words[a].rearrange("p t i -> p (t i)").bitcast(I32))
         for q in range(4):
             nc.sync.dma_start(
-                wsc_raw[32 * q : 32 * q + 4, :, :].bitcast(I32),
+                w4_s_raw[32 * q : 32 * q + 4, :, :].bitcast(I32),
                 w4_scales[:, 4 * q : 4 * q + 4, :].rearrange("a r c -> r a c").bitcast(I32),
             )
-        load_noise(0, 0)
-        load_noise(1, 0)
+        for a in range(2):
+            load_noise(a, 0)
         nc.sync.dma_start(idx2[:], offs2)
         nc.sync.dma_start(wgt_sb[:], wgt)
-        load_wn(0, 0)
-        load_wn(1, 0)
-        load_wn(0, 1)
-        load_wn(1, 1)
-        load_noise(0, 1)
-        load_noise(1, 1)
-        load_mix(0, 0)
-        load_mix(0, 1)
+        for b in range(2):
+            for a in range(2):
+                load_wn(a, b)
+        for a in range(2):
+            load_noise(a, 1)
+        for b in range(2):
+            load_mix(0, b)
         for q in range(4):
-            nc.sync.dma_start(wss_raw[32 * q : 32 * q + 8, :].bitcast(I32), ws_scales[:, 4 * q : 4 * q + 4, :].bitcast(I32))
+            nc.sync.dma_start(ws_s_raw[32 * q : 32 * q + 8, :].bitcast(I32), ws_scales[:, 4 * q : 4 * q + 4, :].bitcast(I32))
         nc.sync.dma_start(ws_raw[:], ws_words.rearrange("a p c i -> p a (c i)").bitcast(I32))
-        for c in range(1, 3):
-            load_mix(c, 0)
-            load_mix(c, 1)
+        for c, b in units[2:]:
+            load_mix(c, b)
 
-        nc.vector.tensor_copy(
-            out=w4[:].bitcast(U16).rearrange("p a (b t m) -> p (a b) t m", b=2, t=4),
-            in_=w4_raw[:].bitcast(U16).rearrange("p a (b m t) -> p (a b) t m", b=2, t=4),
-        )
+        def gather_words(a, j):
+            nc.vector.tensor_copy(out=v_w[a][j][:], in_=tab_w[a][:].bitcast(U32).indirect(idx[:, 32 * j : 32 * (j + 1)]))
+
+        def deal_w4_scales(a):
+            nc.vector.tensor_copy(
+                out=w4_s[a][:].rearrange("p (b i m) -> p b i m", b=2, i=4),
+                in_=w4_s_raw[:, a, :].rearrange("p (b m i) -> p b i m", b=2, i=4),
+            )
+
+        for a in range(2):
+            nc.vector.tensor_copy(
+                out=w4_w[a][:].bitcast(U16).rearrange("p (b i m) -> p b i m", b=2, i=4),
+                in_=w4_raw[a][:].bitcast(U16).rearrange("p (b m i) -> p b i m", b=2, i=4),
+            )
         nc.vector.tensor_copy(out=v_s[0][:], in_=tab_s[:].indirect(idx[:]))
-        nc.scalar.dma_start(v_s[1][0:100, :].bitcast(I32), v_s[0][4:104, :].bitcast(I32))
-        nc.vector.tensor_copy(out=v_w[0][0][:], in_=tab_w[0][:].bitcast(U32).indirect(idx[:, 0 : 32]))
-        nc.vector.tensor_copy(out=v_w[0][1][:], in_=tab_w[0][:].bitcast(U32).indirect(idx[:, 32 : 64]))
-        nc.vector.tensor_copy(
-            out=wsc[0][:].rearrange("p (b t m) -> p b t m", b=2, t=4),
-            in_=wsc_raw[:, 0, :].rearrange("p (b m t) -> p b t m", b=2, t=4),
-        )
-        nc.vector.tensor_copy(out=v_w[1][0][:], in_=tab_w[1][:].bitcast(U32).indirect(idx[:, 0 : 32]))
-        nc.vector.tensor_copy(
-            out=wsc[1][:].rearrange("p (b t m) -> p b t m", b=2, t=4),
-            in_=wsc_raw[:, 1, :].rearrange("p (b m t) -> p b t m", b=2, t=4),
-        )
-        nc.vector.tensor_copy(out=v_w[1][1][:], in_=tab_w[1][:].bitcast(U32).indirect(idx[:, 32 : 64]))
+        nc.scalar.dma_start(v_s[1][0:112, :].bitcast(I32), v_s[0][4:116, :].bitcast(I32))
+        gather_words(0, 0)
+        gather_words(0, 1)
+        deal_w4_scales(0)
+        gather_words(1, 0)
+        deal_w4_scales(1)
+        gather_words(1, 1)
 
         h = {(b, i): kept(f"h{b}_{i}", [P, S], F32) for b in range(2) for i in range(4)}
         x = {}
-        x_tag = [0,1,2,3,0,1]
         den = {(c, b): kept(f"den{c}_{b}", [P, 4, CHUNKS[c]], F32) for c, b in units}
 
         def speech(b, i):
-            col = 512 * b + 128 * i
+            col = PASS * b + P * i
             for j in range(2):
-                bank = psum.tile([P, 512], F32, name="bank", tag=f"bank{(2 * i + j) % 8}")
+                bank = bank_tile(2 * i + j, [P, BANK])
                 for a in range(2):
                     nc.tensor.matmul_mx(
                         out=bank[:],
-                        lhsT=w4[:, a, 2 * col : 2 * col + 256].bitcast(E2M1),
-                        lhsT_scale=wsc[a][:, col : col + 128],
+                        lhsT=w4_w[a][:, 2 * col : 2 * (col + P)].bitcast(E2M1),
+                        lhsT_scale=w4_s[a][:, col : col + P],
                         rhs=v_w[a][j][:].bitcast(E4M3),
-                        rhs_scale=v_s[a][:, 512 * j : 512 * (j + 1)],
+                        rhs_scale=v_s[a][:, BANK * j : BANK * (j + 1)],
                         start=(a == 0),
                         stop=(a == 1),
                     )
-                cast((b, i, j) in [], h[b, i][:, 512 * j : 512 * (j + 1)], bank[:])
+                nc.scalar.copy(out=h[b, i][:, BANK * j : BANK * (j + 1)], in_=bank[:])
 
         def pick(c, b, i):
-            m0, width = starts[c], CHUNKS[c]
             if i == 0:
-                x[c, b] = keep.tile([P, 4, width], F32, name="x", tag=f"x{x_tag[2 * c + b]}")
+                tag = f"x{units.index((c, b)) % PICK_TILES}"
+                x[c, b] = keep.tile([P, 4, CHUNKS[c]], F32, name="x", tag=tag, align_bytes=64)
             nc.vector.tensor_tensor(
                 out=x[c, b][:, i, :],
-                in0=h[b, i][:].indirect(idx2[:, m0 // 16 : (m0 + width) // 16]),
-                in1=wgt_sb[:, m0 : m0 + width],
+                in0=h[b, i][:].indirect(idx2[:, starts[c] // 16 : (starts[c] + CHUNKS[c]) // 16]),
+                in1=wgt_sb[:, chunk_cols(c)],
                 op=ALU.mult,
             )
 
-        def cast(on_vector, out, in_):
-            if on_vector:
-                nc.vector.tensor_copy(out=out, in_=in_)
-            else:
-                nc.scalar.copy(out=out, in_=in_)
+        noise_q = {(a, half): kept(f"noise_q{a}_{half}", [P, HALF], U32) for a in range(2) for half in range(2)}
+        noise_s = {(a, half): kept(f"noise_s{a}_{half}", [P, HALF], U8) for a in range(2) for half in range(2)}
+        wn_q = {(a, b): kept(f"wn_q{a}_{b}", [P, PASS], U32) for a in range(2) for b in range(2)}
+        wn_s = {(a, b): kept(f"wn_s{a}_{b}", [P, PASS], U8) for a in range(2) for b in range(2)}
 
-        noise_q = {(a, half): kept(f"noise_q{a}_{half}", [P, 256], U32) for a in range(2) for half in range(2)}
-        noise_s = {(a, half): kept(f"noise_s{a}_{half}", [P, 256], U8) for a in range(2) for half in range(2)}
-        wn_q = {(a, b): kept(f"wn_q{a}_{b}", [P, 512], U32) for a in range(2) for b in range(2)}
-        wn_s = {(a, b): kept(f"wn_s{a}_{b}", [P, 512], U8) for a in range(2) for b in range(2)}
+        def by_rows(tile):
+            return tile[:].rearrange("p j (c e) -> p c j e", e=4)
 
-        def quantise_noise(a, half, engine):
-            g = grp.tile([P, 256, 4], BF16, name="grouped", tag="grouped", align_bytes=64)
-            cast(
-                engine == "V",
-                g[:].rearrange("p (c e) j -> p c j e", e=4),
-                noise_raw[a, half][:].rearrange("p j (c e) -> p c j e", e=4),
-            )
-            nc.vector.quantize_mx(
-                out=noise_q[a, half][:].bitcast(E4M3), scales=noise_s[a, half][:], in_=g[:].rearrange("p m j -> p (m j)")
-            )
+        def by_words(tile):
+            return tile[:].rearrange("p (c e) j -> p c j e", e=4)
 
-        def quantise_wn(a, b, engines):
-            g = grp.tile([P, 4, P, 4], BF16, name="grouped", tag="grouped", align_bytes=64)
-            for pair, engine in enumerate(engines):
+        def quantise(codes, scales, words):
+            nc.vector.quantize_mx(out=codes.bitcast(E4M3), scales=scales, in_=words)
+
+        def quantise_noise(a, half):
+            words = rounded_tile([P, HALF, 4])
+            nc.scalar.copy(out=by_words(words), in_=by_rows(noise_raw[a, half]))
+            quantise(noise_q[a, half][:], noise_s[a, half][:], words[:].rearrange("p m j -> p (m j)"))
+
+        def quantise_wn(a, b, copy):
+            words = rounded_tile([P, 4, P, 4])
+            for pair in range(2):
                 slots = slice(2 * pair, 2 * pair + 2)
-                cast(
-                    engine == "V",
-                    g[:, slots, :, :].rearrange("p t m j -> p m j t"),
-                    wn_raw[a, b][:].rearrange("p j (m t) -> p m j t", t=4)[:, :, :, slots],
+                copy(
+                    out=words[:, slots, :, :].rearrange("p i m j -> p m j i"),
+                    in_=wn_raw[a, b][:].rearrange("p j (m i) -> p m j i", i=4)[:, :, :, slots],
                 )
-            nc.vector.quantize_mx(
-                out=wn_q[a, b][:].bitcast(E4M3), scales=wn_s[a, b][:], in_=g[:].rearrange("p t m j -> p (t m j)")
-            )
+            quantise(wn_q[a, b][:], wn_s[a, b][:], words[:].rearrange("p i m j -> p (i m j)"))
 
-        def product(c, b, lhs, lhs_scale, rhs, rhs_scale, empty):
-            width = CHUNKS[c]
-            per_bank = 512 // width
-            for i0 in range(0, 4, per_bank):
-                bank = psum.tile([P, per_bank, width], F32, name="bank", tag=f"bank{(starts[c] * 8 + (4 * b + i0) * width) // 512}")
-                for i in range(i0, i0 + per_bank):
+        def noise_power(c, b):
+            half = starts[c] // HALF
+            cols = slice(starts[c] % HALF, starts[c] % HALF + CHUNKS[c])
+            per_bank = BANK // CHUNKS[c]
+            for first in range(0, 4, per_bank):
+                bank = bank_tile(chunk_bank(c, b, first), [P, per_bank, CHUNKS[c]])
+                for i in range(first, first + per_bank):
                     for a in range(2):
                         nc.tensor.matmul_mx(
-                            out=bank[:, i - i0, :],
-                            lhsT=lhs(a, i).bitcast(E4M3),
-                            lhsT_scale=lhs_scale(a, i),
-                            rhs=rhs(a).bitcast(E4M3),
-                            rhs_scale=rhs_scale(a),
+                            out=bank[:, i - first, :],
+                            lhsT=wn_q[a, b][:, P * i : P * (i + 1)].bitcast(E4M3),
+                            lhsT_scale=wn_s[a, b][:, P * i : P * (i + 1)],
+                            rhs=noise_q[a, half][:, cols].bitcast(E4M3),
+                            rhs_scale=noise_s[a, half][:, cols],
                             start=(a == 0),
                             stop=(a == 1),
                         )
-                empty(slice(i0, i0 + per_bank), bank)
-
-        def noise_power(c, b):
-            half = starts[c] // 256
-            cols = slice(starts[c] % 256, starts[c] % 256 + CHUNKS[c])
-            product(
-                c,
-                b,
-                lambda a, i: wn_q[a, b][:, 128 * i : 128 * (i + 1)],
-                lambda a, i: wn_s[a, b][:, 128 * i : 128 * (i + 1)],
-                lambda a: noise_q[a, half][:, cols],
-                lambda a: noise_s[a, half][:, cols],
-                lambda rows, bank: nc.scalar.activation(out=den[c, b][:, rows, :], in_=bank[:], func=ACT.Square),
-            )
+                nc.scalar.activation(out=den[c, b][:, first : first + per_bank, :], in_=bank[:], func=ACT.Square)
 
         z_q = {(c, b): kept(f"z_q{c}_{b}", [P, CHUNKS[c]], U32) for c, b in units}
         z_s = {(c, b): kept(f"z_s{c}_{b}", [P, CHUNKS[c]], U8) for c, b in units}
-        z_g = {}
 
-        def square_x(c, b):
+        def mask_parts(c, b):
+            noise_power(c, b)
             nc.scalar.activation(out=x[c, b][:], in_=x[c, b][:], func=ACT.Square)
-
-        def denominator(c, b):
             nc.vector.scalar_tensor_tensor(
                 out=den[c, b][:].rearrange("p i m -> p (i m)"),
                 in0=x[c, b][:].rearrange("p i m -> p (i m)"),
-                scalar=0.2,
+                scalar=mask_floor,
                 in1=den[c, b][:].rearrange("p i m -> p (i m)"),
                 op0=ALU.add,
                 op1=ALU.add,
             )
-
-        def invert(c, b):
             nc.scalar.activation(out=den[c, b][:], in_=den[c, b][:], func=ACT.Abs_reciprocal_sqrt)
             nc.scalar.activation(out=den[c, b][:], in_=den[c, b][:], func=ACT.Square)
-
-        def numerator(c, b):
             nc.vector.tensor_tensor(out=mix_sb[c, b][:], in0=x[c, b][:], in1=mix_sb[c, b][:], op=ALU.mult)
 
-        def mask_b(c, b):
-            nc.vector.tensor_tensor(out=den[c, b][:], in0=mix_sb[c, b][:], in1=den[c, b][:], op=ALU.mult)
-            g = grp.tile([P, CHUNKS[c], 4], BF16, name="grouped", tag="grouped", align_bytes=64)
-            cast(
-                "VVVVVV"[2 * c + b] == "V",
-                g[:].rearrange("p (c e) i -> p c i e", e=4),
-                den[c, b][:].rearrange("p i (c e) -> p c i e", e=4),
-            )
-            z_g[c, b] = g
-
-        def mask_c(c, b):
-            nc.vector.quantize_mx(
-                out=z_q[c, b][:].bitcast(E4M3), scales=z_s[c, b][:], in_=z_g[c, b][:].rearrange("p m i -> p (m i)")
-            )
-
-        ws = kept("ws", [P, 2, N], I32)
+        ws_w = kept("ws_w", [P, 2, N], I32)
         y_s = kept("y_s", [P, M], U8)
-
         y_banks, y_sb = {}, {}
 
-        def synth_pass(c, a):
-            width = CHUNKS[c]
-            per_bank = 512 // width
+        def masked_mixture(c, b):
+            words = rounded_tile([P, CHUNKS[c], 4])
+            nc.vector.tensor_tensor(out=by_words(words), in0=by_rows(mix_sb[c, b]), in1=by_rows(den[c, b]), op=ALU.mult)
+            quantise(z_q[c, b][:], z_s[c, b][:], words[:].rearrange("p m i -> p (m i)"))
+
+        def synthesis_pass(c, b):
+            per_bank = BANK // CHUNKS[c]
             for g in range(2):
-                for t0 in range(0, 4, per_bank):
-                    if a == 0:
-                        y_banks[c, g, t0] = psum.tile([P, per_bank, width], F32, name="bank", tag=f"bank{(starts[c] * 8 + (4 * g + t0) * width) // 512}")
-                    for t in range(t0, t0 + per_bank):
-                        col = 512 * g + 128 * t
+                for first in range(0, 4, per_bank):
+                    if b == 0:
+                        y_banks[c, g, first] = bank_tile(chunk_bank(c, g, first), [P, per_bank, CHUNKS[c]])
+                    for t in range(first, first + per_bank):
+                        col = PASS * g + P * t
                         nc.tensor.matmul_mx(
-                            out=y_banks[c, g, t0][:, t - t0, :],
-                            lhsT=ws[:, a, col : col + 128].bitcast(E4M3),
-                            lhsT_scale=wss[4 * a : P, col : col + 128],
-                            rhs=z_q[c, a][:].bitcast(E4M3),
-                            rhs_scale=z_s[c, a][:],
-                            start=(a == 0 and t == t0),
-                            stop=(a == 1 and t == t0 + per_bank - 1),
+                            out=y_banks[c, g, first][:, t - first, :],
+                            lhsT=ws_w[:, b, col : col + P].bitcast(E4M3),
+                            lhsT_scale=ws_s[4 * b : P, col : col + P],
+                            rhs=z_q[c, b][:].bitcast(E4M3),
+                            rhs_scale=z_s[c, b][:],
+                            start=(b == 0 and t == first),
+                            stop=(b == 1 and t == first + per_bank - 1),
                         )
 
-        def synthesis(c, g):
-            width = CHUNKS[c]
-            per_bank = 512 // width
-            cols = slice(starts[c], starts[c] + width)
-            y = raw.tile([P, 4, width], F32, name="raw", tag="raw")
-            for t0 in range(0, 4, per_bank):
-                cast(c == len(CHUNKS) - 1 and g == 1, y[:, t0 : t0 + per_bank, :], y_banks[c, g, t0][:])
-            nc.sync.dma_start(out_0[512 * g : 512 * (g + 1), cols].rearrange("(p t) m -> p t m", t=4), y[:])
-            y_sb[c, g] = y
-
-        def planes(c, g):
-            width = CHUNKS[c]
-            cols = slice(starts[c], starts[c] + width)
-            y = y_sb[c, g]
-            yg = grp.tile([P, width, 4], BF16, name="grouped", tag="grouped", align_bytes=64)
-            cast(
-                "VVVVVV"[2 * c + g] == "V",
-                yg[:].rearrange("p (c e) t -> p c t e", e=4),
-                y[:].rearrange("p t (c e) -> p c t e", e=4),
-            )
-            y_q = kept(f"y_q{c}_{g}", [P, width], I32)
-            nc.vector.quantize_mx(
-                out=y_q[:].bitcast(E4M3), scales=y_s[4 * g : P, cols], in_=yg[:].rearrange("p m t -> p (m t)")
-            )
-            nc.sync.dma_start(out_1[g, :, cols, :].rearrange("p m t -> p (m t)").bitcast(I32), y_q[:])
-
-        def deal_ws():
-            nc.vector.tensor_copy(
-                out=ws[:].rearrange("p a (g t m) -> p (a g) m t", g=2, t=4),
-                in_=ws_raw[:].rearrange("p a (g m t) -> p (a g) m t", g=2, t=4),
-            )
-            nc.vector.tensor_copy(
-                out=wss[:].rearrange("p (g t m) -> p g t m", g=2, t=4),
-                in_=wss_raw[:].rearrange("p (g m t) -> p g t m", g=2, t=4),
+        def store_y(c, g):
+            per_bank = BANK // CHUNKS[c]
+            copy = nc.vector.tensor_copy if (c, g) == (last_chunk, 1) else nc.scalar.copy
+            y_sb[c, g] = staged.tile([P, 4, CHUNKS[c]], F32, name="staged", tag="staged")
+            for first in range(0, 4, per_bank):
+                copy(out=y_sb[c, g][:, first : first + per_bank, :], in_=y_banks[c, g, first][:])
+            nc.sync.dma_start(
+                out_0[PASS * g : PASS * (g + 1), chunk_cols(c)].rearrange("(p t) m -> p t m", t=4), y_sb[c, g][:]
             )
 
-        nc_ = len(CHUNKS)
-        def front(c, b):
-            noise_power(c, b)
-            square_x(c, b)
-            denominator(c, b)
-            invert(c, b)
-            numerator(c, b)
-        def back(c, b):
-            mask_b(c, b)
-            mask_c(c, b)
-            synth_pass(c, b)
+        def store_planes(c, g):
+            words = rounded_tile([P, CHUNKS[c], 4])
+            nc.vector.tensor_copy(out=by_words(words), in_=by_rows(y_sb[c, g]))
+            y_q = kept(f"y_q{c}_{g}", [P, CHUNKS[c]], I32)
+            quantise(y_q[:], y_s[4 * g : P, chunk_cols(c)], words[:].rearrange("p m t -> p (m t)"))
+            nc.sync.dma_start(out_1[g, :, chunk_cols(c), :].rearrange("p m t -> p (m t)").bitcast(I32), y_q[:])
+
+        def finish(c, b):
+            masked_mixture(c, b)
+            synthesis_pass(c, b)
             if b == 1:
                 if c > 0:
                     for g in range(2):
-                        planes(c - 1, g)
+                        store_planes(c - 1, g)
                 for g in range(2):
-                    synthesis(c, g)
-                if c == nc_ - 1:
+                    store_y(c, g)
+                if c == last_chunk:
                     for g in range(2):
-                        planes(c, g)
-        def picks_of(c, b):
-            for i in range(4):
-                pick(c, b, i)
+                        store_planes(c, g)
+
         for b in range(2):
             for i in range(4):
                 speech(b, i)
                 pick(0, b, i)
-        quantise_noise(0, 0, "S")
-        quantise_noise(1, 0, "S")
-        quantise_wn(0, 0, "VV")
-        quantise_wn(1, 0, "VV")
-
-        quantise_wn(0, 1, "SS")
-        quantise_wn(1, 1, "SS")
-        front(0, 0)
-        quantise_noise(0, 1, "S")
-        quantise_noise(1, 1, "S")
-        deal_ws()
-        order = units
-        for u, (c, b) in enumerate(order):
-            if u + 2 < len(order) and order[u + 2][0] > 0:
-                picks_of(*order[u + 2])
-            if u + 1 < len(order):
-                front(*order[u + 1])
-            back(c, b)
+        for a in range(2):
+            quantise_noise(a, 0)
+        for b, copy in enumerate((nc.vector.tensor_copy, nc.scalar.copy)):
+            for a in range(2):
+                quantise_wn(a, b, copy)
+        mask_parts(0, 0)
+        for a in range(2):
+            quantise_noise(a, 1)
+        nc.vector.tensor_copy(
+            out=ws_w[:].rearrange("p b (g t m) -> p (b g) m t", g=2, t=4),
+            in_=ws_raw[:].rearrange("p b (g m t) -> p (b g) m t", g=2, t=4),
+        )
+        nc.vector.tensor_copy(
+            out=ws_s[:].rearrange("p (g t m) -> p g t m", g=2, t=4),
+            in_=ws_s_raw[:].rearrange("p (g m t) -> p g t m", g=2, t=4),
+        )
+        for u, (c, b) in enumerate(units):
+            if u + 2 < len(units):
+                for i in range(4):
+                    pick(*units[u + 2], i)
+            if u + 1 < len(units):
+                mask_parts(*units[u + 1])
+            finish(c, b)
         for q in range(4):
             nc.scalar.dma_start(out_2[:, 4 * q : 4 * q + 4, :].bitcast(I32), y_s[32 * q : 32 * q + 8, :].bitcast(I32))

@@ -35,12 +35,14 @@ def tile_list_ratio_mask_synthesis_kernel(
 
     with ExitStack() as ctx:
         keep = ctx.enter_context(tc.tile_pool(name="keep", bufs=1))
-        staged = ctx.enter_context(tc.tile_pool(name="staged", bufs=4))
         rounded = ctx.enter_context(tc.tile_pool(name="rounded", bufs=4))
         psum = ctx.enter_context(tc.psum_pool(name="psum", bufs=1))
 
         def kept(name, shape, dtype):
             return keep.tile(shape, dtype, name=name, align_bytes=64)
+
+        def shared(name, shape, dtype, tag):
+            return keep.tile(shape, dtype, name=name, tag=tag, align_bytes=64)
 
         def rounded_tile(shape):
             return rounded.tile(shape, BF16, name="rounded", tag="rounded", align_bytes=64)
@@ -56,66 +58,87 @@ def tile_list_ratio_mask_synthesis_kernel(
 
         idx = keep.tile([P, S // 16], U16, name="idx")
         idx2 = keep.tile([P, M // 16], U16, name="idx2")
-        tab_s = kept("tab_s", [P, T], U8)
-        tab_w = [kept(f"tab_w{a}", [P, T], I32) for a in range(2)]
-        w4_raw = [kept(f"w4_raw{a}", [P, 2 * H], U8) for a in range(2)]
+        tab_s = shared("tab_s", [P, T], U8, "late")
+        s_raw = shared("s_raw", [P, PASS], U8, "tab1")
+        s_dealt = shared("s_dealt", [P, PASS], U8, "ws")
+        tab_w = [kept("tab_w0", [P, T], I32)]
+        w4_raw = kept("w4_raw", [P, 2, 2 * H], U8)
         w4_w = [kept(f"w4_w{a}", [P, 2 * H], U8) for a in range(2)]
-        w4_s_raw = kept("w4_s_raw", [P, 2, H], U8)
-        w4_s = [kept(f"w4_s{a}", [P, H], U8) for a in range(2)]
-        v_s = [kept(f"v_s{a}", [P, S], U8) for a in range(2)]
+        planes = kept("planes", [P, 2, 2, 2, PASS], U8)
+        v_picked = kept("v_picked", [P, S], U8)
+        v_s = kept("v_s", [P, 2, S], U8)
         v_w = [[kept(f"v_w{a}_{j}", [P, BANK], U32) for j in range(2)] for a in range(2)]
         floor = kept("floor", [P, 16], F32)
-        ws_s_raw = kept("ws_s_raw", [P, N], U8)
-        ws_s = kept("ws_s", [P, N], U8)
-        wgt_sb = kept("wgt_sb", [P, M], F32)
-        ws_raw = kept("ws_raw", [P, 2, N], I32)
 
-        nc.gpsimd.memset(tab_s[:].bitcast(I32), 0)
-        nc.vector.memset(w4_s_raw[:].rearrange("p a c -> p (a c)").bitcast(I32), 0)
+        nc.vector.memset(tab_s[32:64, :].bitcast(I32), 0)
+        nc.vector.memset(tab_s[64:P, :].bitcast(I32), 0)
         nc.vector.memset(floor[:, 0:1], 25.0)
-        nc.gpsimd.memset(v_s[1][:].bitcast(I32), 0)
-        nc.gpsimd.memset(ws_s_raw[:].bitcast(I32), 0)
+        nc.gpsimd.memset(planes[:].rearrange("p a b w c -> p (a b w c)").bitcast(I32), 0)
+        nc.gpsimd.memset(v_s[:].rearrange("p a c -> p (a c)").bitcast(I32), 0)
         mask_floor = floor[:, 8:9]
         nc.scalar.activation(out=mask_floor, in_=floor[:, 0:1], func=ACT.Abs_reciprocal_sqrt)
 
-        noise_raw, wn_raw, mix_sb = {}, {}, {}
+        def gather_words(a, j):
+            nc.vector.tensor_copy(out=v_w[a][j][:], in_=tab_w[a][:].bitcast(U32).indirect(idx[:, 32 * j : 32 * (j + 1)]))
+
+        for w, scales in enumerate((w4_scales, ws_scales)):
+            for a in range(2):
+                nc.sync.dma_start(
+                    s_raw[2 * w + a : P : 4, :].bitcast(I32), scales[a].rearrange("q (b c) -> (q b) c", b=2).bitcast(I32)
+                )
+        nc.sync.dma_start(idx[:], offs)
+        nc.sync.dma_start(tab_s[0:32, :].bitcast(I32), tab_scales.rearrange("a q t -> q a t").bitcast(I32))
+        nc.sync.dma_start(tab_w[0][:], tab_words[0].rearrange("p t i -> p (t i)").bitcast(I32))
+        nc.sync.dma_start(w4_raw[:].bitcast(I32), w4_words.rearrange("a p c -> p a c").bitcast(I32))
+        nc.sync.dma_start(idx2[:], offs2)
+        nc.vector.tensor_copy(
+            out=s_dealt[:].rearrange("p (i m) -> p i m", i=4), in_=s_raw[:].rearrange("p (m i) -> p i m", i=4)
+        )
+        for q in range(4):
+            nc.sync.dma_start(
+                planes[32 * q : 32 * q + 4].rearrange("p a b w c -> p (a b w c)").bitcast(I32),
+                s_dealt[32 * q : 32 * q + 32, :].bitcast(I32),
+            )
+        tab_w.append(shared("tab_w1", [P, T], I32, "tab1"))
+        nc.sync.dma_start(tab_w[1][:], tab_words[1].rearrange("p t i -> p (t i)").bitcast(I32))
+        nc.vector.tensor_copy(out=v_picked[:], in_=tab_s[:].indirect(idx[:]))
+        for q in range(4):
+            nc.sync.dma_start(
+                v_s[32 * q : 32 * q + 4].rearrange("p a c -> p (a c)").bitcast(I32),
+                v_picked[8 * q : 8 * q + 8, :].bitcast(I32),
+            )
+
+        late = shared("late", [P, M + 4 * (2 * M + 2 * H + 2 * M)], F32, "late")
+        wgt_sb = late[:, 0:M]
+
+        def rows(first, width):
+            return late[:, first : first + 4 * width].rearrange("p (j m) -> p j m", j=4)
+
+        noise_raw = {(a, half): rows(M + 4 * HALF * (2 * half + a), HALF) for a in range(2) for half in range(2)}
+        wn_raw = {(a, b): rows(9 * M + 4 * PASS * (2 * b + a), PASS) for a in range(2) for b in range(2)}
+        mix_sb = {(c, b): rows(25 * M + 8 * starts[c] + 4 * b * CHUNKS[c], CHUNKS[c]) for c, b in units}
+        y_sb = {(c, g): rows(9 * M + 8 * starts[c] + 4 * g * CHUNKS[c], CHUNKS[c]) for c, g in units}
 
         def load_noise(a, half):
-            noise_raw[a, half] = kept(f"noise_raw{a}_{half}", [P, 4, HALF], F32)
             nc.sync.dma_start(
-                noise_raw[a, half][:],
+                noise_raw[a, half],
                 noise[PASS * a : PASS * (a + 1), HALF * half : HALF * (half + 1)].rearrange("(p j) m -> p j m", j=4),
             )
 
         def load_wn(a, b):
-            wn_raw[a, b] = staged.tile([P, 4, PASS], F32, name="staged", tag="staged")
             nc.sync.dma_start(
-                wn_raw[a, b][:],
+                wn_raw[a, b],
                 wn[PASS * a : PASS * (a + 1), PASS * b : PASS * (b + 1)].rearrange("(p j) c -> p j c", j=4),
             )
 
         def load_mix(c, b):
-            mix_sb[c, b] = kept(f"mix{c}_{b}", [P, 4, CHUNKS[c]], F32)
             nc.sync.dma_start(
-                mix_sb[c, b][:], mix[PASS * b : PASS * (b + 1), chunk_cols(c)].rearrange("(p i) m -> p i m", i=4)
+                mix_sb[c, b], mix[PASS * b : PASS * (b + 1), chunk_cols(c)].rearrange("(p i) m -> p i m", i=4)
             )
 
-        nc.sync.dma_start(idx[:], offs)
-        nc.sync.dma_start(w4_raw[0][:].bitcast(I32), w4_words[0].bitcast(I32))
-        for q in range(4):
-            nc.sync.dma_start(tab_s[32 * q : 32 * q + 8, :].bitcast(I32), tab_scales[:, 4 * q : 4 * q + 4, :].bitcast(I32))
-        nc.sync.dma_start(w4_raw[1][:].bitcast(I32), w4_words[1].bitcast(I32))
-        for a in range(2):
-            nc.sync.dma_start(tab_w[a][:], tab_words[a].rearrange("p t i -> p (t i)").bitcast(I32))
-        for q in range(4):
-            nc.sync.dma_start(
-                w4_s_raw[32 * q : 32 * q + 4, :, :].bitcast(I32),
-                w4_scales[:, 4 * q : 4 * q + 4, :].rearrange("a r c -> r a c").bitcast(I32),
-            )
         for a in range(2):
             load_noise(a, 0)
-        nc.sync.dma_start(idx2[:], offs2)
-        nc.sync.dma_start(wgt_sb[:], wgt)
+        nc.sync.dma_start(wgt_sb, wgt)
         for b in range(2):
             for a in range(2):
                 load_wn(a, b)
@@ -123,54 +146,39 @@ def tile_list_ratio_mask_synthesis_kernel(
             load_noise(a, 1)
         for b in range(2):
             load_mix(0, b)
-        for q in range(4):
-            nc.sync.dma_start(ws_s_raw[32 * q : 32 * q + 8, :].bitcast(I32), ws_scales[:, 4 * q : 4 * q + 4, :].bitcast(I32))
+        ws_raw = shared("ws_raw", [P, 2, N], I32, "ws")
         nc.sync.dma_start(ws_raw[:], ws_words.rearrange("a p c i -> p a (c i)").bitcast(I32))
         for c, b in units[2:]:
             load_mix(c, b)
 
-        def gather_words(a, j):
-            nc.vector.tensor_copy(out=v_w[a][j][:], in_=tab_w[a][:].bitcast(U32).indirect(idx[:, 32 * j : 32 * (j + 1)]))
-
-        def deal_w4_scales(a):
-            nc.vector.tensor_copy(
-                out=w4_s[a][:].rearrange("p (b i m) -> p b i m", b=2, i=4),
-                in_=w4_s_raw[:, a, :].rearrange("p (b m i) -> p b i m", b=2, i=4),
-            )
-
+        gather_words(0, 0)
         for a in range(2):
             nc.vector.tensor_copy(
                 out=w4_w[a][:].bitcast(U16).rearrange("p (b i m) -> p b i m", b=2, i=4),
-                in_=w4_raw[a][:].bitcast(U16).rearrange("p (b m i) -> p b i m", b=2, i=4),
+                in_=w4_raw[:, a, :].bitcast(U16).rearrange("p (b m i) -> p b i m", b=2, i=4),
             )
-        nc.vector.tensor_copy(out=v_s[0][:], in_=tab_s[:].indirect(idx[:]))
-        nc.scalar.dma_start(v_s[1][0:112, :].bitcast(I32), v_s[0][4:116, :].bitcast(I32))
-        gather_words(0, 0)
-        gather_words(0, 1)
-        deal_w4_scales(0)
         gather_words(1, 0)
-        deal_w4_scales(1)
+        gather_words(0, 1)
         gather_words(1, 1)
 
         h = {(b, i): kept(f"h{b}_{i}", [P, S], F32) for b in range(2) for i in range(4)}
         x = {}
         den = {(c, b): kept(f"den{c}_{b}", [P, 4, CHUNKS[c]], F32) for c, b in units}
 
-        def speech(b, i):
+        def speech(b, i, j):
             col = PASS * b + P * i
-            for j in range(2):
-                bank = bank_tile(2 * i + j, [P, BANK])
-                for a in range(2):
-                    nc.tensor.matmul_mx(
-                        out=bank[:],
-                        lhsT=w4_w[a][:, 2 * col : 2 * (col + P)].bitcast(E2M1),
-                        lhsT_scale=w4_s[a][:, col : col + P],
-                        rhs=v_w[a][j][:].bitcast(E4M3),
-                        rhs_scale=v_s[a][:, BANK * j : BANK * (j + 1)],
-                        start=(a == 0),
-                        stop=(a == 1),
-                    )
-                nc.scalar.copy(out=h[b, i][:, BANK * j : BANK * (j + 1)], in_=bank[:])
+            bank = bank_tile(2 * i + j, [P, BANK])
+            for a in range(2):
+                nc.tensor.matmul_mx(
+                    out=bank[:],
+                    lhsT=w4_w[a][:, 2 * col : 2 * (col + P)].bitcast(E2M1),
+                    lhsT_scale=planes[:, b, 0, a, P * i : P * (i + 1)],
+                    rhs=v_w[a][j][:].bitcast(E4M3),
+                    rhs_scale=v_s[:, a, BANK * j : BANK * (j + 1)],
+                    start=(a == 0),
+                    stop=(a == 1),
+                )
+            nc.scalar.copy(out=h[b, i][:, BANK * j : BANK * (j + 1)], in_=bank[:])
 
         def pick(c, b, i):
             if i == 0:
@@ -189,7 +197,7 @@ def tile_list_ratio_mask_synthesis_kernel(
         wn_s = {(a, b): kept(f"wn_s{a}_{b}", [P, PASS], U8) for a in range(2) for b in range(2)}
 
         def by_rows(tile):
-            return tile[:].rearrange("p j (c e) -> p c j e", e=4)
+            return tile.rearrange("p j (c e) -> p c j e", e=4)
 
         def by_words(tile):
             return tile[:].rearrange("p (c e) j -> p c j e", e=4)
@@ -197,9 +205,9 @@ def tile_list_ratio_mask_synthesis_kernel(
         def quantise(codes, scales, words):
             nc.vector.quantize_mx(out=codes.bitcast(E4M3), scales=scales, in_=words)
 
-        def quantise_noise(a, half):
+        def quantise_noise(a, half, copy):
             words = rounded_tile([P, HALF, 4])
-            nc.scalar.copy(out=by_words(words), in_=by_rows(noise_raw[a, half]))
+            copy(out=by_words(words), in_=by_rows(noise_raw[a, half]))
             quantise(noise_q[a, half][:], noise_s[a, half][:], words[:].rearrange("p m j -> p (m j)"))
 
         def quantise_wn(a, b, copy):
@@ -208,7 +216,7 @@ def tile_list_ratio_mask_synthesis_kernel(
                 slots = slice(2 * pair, 2 * pair + 2)
                 copy(
                     out=words[:, slots, :, :].rearrange("p i m j -> p m j i"),
-                    in_=wn_raw[a, b][:].rearrange("p j (m i) -> p m j i", i=4)[:, :, :, slots],
+                    in_=wn_raw[a, b].rearrange("p j (m i) -> p m j i", i=4)[:, :, :, slots],
                 )
             quantise(wn_q[a, b][:], wn_s[a, b][:], words[:].rearrange("p i m j -> p (i m j)"))
 
@@ -247,15 +255,15 @@ def tile_list_ratio_mask_synthesis_kernel(
             )
             nc.scalar.activation(out=den[c, b][:], in_=den[c, b][:], func=ACT.Abs_reciprocal_sqrt)
             nc.scalar.activation(out=den[c, b][:], in_=den[c, b][:], func=ACT.Square)
-            nc.vector.tensor_tensor(out=mix_sb[c, b][:], in0=x[c, b][:], in1=mix_sb[c, b][:], op=ALU.mult)
+            nc.vector.tensor_tensor(out=mix_sb[c, b], in0=x[c, b][:], in1=mix_sb[c, b], op=ALU.mult)
 
         ws_w = kept("ws_w", [P, 2, N], I32)
         y_s = kept("y_s", [P, M], U8)
-        y_banks, y_sb = {}, {}
+        y_banks = {}
 
         def masked_mixture(c, b):
             words = rounded_tile([P, CHUNKS[c], 4])
-            nc.vector.tensor_tensor(out=by_words(words), in0=by_rows(mix_sb[c, b]), in1=by_rows(den[c, b]), op=ALU.mult)
+            nc.vector.tensor_tensor(out=by_words(words), in0=by_rows(mix_sb[c, b]), in1=by_rows(den[c, b][:]), op=ALU.mult)
             quantise(z_q[c, b][:], z_s[c, b][:], words[:].rearrange("p m i -> p (m i)"))
 
         def synthesis_pass(c, b):
@@ -269,7 +277,7 @@ def tile_list_ratio_mask_synthesis_kernel(
                         nc.tensor.matmul_mx(
                             out=y_banks[c, g, first][:, t - first, :],
                             lhsT=ws_w[:, b, col : col + P].bitcast(E4M3),
-                            lhsT_scale=ws_s[4 * b : P, col : col + P],
+                            lhsT_scale=planes[:, g, 1, b, P * t : P * (t + 1)],
                             rhs=z_q[c, b][:].bitcast(E4M3),
                             rhs_scale=z_s[c, b][:],
                             start=(b == 0 and t == first),
@@ -279,11 +287,10 @@ def tile_list_ratio_mask_synthesis_kernel(
         def store_y(c, g):
             per_bank = BANK // CHUNKS[c]
             copy = nc.vector.tensor_copy if (c, g) == (last_chunk, 1) else nc.scalar.copy
-            y_sb[c, g] = staged.tile([P, 4, CHUNKS[c]], F32, name="staged", tag="staged")
             for first in range(0, 4, per_bank):
                 copy(out=y_sb[c, g][:, first : first + per_bank, :], in_=y_banks[c, g, first][:])
             nc.sync.dma_start(
-                out_0[PASS * g : PASS * (g + 1), chunk_cols(c)].rearrange("(p t) m -> p t m", t=4), y_sb[c, g][:]
+                out_0[PASS * g : PASS * (g + 1), chunk_cols(c)].rearrange("(p t) m -> p t m", t=4), y_sb[c, g]
             )
 
         def store_planes(c, g):
@@ -306,25 +313,26 @@ def tile_list_ratio_mask_synthesis_kernel(
                     for g in range(2):
                         store_planes(c, g)
 
-        for b in range(2):
-            for i in range(4):
-                speech(b, i)
-                pick(0, b, i)
+        for i in range(4):
+            speech(0, i, 0)
+        for i in range(4):
+            speech(0, i, 1)
+            pick(0, 0, i)
+        for i in range(4):
+            for j in range(2):
+                speech(1, i, j)
+            pick(0, 1, i)
         for a in range(2):
-            quantise_noise(a, 0)
+            quantise_noise(a, 0, nc.vector.tensor_copy)
         for b, copy in enumerate((nc.vector.tensor_copy, nc.scalar.copy)):
             for a in range(2):
                 quantise_wn(a, b, copy)
         mask_parts(0, 0)
         for a in range(2):
-            quantise_noise(a, 1)
+            quantise_noise(a, 1, nc.scalar.copy)
         nc.vector.tensor_copy(
             out=ws_w[:].rearrange("p b (g t m) -> p (b g) m t", g=2, t=4),
             in_=ws_raw[:].rearrange("p b (g m t) -> p (b g) m t", g=2, t=4),
-        )
-        nc.vector.tensor_copy(
-            out=ws_s[:].rearrange("p (g t m) -> p g t m", g=2, t=4),
-            in_=ws_s_raw[:].rearrange("p (g m t) -> p g t m", g=2, t=4),
         )
         for u, (c, b) in enumerate(units):
             if u + 2 < len(units):

@@ -20,7 +20,7 @@ E2M1 = mybir.dt.float4_e2m1fn_x4
 ACT = mybir.ActivationFunctionType
 ALU = mybir.AluOpType
 
-CHUNKS = [256, 128, 128]
+CHUNKS = [128, 128, 128, 128]
 PICK_TILES = 3
 
 
@@ -114,16 +114,10 @@ def tile_list_ratio_mask_synthesis_kernel(
         def rows(first, width):
             return late[:, first : first + 4 * width].rearrange("p (j m) -> p j m", j=4)
 
-        noise_raw = {(a, half): rows(M + 4 * HALF * (2 * half + a), HALF) for a in range(2) for half in range(2)}
+        noise_all = [rows(M + 4 * M * a, M) for a in range(2)]
         wn_raw = {(a, b): rows(9 * M + 4 * PASS * (2 * b + a), PASS) for a in range(2) for b in range(2)}
-        mix_sb = {(c, b): rows(25 * M + 8 * starts[c] + 4 * b * CHUNKS[c], CHUNKS[c]) for c, b in units}
-        y_sb = {(c, g): rows(9 * M + 8 * starts[c] + 4 * g * CHUNKS[c], CHUNKS[c]) for c, g in units}
-
-        def load_noise(a, half):
-            nc.sync.dma_start(
-                noise_raw[a, half],
-                noise[PASS * a : PASS * (a + 1), HALF * half : HALF * (half + 1)].rearrange("(p j) m -> p j m", j=4),
-            )
+        mix_all = [rows(25 * M + 4 * M * b, M) for b in range(2)]
+        y_sb = {(c, g): rows(M + 8 * starts[c] + 4 * g * CHUNKS[c], CHUNKS[c]) for c, g in units}
 
         def load_wn(a, b):
             nc.sync.dma_start(
@@ -131,25 +125,19 @@ def tile_list_ratio_mask_synthesis_kernel(
                 wn[PASS * a : PASS * (a + 1), PASS * b : PASS * (b + 1)].rearrange("(p j) c -> p j c", j=4),
             )
 
-        def load_mix(c, b):
-            nc.sync.dma_start(
-                mix_sb[c, b], mix[PASS * b : PASS * (b + 1), chunk_cols(c)].rearrange("(p i) m -> p i m", i=4)
-            )
+        def load_rows(tile, source, a):
+            nc.sync.dma_start(tile, source[PASS * a : PASS * (a + 1), :].rearrange("(p j) m -> p j m", j=4))
 
         for a in range(2):
-            load_noise(a, 0)
+            load_rows(noise_all[a], noise, a)
         nc.sync.dma_start(wgt_sb, wgt)
         for b in range(2):
             for a in range(2):
                 load_wn(a, b)
-        for a in range(2):
-            load_noise(a, 1)
-        for b in range(2):
-            load_mix(0, b)
+        load_rows(mix_all[0], mix, 0)
         ws_raw = shared("ws_raw", [P, 2, N], I32, "ws")
         nc.sync.dma_start(ws_raw[:], ws_words.rearrange("a p c i -> p a (c i)").bitcast(I32))
-        for c, b in units[2:]:
-            load_mix(c, b)
+        load_rows(mix_all[1], mix, 1)
 
         gather_words(0, 0)
         for a in range(2):
@@ -162,8 +150,8 @@ def tile_list_ratio_mask_synthesis_kernel(
         gather_words(1, 1)
 
         h = {(b, i): kept(f"h{b}_{i}", [P, S], F32) for b in range(2) for i in range(4)}
-        x = {}
-        den = {(c, b): kept(f"den{c}_{b}", [P, 4, CHUNKS[c]], F32) for c, b in units}
+        x = [kept("x0", [P, 4, M], F32)[:], wn_raw[1, 0]]
+        den = [kept(f"den{b}", [P, 4, M], F32) for b in range(2)]
 
         def speech(b, i, j):
             col = PASS * b + P * i
@@ -180,19 +168,11 @@ def tile_list_ratio_mask_synthesis_kernel(
                 )
             nc.scalar.copy(out=h[b, i][:, BANK * j : BANK * (j + 1)], in_=bank[:])
 
-        def pick(c, b, i):
-            if i == 0:
-                tag = f"x{units.index((c, b)) % PICK_TILES}"
-                x[c, b] = keep.tile([P, 4, CHUNKS[c]], F32, name="x", tag=tag, align_bytes=64)
-            nc.vector.tensor_tensor(
-                out=x[c, b][:, i, :],
-                in0=h[b, i][:].indirect(idx2[:, starts[c] // 16 : (starts[c] + CHUNKS[c]) // 16]),
-                in1=wgt_sb[:, chunk_cols(c)],
-                op=ALU.mult,
-            )
+        def pick(b, i):
+            nc.vector.tensor_tensor(out=x[b][:, i, :], in0=h[b, i][:].indirect(idx2[:]), in1=wgt_sb, op=ALU.mult)
 
-        noise_q = {(a, half): kept(f"noise_q{a}_{half}", [P, HALF], U32) for a in range(2) for half in range(2)}
-        noise_s = {(a, half): kept(f"noise_s{a}_{half}", [P, HALF], U8) for a in range(2) for half in range(2)}
+        noise_q = [kept(f"noise_q{a}", [P, M], U32) for a in range(2)]
+        noise_s = [kept(f"noise_s{a}", [P, M], U8) for a in range(2)]
         wn_q = {(a, b): kept(f"wn_q{a}_{b}", [P, PASS], U32) for a in range(2) for b in range(2)}
         wn_s = {(a, b): kept(f"wn_s{a}_{b}", [P, PASS], U8) for a in range(2) for b in range(2)}
 
@@ -200,15 +180,15 @@ def tile_list_ratio_mask_synthesis_kernel(
             return tile.rearrange("p j (c e) -> p c j e", e=4)
 
         def by_words(tile):
-            return tile[:].rearrange("p (c e) j -> p c j e", e=4)
+            return tile.rearrange("p (c e) j -> p c j e", e=4)
 
         def quantise(codes, scales, words):
             nc.vector.quantize_mx(out=codes.bitcast(E4M3), scales=scales, in_=words)
 
-        def quantise_noise(a, half, copy):
-            words = rounded_tile([P, HALF, 4])
-            copy(out=by_words(words), in_=by_rows(noise_raw[a, half]))
-            quantise(noise_q[a, half][:], noise_s[a, half][:], words[:].rearrange("p m j -> p (m j)"))
+        def quantise_noise(a, copy):
+            words = rounded_tile([P, M, 4])
+            copy(out=by_words(words[:]), in_=by_rows(noise_all[a]))
+            quantise(noise_q[a][:], noise_s[a][:], words[:].rearrange("p m j -> p (m j)"))
 
         def quantise_wn(a, b, copy):
             words = rounded_tile([P, 4, P, 4])
@@ -220,51 +200,46 @@ def tile_list_ratio_mask_synthesis_kernel(
                 )
             quantise(wn_q[a, b][:], wn_s[a, b][:], words[:].rearrange("p i m j -> p (i m j)"))
 
-        def noise_power(c, b):
-            half = starts[c] // HALF
-            cols = slice(starts[c] % HALF, starts[c] % HALF + CHUNKS[c])
-            per_bank = BANK // CHUNKS[c]
-            for first in range(0, 4, per_bank):
-                bank = bank_tile(chunk_bank(c, b, first), [P, per_bank, CHUNKS[c]])
-                for i in range(first, first + per_bank):
-                    for a in range(2):
-                        nc.tensor.matmul_mx(
-                            out=bank[:, i - first, :],
-                            lhsT=wn_q[a, b][:, P * i : P * (i + 1)].bitcast(E4M3),
-                            lhsT_scale=wn_s[a, b][:, P * i : P * (i + 1)],
-                            rhs=noise_q[a, half][:, cols].bitcast(E4M3),
-                            rhs_scale=noise_s[a, half][:, cols],
-                            start=(a == 0),
-                            stop=(a == 1),
-                        )
-                nc.scalar.activation(out=den[c, b][:, first : first + per_bank, :], in_=bank[:], func=ACT.Square)
+        def noise_power(b):
+            for i in range(4):
+                bank = bank_tile(4 * b + i, [P, M])
+                for a in range(2):
+                    nc.tensor.matmul_mx(
+                        out=bank[:],
+                        lhsT=wn_q[a, b][:, P * i : P * (i + 1)].bitcast(E4M3),
+                        lhsT_scale=wn_s[a, b][:, P * i : P * (i + 1)],
+                        rhs=noise_q[a][:].bitcast(E4M3),
+                        rhs_scale=noise_s[a][:],
+                        start=(a == 0),
+                        stop=(a == 1),
+                    )
+                nc.scalar.activation(out=den[b][:, i, :], in_=bank[:], func=ACT.Square)
 
-        z_q = {(c, b): kept(f"z_q{c}_{b}", [P, CHUNKS[c]], U32) for c, b in units}
-        z_s = {(c, b): kept(f"z_s{c}_{b}", [P, CHUNKS[c]], U8) for c, b in units}
+        z_q = [kept(f"z_q{b}", [P, M], U32) for b in range(2)]
+        z_s = [kept(f"z_s{b}", [P, M], U8) for b in range(2)]
 
-        def mask_parts(c, b):
-            noise_power(c, b)
-            nc.scalar.activation(out=x[c, b][:], in_=x[c, b][:], func=ACT.Square)
-            nc.vector.scalar_tensor_tensor(
-                out=den[c, b][:].rearrange("p i m -> p (i m)"),
-                in0=x[c, b][:].rearrange("p i m -> p (i m)"),
-                scalar=mask_floor,
-                in1=den[c, b][:].rearrange("p i m -> p (i m)"),
-                op0=ALU.add,
-                op1=ALU.add,
+        def square(b, cols):
+            nc.scalar.activation(out=x[b][:, :, cols], in_=x[b][:, :, cols], func=ACT.Square)
+
+        def numerator(b, cols):
+            nc.vector.tensor_tensor(out=mix_all[b][:, :, cols], in0=x[b][:, :, cols], in1=mix_all[b][:, :, cols], op=ALU.mult)
+
+        def inverse(b, cols):
+            part = den[b][:, :, cols]
+            nc.vector.tensor_tensor(out=part, in0=x[b][:, :, cols], in1=part, op=ALU.add)
+            nc.scalar.activation(out=part, in_=part, func=ACT.Abs_reciprocal_sqrt, bias=mask_floor)
+            nc.scalar.activation(out=part, in_=part, func=ACT.Square)
+
+        def masked_mixture(b, cols):
+            words = rounded_tile([P, cols.stop - cols.start, 4])
+            nc.vector.tensor_tensor(
+                out=by_words(words[:]), in0=by_rows(mix_all[b][:, :, cols]), in1=by_rows(den[b][:, :, cols]), op=ALU.mult
             )
-            nc.scalar.activation(out=den[c, b][:], in_=den[c, b][:], func=ACT.Abs_reciprocal_sqrt)
-            nc.scalar.activation(out=den[c, b][:], in_=den[c, b][:], func=ACT.Square)
-            nc.vector.tensor_tensor(out=mix_sb[c, b], in0=x[c, b][:], in1=mix_sb[c, b], op=ALU.mult)
+            quantise(z_q[b][:, cols], z_s[b][:, cols], words[:].rearrange("p m i -> p (m i)"))
 
         ws_w = kept("ws_w", [P, 2, N], I32)
         y_s = kept("y_s", [P, M], U8)
         y_banks = {}
-
-        def masked_mixture(c, b):
-            words = rounded_tile([P, CHUNKS[c], 4])
-            nc.vector.tensor_tensor(out=by_words(words), in0=by_rows(mix_sb[c, b]), in1=by_rows(den[c, b][:]), op=ALU.mult)
-            quantise(z_q[c, b][:], z_s[c, b][:], words[:].rearrange("p m i -> p (m i)"))
 
         def synthesis_pass(c, b):
             per_bank = BANK // CHUNKS[c]
@@ -278,8 +253,8 @@ def tile_list_ratio_mask_synthesis_kernel(
                             out=y_banks[c, g, first][:, t - first, :],
                             lhsT=ws_w[:, b, col : col + P].bitcast(E4M3),
                             lhsT_scale=planes[:, g, 1, b, P * t : P * (t + 1)],
-                            rhs=z_q[c, b][:].bitcast(E4M3),
-                            rhs_scale=z_s[c, b][:],
+                            rhs=z_q[b][:, chunk_cols(c)].bitcast(E4M3),
+                            rhs_scale=z_s[b][:, chunk_cols(c)],
                             start=(b == 0 and t == first),
                             stop=(b == 1 and t == first + per_bank - 1),
                         )
@@ -295,51 +270,58 @@ def tile_list_ratio_mask_synthesis_kernel(
 
         def store_planes(c, g):
             words = rounded_tile([P, CHUNKS[c], 4])
-            nc.vector.tensor_copy(out=by_words(words), in_=by_rows(y_sb[c, g]))
+            nc.vector.tensor_copy(out=by_words(words[:]), in_=by_rows(y_sb[c, g]))
             y_q = kept(f"y_q{c}_{g}", [P, CHUNKS[c]], I32)
             quantise(y_q[:], y_s[4 * g : P, chunk_cols(c)], words[:].rearrange("p m t -> p (m t)"))
             nc.sync.dma_start(out_1[g, :, chunk_cols(c), :].rearrange("p m t -> p (m t)").bitcast(I32), y_q[:])
 
-        def finish(c, b):
-            masked_mixture(c, b)
-            synthesis_pass(c, b)
-            if b == 1:
-                if c > 0:
-                    for g in range(2):
-                        store_planes(c - 1, g)
-                for g in range(2):
-                    store_y(c, g)
-                if c == last_chunk:
-                    for g in range(2):
-                        store_planes(c, g)
-
+        whole = slice(0, M)
+        halves = [slice(0, HALF), slice(HALF, M)]
         for i in range(4):
             speech(0, i, 0)
         for i in range(4):
             speech(0, i, 1)
-            pick(0, 0, i)
+            pick(0, i)
         for i in range(4):
             for j in range(2):
                 speech(1, i, j)
-            pick(0, 1, i)
-        for a in range(2):
-            quantise_noise(a, 0, nc.vector.tensor_copy)
-        for b, copy in enumerate((nc.vector.tensor_copy, nc.scalar.copy)):
-            for a in range(2):
-                quantise_wn(a, b, copy)
-        mask_parts(0, 0)
-        for a in range(2):
-            quantise_noise(a, 1, nc.scalar.copy)
+        quantise_noise(0, nc.vector.tensor_copy)
+        quantise_noise(1, nc.vector.tensor_copy)
+        quantise_wn(0, 0, nc.vector.tensor_copy)
+        quantise_wn(1, 0, nc.vector.tensor_copy)
+        square(0, whole)
+        noise_power(0)
+        for cols in halves:
+            inverse(0, cols)
+        quantise_wn(0, 1, nc.scalar.copy)
+        quantise_wn(1, 1, nc.scalar.copy)
+        for i in range(4):
+            pick(1, i)
+        noise_power(1)
+        for c in range(len(CHUNKS)):
+            square(1, chunk_cols(c))
+        numerator(0, whole)
         nc.vector.tensor_copy(
             out=ws_w[:].rearrange("p b (g t m) -> p (b g) m t", g=2, t=4),
             in_=ws_raw[:].rearrange("p b (g m t) -> p (b g) m t", g=2, t=4),
         )
-        for u, (c, b) in enumerate(units):
-            if u + 2 < len(units):
-                for i in range(4):
-                    pick(*units[u + 2], i)
-            if u + 1 < len(units):
-                mask_parts(*units[u + 1])
-            finish(c, b)
+        for cols in halves:
+            masked_mixture(0, cols)
+        for c in range(len(CHUNKS)):
+            synthesis_pass(c, 0)
+        inverse(1, chunk_cols(0))
+        for c in range(len(CHUNKS)):
+            if c < last_chunk:
+                inverse(1, chunk_cols(c + 1))
+            numerator(1, chunk_cols(c))
+            masked_mixture(1, chunk_cols(c))
+            synthesis_pass(c, 1)
+            if c > 0:
+                for g in range(2):
+                    store_planes(c - 1, g)
+            for g in range(2):
+                store_y(c, g)
+        for g in range(2):
+            store_planes(last_chunk, g)
         for q in range(4):
             nc.scalar.dma_start(out_2[:, 4 * q : 4 * q + 4, :].bitcast(I32), y_s[32 * q : 32 * q + 8, :].bitcast(I32))

@@ -20,7 +20,7 @@ E2M1 = mybir.dt.float4_e2m1fn_x4
 ACT = mybir.ActivationFunctionType
 ALU = mybir.AluOpType
 
-CHUNKS = [128, 128, 128, 128]
+CHUNKS = [256, 128, 128]
 PICK_TILES = 3
 
 
@@ -67,7 +67,7 @@ def tile_list_ratio_mask_synthesis_kernel(
         planes = kept("planes", [P, 2, 2, 2, PASS], U8)
         v_picked = kept("v_picked", [P, S], U8)
         v_s = kept("v_s", [P, 2, S], U8)
-        v_w = [[kept(f"v_w{a}_{j}", [P, BANK], U32) for j in range(2)] for a in range(2)]
+        v_w = [[shared("v_w", [P, BANK], U32, f"v_w{a}_{j}") for j in range(2)] for a in range(2)]
         floor = kept("floor", [P, 16], F32)
 
         nc.vector.memset(tab_s[32:64, :].bitcast(I32), 0)
@@ -149,8 +149,8 @@ def tile_list_ratio_mask_synthesis_kernel(
         gather_words(0, 1)
         gather_words(1, 1)
 
-        h = {(b, i): kept(f"h{b}_{i}", [P, S], F32) for b in range(2) for i in range(4)}
-        x = [kept("x0", [P, 4, M], F32)[:], wn_raw[1, 0]]
+        h = {(b, i): shared("h", [P, S], F32, f"h{b}_{i}") for b in range(2) for i in range(4)}
+        x = [kept("x0", [P, 4, M], F32)[:], kept("x1", [P, 4, M], F32)[:]]
         den = [kept(f"den{b}", [P, 4, M], F32) for b in range(2)]
 
         def speech(b, i, j):
@@ -169,7 +169,7 @@ def tile_list_ratio_mask_synthesis_kernel(
             nc.scalar.copy(out=h[b, i][:, BANK * j : BANK * (j + 1)], in_=bank[:])
 
         def pick(b, i):
-            nc.vector.tensor_tensor(out=x[b][:, i, :], in0=h[b, i][:].indirect(idx2[:]), in1=wgt_sb, op=ALU.mult)
+            nc.vector.tensor_tensor(out=picked[b][:, i, :], in0=h[b, i][:].indirect(idx2[:]), in1=wgt_sb, op=ALU.mult)
 
         noise_q = [kept(f"noise_q{a}", [P, M], U32) for a in range(2)]
         noise_s = [kept(f"noise_s{a}", [P, M], U8) for a in range(2)]
@@ -200,29 +200,34 @@ def tile_list_ratio_mask_synthesis_kernel(
                 )
             quantise(wn_q[a, b][:], wn_s[a, b][:], words[:].rearrange("p i m j -> p (i m j)"))
 
-        def noise_power(b):
-            for i in range(4):
-                bank = bank_tile(4 * b + i, [P, M])
-                for a in range(2):
-                    nc.tensor.matmul_mx(
-                        out=bank[:],
-                        lhsT=wn_q[a, b][:, P * i : P * (i + 1)].bitcast(E4M3),
-                        lhsT_scale=wn_s[a, b][:, P * i : P * (i + 1)],
-                        rhs=noise_q[a][:].bitcast(E4M3),
-                        rhs_scale=noise_s[a][:],
-                        start=(a == 0),
-                        stop=(a == 1),
-                    )
-                nc.scalar.activation(out=den[b][:, i, :], in_=bank[:], func=ACT.Square)
+        def noise_power(c, b):
+            per_bank = BANK // CHUNKS[c]
+            for first in range(0, 4, per_bank):
+                bank = bank_tile(chunk_bank(c, b, first), [P, per_bank, CHUNKS[c]])
+                for i in range(first, first + per_bank):
+                    for a in range(2):
+                        nc.tensor.matmul_mx(
+                            out=bank[:, i - first, :],
+                            lhsT=wn_q[a, b][:, P * i : P * (i + 1)].bitcast(E4M3),
+                            lhsT_scale=wn_s[a, b][:, P * i : P * (i + 1)],
+                            rhs=noise_q[a][:, chunk_cols(c)].bitcast(E4M3),
+                            rhs_scale=noise_s[a][:, chunk_cols(c)],
+                            start=(a == 0),
+                            stop=(a == 1),
+                        )
+                nc.scalar.activation(out=den[b][:, first : first + per_bank, chunk_cols(c)], in_=bank[:], func=ACT.Square)
 
         z_q = [kept(f"z_q{b}", [P, M], U32) for b in range(2)]
         z_s = [kept(f"z_s{b}", [P, M], U8) for b in range(2)]
 
+        picked = list(x)
+        x[0] = shared("x_squared", [P, 4, M], F32, "v_w1_1")[:]
+
         def square(b, cols):
-            nc.scalar.activation(out=x[b][:, :, cols], in_=x[b][:, :, cols], func=ACT.Square)
+            nc.scalar.activation(out=x[b][:, :, cols], in_=picked[b][:, :, cols], func=ACT.Square)
 
         def numerator(b, cols):
-            nc.vector.tensor_tensor(out=mix_all[b][:, :, cols], in0=x[b][:, :, cols], in1=mix_all[b][:, :, cols], op=ALU.mult)
+            nc.vector.tensor_tensor(out=x[b][:, :, cols], in0=x[b][:, :, cols], in1=mix_all[b][:, :, cols], op=ALU.mult)
 
         def inverse(b, cols):
             part = den[b][:, :, cols]
@@ -233,11 +238,11 @@ def tile_list_ratio_mask_synthesis_kernel(
         def masked_mixture(b, cols):
             words = rounded_tile([P, cols.stop - cols.start, 4])
             nc.vector.tensor_tensor(
-                out=by_words(words[:]), in0=by_rows(mix_all[b][:, :, cols]), in1=by_rows(den[b][:, :, cols]), op=ALU.mult
+                out=by_words(words[:]), in0=by_rows(x[b][:, :, cols]), in1=by_rows(den[b][:, :, cols]), op=ALU.mult
             )
             quantise(z_q[b][:, cols], z_s[b][:, cols], words[:].rearrange("p m i -> p (m i)"))
 
-        ws_w = kept("ws_w", [P, 2, N], I32)
+        ws_w = shared("ws_w", [P, 2, N], I32, "h1_3")
         y_s = kept("y_s", [P, M], U8)
         y_banks = {}
 
@@ -275,8 +280,22 @@ def tile_list_ratio_mask_synthesis_kernel(
             quantise(y_q[:], y_s[4 * g : P, chunk_cols(c)], words[:].rearrange("p m t -> p (m t)"))
             nc.sync.dma_start(out_1[g, :, chunk_cols(c), :].rearrange("p m t -> p (m t)").bitcast(I32), y_q[:])
 
+        def deal_ws():
+            nc.vector.tensor_copy(
+                out=ws_w[:].rearrange("p b (g t m) -> p (b g) m t", g=2, t=4),
+                in_=ws_raw[:].rearrange("p b (g m t) -> p (b g) m t", g=2, t=4),
+            )
+
+        def finish(c, b):
+            masked_mixture(b, chunk_cols(c))
+            synthesis_pass(c, b)
+
+        def store_both(store, c):
+            for g in range(2):
+                store(c, g)
+
         whole = slice(0, M)
-        halves = [slice(0, HALF), slice(HALF, M)]
+        on_vector, on_scalar = nc.vector.tensor_copy, nc.scalar.copy
         for i in range(4):
             speech(0, i, 0)
         for i in range(4):
@@ -285,43 +304,37 @@ def tile_list_ratio_mask_synthesis_kernel(
         for i in range(4):
             for j in range(2):
                 speech(1, i, j)
-        quantise_noise(0, nc.vector.tensor_copy)
-        quantise_noise(1, nc.vector.tensor_copy)
-        quantise_wn(0, 0, nc.vector.tensor_copy)
-        quantise_wn(1, 0, nc.vector.tensor_copy)
+        for a in range(2):
+            quantise_noise(a, on_vector)
+        for a in range(2):
+            quantise_wn(a, 0, on_vector)
         square(0, whole)
-        noise_power(0)
-        for cols in halves:
-            inverse(0, cols)
-        quantise_wn(0, 1, nc.scalar.copy)
-        quantise_wn(1, 1, nc.scalar.copy)
+        for a in range(2):
+            quantise_wn(a, 1, on_scalar)
+        for c in range(len(CHUNKS)):
+            noise_power(c, 0)
         for i in range(4):
             pick(1, i)
-        noise_power(1)
-        for c in range(len(CHUNKS)):
-            square(1, chunk_cols(c))
-        numerator(0, whole)
-        nc.vector.tensor_copy(
-            out=ws_w[:].rearrange("p b (g t m) -> p (b g) m t", g=2, t=4),
-            in_=ws_raw[:].rearrange("p b (g m t) -> p (b g) m t", g=2, t=4),
-        )
-        for cols in halves:
-            masked_mixture(0, cols)
-        for c in range(len(CHUNKS)):
-            synthesis_pass(c, 0)
+        square(1, chunk_cols(0))
+        noise_power(0, 1)
+        inverse(0, chunk_cols(0))
+        deal_ws()
         inverse(1, chunk_cols(0))
+        square(1, slice(starts[1], M))
+        for c in range(1, len(CHUNKS)):
+            noise_power(c, 1)
         for c in range(len(CHUNKS)):
+            numerator(0, chunk_cols(c))
+            finish(c, 0)
+            if c < last_chunk:
+                inverse(0, chunk_cols(c + 1))
+            numerator(1, chunk_cols(c))
+            finish(c, 1)
             if c < last_chunk:
                 inverse(1, chunk_cols(c + 1))
-            numerator(1, chunk_cols(c))
-            masked_mixture(1, chunk_cols(c))
-            synthesis_pass(c, 1)
+            store_both(store_y, c)
             if c > 0:
-                for g in range(2):
-                    store_planes(c - 1, g)
-            for g in range(2):
-                store_y(c, g)
-        for g in range(2):
-            store_planes(last_chunk, g)
+                store_both(store_planes, c - 1)
+        store_both(store_planes, last_chunk)
         for q in range(4):
             nc.scalar.dma_start(out_2[:, 4 * q : 4 * q + 4, :].bitcast(I32), y_s[32 * q : 32 * q + 8, :].bitcast(I32))

@@ -60,12 +60,12 @@ def tile_list_ratio_mask_synthesis_kernel(
         idx2 = keep.tile([P, M // 16], U16, name="idx2")
         tab_s = shared("tab_s", [P, T], U8, "late")
         s_raw = shared("s_raw", [P, PASS], U8, "tab1")
-        s_dealt = shared("s_dealt", [P, PASS], U8, "ws")
+        s_dealt = kept("s_dealt", [P, PASS], U8)
         tab_w = [kept("tab_w0", [P, T], I32)]
         w4_raw = kept("w4_raw", [P, 2, 2 * H], U8)
         w4_w = [kept(f"w4_w{a}", [P, 2 * H], U8) for a in range(2)]
-        planes = kept("planes", [P, 2, 2, 2, PASS], U8)
-        v_picked = kept("v_picked", [P, S], U8)
+        planes = [kept(f"planes{w}", [P, 2, 2, PASS], U8) for w in range(2)]
+        v_picked = shared("v_picked", [P, S], U8, "ws")
         v_s = kept("v_s", [P, 2, S], U8)
         v_w = [[shared("v_w", [P, BANK], U32, f"v_w{a}_{j}") for j in range(2)] for a in range(2)]
         floor = kept("floor", [P, 16], F32)
@@ -73,7 +73,8 @@ def tile_list_ratio_mask_synthesis_kernel(
         nc.vector.memset(tab_s[32:64, :].bitcast(I32), 0)
         nc.vector.memset(tab_s[64:P, :].bitcast(I32), 0)
         nc.vector.memset(floor[:, 0:1], 25.0)
-        nc.gpsimd.memset(planes[:].rearrange("p a b w c -> p (a b w c)").bitcast(I32), 0)
+        for plane in planes:
+            nc.gpsimd.memset(plane[:].rearrange("p b a c -> p (b a c)").bitcast(I32), 0)
         nc.gpsimd.memset(v_s[:].rearrange("p a c -> p (a c)").bitcast(I32), 0)
         mask_floor = floor[:, 8:9]
         nc.scalar.activation(out=mask_floor, in_=floor[:, 0:1], func=ACT.Abs_reciprocal_sqrt)
@@ -84,7 +85,7 @@ def tile_list_ratio_mask_synthesis_kernel(
         for w, scales in enumerate((w4_scales, ws_scales)):
             for a in range(2):
                 nc.sync.dma_start(
-                    s_raw[2 * w + a : P : 4, :].bitcast(I32), scales[a].rearrange("q (b c) -> (q b) c", b=2).bitcast(I32)
+                    s_raw[64 * w + a : 64 * (w + 1) : 2, :].bitcast(I32), scales[a].rearrange("q (b c) -> (q b) c", b=2).bitcast(I32)
                 )
         nc.sync.dma_start(idx[:], offs)
         nc.sync.dma_start(tab_s[0:32, :].bitcast(I32), tab_scales.rearrange("a q t -> q a t").bitcast(I32))
@@ -94,11 +95,15 @@ def tile_list_ratio_mask_synthesis_kernel(
         nc.vector.tensor_copy(
             out=s_dealt[:].rearrange("p (i m) -> p i m", i=4), in_=s_raw[:].rearrange("p (m i) -> p i m", i=4)
         )
-        for q in range(4):
-            nc.sync.dma_start(
-                planes[32 * q : 32 * q + 4].rearrange("p a b w c -> p (a b w c)").bitcast(I32),
-                s_dealt[32 * q : 32 * q + 32, :].bitcast(I32),
-            )
+
+        def place_planes(w):
+            for q in range(4):
+                nc.sync.dma_start(
+                    planes[w][32 * q : 32 * q + 4].rearrange("p b a c -> p (b a c)").bitcast(I32),
+                    s_dealt[64 * w + 16 * q : 64 * w + 16 * q + 16, :].bitcast(I32),
+                )
+
+        place_planes(0)
         tab_w.append(shared("tab_w1", [P, T], I32, "tab1"))
         nc.sync.dma_start(tab_w[1][:], tab_words[1].rearrange("p t i -> p (t i)").bitcast(I32))
         nc.vector.tensor_copy(out=v_picked[:], in_=tab_s[:].indirect(idx[:]))
@@ -138,6 +143,7 @@ def tile_list_ratio_mask_synthesis_kernel(
         ws_raw = shared("ws_raw", [P, 2, N], I32, "ws")
         nc.sync.dma_start(ws_raw[:], ws_words.rearrange("a p c i -> p a (c i)").bitcast(I32))
         load_rows(mix_all[1], mix, 1)
+        place_planes(1)
 
         gather_words(0, 0)
         for a in range(2):
@@ -160,7 +166,7 @@ def tile_list_ratio_mask_synthesis_kernel(
                 nc.tensor.matmul_mx(
                     out=bank[:],
                     lhsT=w4_w[a][:, 2 * col : 2 * (col + P)].bitcast(E2M1),
-                    lhsT_scale=planes[:, b, 0, a, P * i : P * (i + 1)],
+                    lhsT_scale=planes[0][:, b, a, P * i : P * (i + 1)],
                     rhs=v_w[a][j][:].bitcast(E4M3),
                     rhs_scale=v_s[:, a, BANK * j : BANK * (j + 1)],
                     start=(a == 0),
@@ -257,7 +263,7 @@ def tile_list_ratio_mask_synthesis_kernel(
                         nc.tensor.matmul_mx(
                             out=y_banks[c, g, first][:, t - first, :],
                             lhsT=ws_w[:, b, col : col + P].bitcast(E4M3),
-                            lhsT_scale=planes[:, g, 1, b, P * t : P * (t + 1)],
+                            lhsT_scale=planes[1][:, g, b, P * t : P * (t + 1)],
                             rhs=z_q[b][:, chunk_cols(c)].bitcast(E4M3),
                             rhs_scale=z_s[b][:, chunk_cols(c)],
                             start=(b == 0 and t == first),
@@ -266,7 +272,7 @@ def tile_list_ratio_mask_synthesis_kernel(
 
         def store_y(c, g):
             per_bank = BANK // CHUNKS[c]
-            copy = nc.vector.tensor_copy if (c, g) == (last_chunk, 1) else nc.scalar.copy
+            copy = nc.scalar.copy
             for first in range(0, 4, per_bank):
                 copy(out=y_sb[c, g][:, first : first + per_bank, :], in_=y_banks[c, g, first][:])
             nc.sync.dma_start(
@@ -275,7 +281,7 @@ def tile_list_ratio_mask_synthesis_kernel(
 
         def store_planes(c, g):
             words = rounded_tile([P, CHUNKS[c], 4])
-            nc.vector.tensor_copy(out=by_words(words[:]), in_=by_rows(y_sb[c, g]))
+            nc.vector.tensor_copy(out=by_words(words[:]), in_=by_rows(y_banks[c, g, 0][:] if c == last_chunk else y_sb[c, g]))
             y_q = kept(f"y_q{c}_{g}", [P, CHUNKS[c]], I32)
             quantise(y_q[:], y_s[4 * g : P, chunk_cols(c)], words[:].rearrange("p m t -> p (m t)"))
             nc.sync.dma_start(out_1[g, :, chunk_cols(c), :].rearrange("p m t -> p (m t)").bitcast(I32), y_q[:])
@@ -295,6 +301,17 @@ def tile_list_ratio_mask_synthesis_kernel(
                 store(c, g)
 
         whole = slice(0, M)
+        idle_bank = bank_tile(7, [P, BANK])
+        for turn in range(4):
+            nc.tensor.matmul_mx(
+                out=idle_bank[:],
+                lhsT=w4_raw[:, 0, 0 : 2 * P].bitcast(E2M1),
+                lhsT_scale=planes[0][:, 0, 0, 0:P],
+                rhs=v_w[0][0][:].bitcast(E4M3),
+                rhs_scale=planes[0][:, 0, 0, :],
+                start=True,
+                stop=True,
+            )
         on_vector, on_scalar = nc.vector.tensor_copy, nc.scalar.copy
         for i in range(4):
             speech(0, i, 0)
@@ -332,9 +349,11 @@ def tile_list_ratio_mask_synthesis_kernel(
             finish(c, 1)
             if c < last_chunk:
                 inverse(1, chunk_cols(c + 1))
-            store_both(store_y, c)
             if c > 0:
                 store_both(store_planes, c - 1)
+            if c < last_chunk:
+                store_both(store_y, c)
         store_both(store_planes, last_chunk)
+        store_both(store_y, last_chunk)
         for q in range(4):
-            nc.scalar.dma_start(out_2[:, 4 * q : 4 * q + 4, :].bitcast(I32), y_s[32 * q : 32 * q + 8, :].bitcast(I32))
+            (nc.scalar, nc.sync)[q % 2].dma_start(out_2[:, 4 * q : 4 * q + 4, :].bitcast(I32), y_s[32 * q : 32 * q + 8, :].bitcast(I32))

@@ -156,7 +156,7 @@ def tile_list_ratio_mask_synthesis_kernel(
         gather_words(1, 1)
 
         h = {(b, i): shared("h", [P, S], F32, f"h{b}_{i}") for b in range(2) for i in range(4)}
-        x = [kept("x0", [P, 4, M], F32)[:], kept("x1", [P, 4, M], F32)[:]]
+        x = [kept("x0", [P, 4, M], F32)[:], late[:, 9 * M : 25 * M].rearrange("p (i w) -> p i w", i=4)[:, :, 0:M]]
         den = [kept(f"den{b}", [P, 4, M], F32) for b in range(2)]
 
         def speech(b, i, j):
@@ -321,25 +321,24 @@ def tile_list_ratio_mask_synthesis_kernel(
         for i in range(4):
             for j in range(2):
                 speech(1, i, j)
-        for a in range(2):
-            quantise_noise(a, on_vector)
-        for a in range(2):
-            quantise_wn(a, 0, on_vector)
+        quantise_noise(0, on_vector)
+        quantise_noise(1, on_vector)
+        quantise_wn(0, 0, on_vector)
+        quantise_wn(1, 0, on_scalar)
         square(0, whole)
-        for a in range(2):
-            quantise_wn(a, 1, on_scalar)
+        quantise_wn(0, 1, on_scalar)
+        quantise_wn(1, 1, on_scalar)
         for c in range(len(CHUNKS)):
             noise_power(c, 0)
         for i in range(4):
             pick(1, i)
-        square(1, chunk_cols(0))
-        noise_power(0, 1)
+        for c in range(len(CHUNKS)):
+            noise_power(c, 1)
         inverse(0, chunk_cols(0))
+        square(1, chunk_cols(0))
         deal_ws()
         inverse(1, chunk_cols(0))
         square(1, slice(starts[1], M))
-        for c in range(1, len(CHUNKS)):
-            noise_power(c, 1)
         for c in range(len(CHUNKS)):
             numerator(0, chunk_cols(c))
             finish(c, 0)

@@ -250,6 +250,7 @@ def tile_list_ratio_mask_synthesis_kernel(
 
         ws_w = shared("ws_w", [P, 2, N], I32, "h1_3")
         y_s = kept("y_s", [P, M], U8)
+        y_q = [kept(f"y_q{c}", [P, 2, width], I32) for c, width in enumerate(CHUNKS)]
         y_banks = {}
 
         def synthesis_pass(c, b):
@@ -281,10 +282,10 @@ def tile_list_ratio_mask_synthesis_kernel(
 
         def store_planes(c, g):
             words = rounded_tile([P, CHUNKS[c], 4])
-            nc.vector.tensor_copy(out=by_words(words[:]), in_=by_rows(y_banks[c, g, 0][:] if c == last_chunk else y_sb[c, g]))
-            y_q = kept(f"y_q{c}_{g}", [P, CHUNKS[c]], I32)
-            quantise(y_q[:], y_s[4 * g : P, chunk_cols(c)], words[:].rearrange("p m t -> p (m t)"))
-            nc.sync.dma_start(out_1[g, :, chunk_cols(c), :].rearrange("p m t -> p (m t)").bitcast(I32), y_q[:])
+            nc.vector.tensor_copy(out=by_words(words[:]), in_=by_rows(y_sb[c, g]))
+            quantise(y_q[c][:, g, :], y_s[4 * g : P, chunk_cols(c)], words[:].rearrange("p m t -> p (m t)"))
+            if g == 1:
+                nc.sync.dma_start(out_1[:, :, chunk_cols(c), :].rearrange("g p m t -> p g (m t)").bitcast(I32), y_q[c][:])
 
         def deal_ws():
             nc.vector.tensor_copy(
@@ -328,31 +329,30 @@ def tile_list_ratio_mask_synthesis_kernel(
         square(0, whole)
         quantise_wn(0, 1, on_scalar)
         quantise_wn(1, 1, on_scalar)
-        for c in range(len(CHUNKS)):
-            noise_power(c, 0)
+        noise_power(0, 0)
         for i in range(4):
             pick(1, i)
-        for c in range(len(CHUNKS)):
-            noise_power(c, 1)
+        noise_power(0, 1)
         inverse(0, chunk_cols(0))
         square(1, chunk_cols(0))
-        deal_ws()
         inverse(1, chunk_cols(0))
-        square(1, slice(starts[1], M))
+        deal_ws()
+        for b in range(2):
+            numerator(b, chunk_cols(0))
+            finish(0, b)
+        for c in range(1, len(CHUNKS)):
+            noise_power(c, 0)
+            noise_power(c, 1)
+            square(1, chunk_cols(c))
+            for b in range(2):
+                inverse(b, chunk_cols(c))
+        for c in range(1, len(CHUNKS)):
+            for b in range(2):
+                numerator(b, chunk_cols(c))
+                finish(c, b)
+        for c in range(0, len(CHUNKS)):
+            store_both(store_y, c)
         for c in range(len(CHUNKS)):
-            numerator(0, chunk_cols(c))
-            finish(c, 0)
-            if c < last_chunk:
-                inverse(0, chunk_cols(c + 1))
-            numerator(1, chunk_cols(c))
-            finish(c, 1)
-            if c < last_chunk:
-                inverse(1, chunk_cols(c + 1))
-            if c > 0:
-                store_both(store_planes, c - 1)
-            if c < last_chunk:
-                store_both(store_y, c)
-        store_both(store_planes, last_chunk)
-        store_both(store_y, last_chunk)
+            store_both(store_planes, c)
         for q in range(4):
             (nc.scalar, nc.sync)[q % 2].dma_start(out_2[:, 4 * q : 4 * q + 4, :].bitcast(I32), y_s[32 * q : 32 * q + 8, :].bitcast(I32))

@@ -89,8 +89,8 @@ def tile_list_ratio_mask_synthesis_kernel(
                 )
         nc.sync.dma_start(idx[:], offs)
         nc.sync.dma_start(tab_s[0:32, :].bitcast(I32), tab_scales.rearrange("a q t -> q a t").bitcast(I32))
-        nc.sync.dma_start(tab_w[0][:], tab_words[0].rearrange("p t i -> p (t i)").bitcast(I32))
         nc.sync.dma_start(w4_raw[:].bitcast(I32), w4_words.rearrange("a p c -> p a c").bitcast(I32))
+        nc.sync.dma_start(tab_w[0][:], tab_words[0].rearrange("p t i -> p (t i)").bitcast(I32))
         nc.sync.dma_start(idx2[:], offs2)
         nc.vector.tensor_copy(
             out=s_dealt[:].rearrange("p (i m) -> p i m", i=4), in_=s_raw[:].rearrange("p (m i) -> p i m", i=4)
@@ -147,9 +147,9 @@ def tile_list_ratio_mask_synthesis_kernel(
 
         gather_words(0, 0)
         for a in range(2):
-            nc.vector.tensor_copy(
-                out=w4_w[a][:].bitcast(U16).rearrange("p (b i m) -> p b i m", b=2, i=4),
-                in_=w4_raw[:, a, :].bitcast(U16).rearrange("p (b m i) -> p b i m", b=2, i=4),
+            nc.gpsimd.tensor_copy(
+                out=w4_w[a][:].rearrange("p (b i m e) -> p b i m e", b=2, i=4, e=2),
+                in_=w4_raw[:, a, :].rearrange("p (b m i e) -> p b i m e", b=2, i=4, e=2),
             )
         gather_words(1, 0)
         gather_words(0, 1)
@@ -275,10 +275,12 @@ def tile_list_ratio_mask_synthesis_kernel(
             per_bank = BANK // CHUNKS[c]
             copy = nc.scalar.copy
             for first in range(0, 4, per_bank):
-                copy(out=y_sb[c, g][:, first : first + per_bank, :], in_=y_banks[c, g, first][:])
-            nc.sync.dma_start(
-                out_0[PASS * g : PASS * (g + 1), chunk_cols(c)].rearrange("(p t) m -> p t m", t=4), y_sb[c, g]
-            )
+                slots = slice(first, first + per_bank)
+                copy(out=y_sb[c, g][:, slots, :], in_=y_banks[c, g, first][:])
+                nc.sync.dma_start(
+                    out_0[PASS * g : PASS * (g + 1), chunk_cols(c)].rearrange("(p t) m -> p t m", t=4)[:, slots, :],
+                    y_sb[c, g][:, slots, :],
+                )
 
         def store_planes(c, g):
             words = rounded_tile([P, CHUNKS[c], 4])

@@ -191,12 +191,15 @@ def tile_list_ratio_mask_synthesis_kernel(
         def quantise(codes, scales, words):
             nc.vector.quantize_mx(out=codes.bitcast(E4M3), scales=scales, in_=words)
 
-        def quantise_noise(a, copy):
+        def round_noise(a, copy):
             words = rounded_tile([P, M, 4])
             copy(out=by_words(words[:]), in_=by_rows(noise_all[a]))
+            return words
+
+        def quantise_noise(a, words):
             quantise(noise_q[a][:], noise_s[a][:], words[:].rearrange("p m j -> p (m j)"))
 
-        def quantise_wn(a, b, copy):
+        def round_wn(a, b, copy):
             words = rounded_tile([P, 4, P, 4])
             for pair in range(2):
                 slots = slice(2 * pair, 2 * pair + 2)
@@ -204,6 +207,9 @@ def tile_list_ratio_mask_synthesis_kernel(
                     out=words[:, slots, :, :].rearrange("p i m j -> p m j i"),
                     in_=wn_raw[a, b].rearrange("p j (m i) -> p m j i", i=4)[:, :, :, slots],
                 )
+            return words
+
+        def quantise_wn(a, b, words):
             quantise(wn_q[a, b][:], wn_s[a, b][:], words[:].rearrange("p i m j -> p (i m j)"))
 
         def noise_power(c, b):
@@ -232,21 +238,30 @@ def tile_list_ratio_mask_synthesis_kernel(
         def square(b, cols):
             nc.scalar.activation(out=x[b][:, :, cols], in_=picked[b][:, :, cols], func=ACT.Square)
 
-        def numerator(b, cols):
+        def numerator(c, b):
+            cols = chunk_cols(c)
             nc.vector.tensor_tensor(out=x[b][:, :, cols], in0=x[b][:, :, cols], in1=mix_all[b][:, :, cols], op=ALU.mult)
 
-        def inverse(b, cols):
-            part = den[b][:, :, cols]
-            nc.vector.tensor_tensor(out=part, in0=x[b][:, :, cols], in1=part, op=ALU.add)
+        def power_sum(c, b):
+            part = den[b][:, :, chunk_cols(c)]
+            nc.vector.tensor_tensor(out=part, in0=x[b][:, :, chunk_cols(c)], in1=part, op=ALU.add)
+
+        def root(c, b):
+            part = den[b][:, :, chunk_cols(c)]
             nc.scalar.activation(out=part, in_=part, func=ACT.Abs_reciprocal_sqrt, bias=mask_floor)
+
+        def invert(c, b):
+            part = den[b][:, :, chunk_cols(c)]
             nc.scalar.activation(out=part, in_=part, func=ACT.Square)
 
-        def masked_mixture(b, cols):
-            words = rounded_tile([P, cols.stop - cols.start, 4])
+        z_words = {}
+
+        def round_z(c, b):
+            cols = chunk_cols(c)
+            z_words[c, b] = rounded_tile([P, CHUNKS[c], 4])
             nc.vector.tensor_tensor(
-                out=by_words(words[:]), in0=by_rows(x[b][:, :, cols]), in1=by_rows(den[b][:, :, cols]), op=ALU.mult
+                out=by_words(z_words[c, b][:]), in0=by_rows(x[b][:, :, cols]), in1=by_rows(den[b][:, :, cols]), op=ALU.mult
             )
-            quantise(z_q[b][:, cols], z_s[b][:, cols], words[:].rearrange("p m i -> p (m i)"))
 
         ws_w = shared("ws_w", [P, 2, N], I32, "h1_3")
         y_s = kept("y_s", [P, M], U8)
@@ -282,10 +297,14 @@ def tile_list_ratio_mask_synthesis_kernel(
                     y_sb[c, g][:, slots, :],
                 )
 
+        y_words = {}
+
+        def round_y(c, g):
+            y_words[c, g] = rounded_tile([P, CHUNKS[c], 4])
+            nc.vector.tensor_copy(out=by_words(y_words[c, g][:]), in_=by_rows(y_sb[c, g]))
+
         def store_planes(c, g):
-            words = rounded_tile([P, CHUNKS[c], 4])
-            nc.vector.tensor_copy(out=by_words(words[:]), in_=by_rows(y_sb[c, g]))
-            quantise(y_q[c][:, g, :], y_s[4 * g : P, chunk_cols(c)], words[:].rearrange("p m t -> p (m t)"))
+            quantise(y_q[c][:, g, :], y_s[4 * g : P, chunk_cols(c)], y_words[c, g][:].rearrange("p m t -> p (m t)"))
             if g == 1:
                 nc.sync.dma_start(out_1[:, :, chunk_cols(c), :].rearrange("g p m t -> p g (m t)").bitcast(I32), y_q[c][:])
 
@@ -296,7 +315,8 @@ def tile_list_ratio_mask_synthesis_kernel(
             )
 
         def finish(c, b):
-            masked_mixture(b, chunk_cols(c))
+            cols = chunk_cols(c)
+            quantise(z_q[b][:, cols], z_s[b][:, cols], z_words[c, b][:].rearrange("p m i -> p (m i)"))
             synthesis_pass(c, b)
 
         def store_both(store, c):
@@ -324,37 +344,64 @@ def tile_list_ratio_mask_synthesis_kernel(
         for i in range(4):
             for j in range(2):
                 speech(1, i, j)
-        quantise_noise(0, on_vector)
-        quantise_noise(1, on_vector)
-        quantise_wn(0, 0, on_vector)
-        quantise_wn(1, 0, on_scalar)
+        noise_words = [round_noise(a, on_vector) for a in range(2)]
+        quantise_noise(0, noise_words[0])
+        first_wn = round_wn(0, 0, on_vector)
+        quantise_noise(1, noise_words[1])
+        second_wn = round_wn(1, 0, on_scalar)
+        quantise_wn(0, 0, first_wn)
+        quantise_wn(1, 0, second_wn)
         square(0, whole)
-        quantise_wn(0, 1, on_scalar)
-        quantise_wn(1, 1, on_scalar)
+        quantise_wn(0, 1, round_wn(0, 1, on_scalar))
+        quantise_wn(1, 1, round_wn(1, 1, on_scalar))
         noise_power(0, 0)
         for i in range(4):
             pick(1, i)
         noise_power(0, 1)
-        inverse(0, chunk_cols(0))
+        power_sum(0, 0)
+        root(0, 0)
         square(1, chunk_cols(0))
-        inverse(1, chunk_cols(0))
+        invert(0, 0)
+        power_sum(0, 1)
+        root(0, 1)
+        noise_power(1, 0)
+        invert(0, 1)
+        numerator(0, 0)
         deal_ws()
+        round_z(0, 0)
+        numerator(0, 1)
+        finish(0, 0)
+        noise_power(1, 1)
+        square(1, chunk_cols(1))
+        power_sum(1, 0)
+        root(1, 0)
+        round_z(0, 1)
+        power_sum(1, 1)
+        finish(0, 1)
+        root(1, 1)
+        invert(1, 0)
+        invert(1, 1)
+        noise_power(2, 0)
+        noise_power(2, 1)
+        square(1, chunk_cols(2))
         for b in range(2):
-            numerator(b, chunk_cols(0))
-            finish(0, b)
-        for c in range(1, len(CHUNKS)):
-            noise_power(c, 0)
-            noise_power(c, 1)
-            square(1, chunk_cols(c))
+            power_sum(2, b)
+            numerator(1, b)
+        for step in (root, invert):
             for b in range(2):
-                inverse(b, chunk_cols(c))
-        for c in range(1, len(CHUNKS)):
+                step(2, b)
+        for b in range(2):
+            round_z(1, b)
+        for b in range(2):
+            finish(1, b)
+            numerator(2, b)
+        for step in (round_z, finish):
             for b in range(2):
-                numerator(b, chunk_cols(c))
-                finish(c, b)
-        for c in range(0, len(CHUNKS)):
+                step(2, b)
+        for c in range(len(CHUNKS)):
             store_both(store_y, c)
         for c in range(len(CHUNKS)):
+            store_both(round_y, c)
             store_both(store_planes, c)
         for q in range(4):
             (nc.scalar, nc.sync)[q % 2].dma_start(out_2[:, 4 * q : 4 * q + 4, :].bitcast(I32), y_s[32 * q : 32 * q + 8, :].bitcast(I32))

@@ -59,59 +59,64 @@ def tile_list_ratio_mask_synthesis_kernel(
         idx = keep.tile([P, S // 16], U16, name="idx")
         idx2 = keep.tile([P, M // 16], U16, name="idx2")
         tab_s = shared("tab_s", [P, T], U8, "late")
-        s_raw = shared("s_raw", [P, PASS], U8, "tab1")
+        w4_s = kept("w4_s", [P, 2, H], U8)
+        s_raw = kept("s_raw", [P, PASS], U8)
         s_dealt = kept("s_dealt", [P, PASS], U8)
         tab_w = [kept("tab_w0", [P, T], I32)]
         w4_raw = kept("w4_raw", [P, 2, 2 * H], U8)
-        w4_w = [kept(f"w4_w{a}", [P, 2 * H], U8) for a in range(2)]
-        planes = [kept(f"planes{w}", [P, 2, 2, PASS], U8) for w in range(2)]
+        w4_w = [kept(f"w4_w{b}", [P, 2, 2 * PASS], U8) for b in range(2)]
+        w4_plane = kept("w4_plane", [P, 2, H], U8)
+        ws_plane = kept("ws_plane", [P, 2, 2, PASS], U8)
         v_picked = shared("v_picked", [P, S], U8, "ws")
         v_s = kept("v_s", [P, 2, S], U8)
         v_w = [[shared("v_w", [P, BANK], U32, f"v_w{a}_{j}") for j in range(2)] for a in range(2)]
         floor = kept("floor", [P, 16], F32)
 
+        nc.vector.memset(w4_s[:].rearrange("p a c -> p (a c)").bitcast(I32), 0)
         nc.vector.memset(tab_s[32:64, :].bitcast(I32), 0)
         nc.vector.memset(tab_s[64:P, :].bitcast(I32), 0)
         nc.vector.memset(floor[:, 0:1], 25.0)
-        for plane in planes:
-            nc.gpsimd.memset(plane[:].rearrange("p b a c -> p (b a c)").bitcast(I32), 0)
-        nc.gpsimd.memset(v_s[:].rearrange("p a c -> p (a c)").bitcast(I32), 0)
+        nc.vector.memset(v_s[:].rearrange("p a c -> p (a c)").bitcast(I32), 0)
+        nc.vector.memset(ws_plane[:].rearrange("p b a c -> p (b a c)").bitcast(I32), 0)
+        nc.vector.memset(s_raw[64:P, :].bitcast(I32), 0)
         mask_floor = floor[:, 8:9]
         nc.scalar.activation(out=mask_floor, in_=floor[:, 0:1], func=ACT.Abs_reciprocal_sqrt)
 
         def gather_words(a, j):
             nc.vector.tensor_copy(out=v_w[a][j][:], in_=tab_w[a][:].bitcast(U32).indirect(idx[:, 32 * j : 32 * (j + 1)]))
 
-        for w, scales in enumerate((w4_scales, ws_scales)):
-            for a in range(2):
-                nc.sync.dma_start(
-                    s_raw[64 * w + a : 64 * (w + 1) : 2, :].bitcast(I32), scales[a].rearrange("q (b c) -> (q b) c", b=2).bitcast(I32)
-                )
+        for a in range(2):
+            nc.sync.dma_start(tab_s[a:32:2, :].bitcast(I32), tab_scales[a].rearrange("(q r) t -> r q t", r=4).bitcast(I32))
         nc.sync.dma_start(idx[:], offs)
-        nc.sync.dma_start(tab_s[0:32, :].bitcast(I32), tab_scales.rearrange("a q t -> q a t").bitcast(I32))
-        nc.sync.dma_start(w4_raw[:].bitcast(I32), w4_words.rearrange("a p c -> p a c").bitcast(I32))
+        for r in range(4):
+            nc.sync.dma_start(w4_s[r:P:32].bitcast(I32), w4_scales.rearrange("a (q r) c -> r q a c", r=4)[r].bitcast(I32))
+        tab_w.append(kept("tab_w1", [P, T], I32))
         nc.sync.dma_start(tab_w[0][:], tab_words[0].rearrange("p t i -> p (t i)").bitcast(I32))
-        nc.sync.dma_start(idx2[:], offs2)
-        nc.vector.tensor_copy(
-            out=s_dealt[:].rearrange("p (i m) -> p i m", i=4), in_=s_raw[:].rearrange("p (m i) -> p i m", i=4)
-        )
-
-        def place_planes(w):
-            for q in range(4):
-                nc.sync.dma_start(
-                    planes[w][32 * q : 32 * q + 4].rearrange("p b a c -> p (b a c)").bitcast(I32),
-                    s_dealt[64 * w + 16 * q : 64 * w + 16 * q + 16, :].bitcast(I32),
-                )
-
-        place_planes(0)
-        tab_w.append(shared("tab_w1", [P, T], I32, "tab1"))
+        nc.sync.dma_start(w4_raw[:].bitcast(I32), w4_words.rearrange("a p c -> p a c").bitcast(I32))
         nc.sync.dma_start(tab_w[1][:], tab_words[1].rearrange("p t i -> p (t i)").bitcast(I32))
         nc.vector.tensor_copy(out=v_picked[:], in_=tab_s[:].indirect(idx[:]))
-        for q in range(4):
+        nc.vector.tensor_copy(
+            out=w4_plane[:].rearrange("p a (b i m) -> p (a b) i m", b=2, i=4), in_=w4_s[:].rearrange("p a (b m i) -> p (a b) i m", b=2, i=4)
+        )
+        for r in range(4):
             nc.sync.dma_start(
-                v_s[32 * q : 32 * q + 4].rearrange("p a c -> p (a c)").bitcast(I32),
-                v_picked[8 * q : 8 * q + 8, :].bitcast(I32),
+                v_s[r:P:32].rearrange("p a c -> p (a c)").bitcast(I32),
+                v_picked[8 * r : 8 * r + 8, :].bitcast(I32),
             )
+
+        def load_ws_scales():
+            for a in range(2):
+                nc.sync.dma_start(s_raw[a:64:2, :].bitcast(I32), ws_scales[a].rearrange("q (b c) -> (q b) c", b=2).bitcast(I32))
+            nc.vector.tensor_copy(
+                out=s_dealt[:].rearrange("p (i m) -> p i m", i=4), in_=s_raw[:].rearrange("p (m i) -> p i m", i=4)
+            )
+
+        def place_ws_scales():
+            for q in range(4):
+                nc.sync.dma_start(
+                    ws_plane[32 * q : 32 * q + 4].rearrange("p b a c -> p (b a c)").bitcast(I32),
+                    s_dealt[16 * q : 16 * q + 16, :].bitcast(I32),
+                )
 
         late = shared("late", [P, M + 4 * (2 * M + 2 * H + 2 * M)], F32, "late")
         wgt_sb = late[:, 0:M]
@@ -133,8 +138,10 @@ def tile_list_ratio_mask_synthesis_kernel(
         def load_rows(tile, source, a):
             nc.sync.dma_start(tile, source[PASS * a : PASS * (a + 1), :].rearrange("(p j) m -> p j m", j=4))
 
-        for a in range(2):
-            load_rows(noise_all[a], noise, a)
+        nc.sync.dma_start(idx2[:], offs2)
+        load_rows(noise_all[0], noise, 0)
+        load_ws_scales()
+        load_rows(noise_all[1], noise, 1)
         nc.sync.dma_start(wgt_sb, wgt)
         for b in range(2):
             for a in range(2):
@@ -143,13 +150,13 @@ def tile_list_ratio_mask_synthesis_kernel(
         ws_raw = shared("ws_raw", [P, 2, N], I32, "ws")
         nc.sync.dma_start(ws_raw[:], ws_words.rearrange("a p c i -> p a (c i)").bitcast(I32))
         load_rows(mix_all[1], mix, 1)
-        place_planes(1)
+        place_ws_scales()
 
         gather_words(0, 0)
-        for a in range(2):
+        for b in range(2):
             nc.gpsimd.tensor_copy(
-                out=w4_w[a][:].rearrange("p (b i m e) -> p b i m e", b=2, i=4, e=2),
-                in_=w4_raw[:, a, :].rearrange("p (b m i e) -> p b i m e", b=2, i=4, e=2),
+                out=w4_w[b][:].rearrange("p a (i m e) -> p a i m e", i=4, e=2),
+                in_=w4_raw[:, :, 2 * PASS * b : 2 * PASS * (b + 1)].rearrange("p a (m i e) -> p a i m e", i=4, e=2),
             )
         gather_words(1, 0)
         gather_words(0, 1)
@@ -165,8 +172,8 @@ def tile_list_ratio_mask_synthesis_kernel(
             for a in range(2):
                 nc.tensor.matmul_mx(
                     out=bank[:],
-                    lhsT=w4_w[a][:, 2 * col : 2 * (col + P)].bitcast(E2M1),
-                    lhsT_scale=planes[0][:, b, a, P * i : P * (i + 1)],
+                    lhsT=w4_w[b][:, a, 2 * P * i : 2 * P * (i + 1)].bitcast(E2M1),
+                    lhsT_scale=w4_plane[:, a, col : col + P],
                     rhs=v_w[a][j][:].bitcast(E4M3),
                     rhs_scale=v_s[:, a, BANK * j : BANK * (j + 1)],
                     start=(a == 0),
@@ -279,7 +286,7 @@ def tile_list_ratio_mask_synthesis_kernel(
                         nc.tensor.matmul_mx(
                             out=y_banks[c, g, first][:, t - first, :],
                             lhsT=ws_w[:, b, col : col + P].bitcast(E4M3),
-                            lhsT_scale=planes[1][:, g, b, P * t : P * (t + 1)],
+                            lhsT_scale=ws_plane[:, g, b, P * t : P * (t + 1)],
                             rhs=z_q[b][:, chunk_cols(c)].bitcast(E4M3),
                             rhs_scale=z_s[b][:, chunk_cols(c)],
                             start=(b == 0 and t == first),
@@ -329,9 +336,9 @@ def tile_list_ratio_mask_synthesis_kernel(
             nc.tensor.matmul_mx(
                 out=idle_bank[:],
                 lhsT=w4_raw[:, 0, 0 : 2 * P].bitcast(E2M1),
-                lhsT_scale=planes[0][:, 0, 0, 0:P],
+                lhsT_scale=w4_s[:, 0, 0:P],
                 rhs=v_w[0][0][:].bitcast(E4M3),
-                rhs_scale=planes[0][:, 0, 0, :],
+                rhs_scale=w4_s[:, 0, 0:BANK],
                 start=True,
                 stop=True,
             )

@@ -60,10 +60,9 @@ def tile_list_ratio_mask_synthesis_kernel(
         idx2 = keep.tile([P, M // 16], U16, name="idx2")
         tab_s = shared("tab_s", [P, T], U8, "late")
         w4_s = kept("w4_s", [P, 2, H], U8)
-        s_raw = kept("s_raw", [P, PASS], U8)
         s_dealt = kept("s_dealt", [P, PASS], U8)
         tab_w = [kept("tab_w0", [P, T], I32)]
-        w4_raw = kept("w4_raw", [P, 2, 2 * H], U8)
+        w4_raw = [kept(f"w4_raw{b}", [P, 2, 2 * PASS], U8) for b in range(2)]
         w4_w = [kept(f"w4_w{b}", [P, 2, 2 * PASS], U8) for b in range(2)]
         w4_plane = kept("w4_plane", [P, 2, H], U8)
         ws_plane = kept("ws_plane", [P, 2, 2, PASS], U8)
@@ -78,7 +77,6 @@ def tile_list_ratio_mask_synthesis_kernel(
         nc.vector.memset(floor[:, 0:1], 25.0)
         nc.vector.memset(v_s[:].rearrange("p a c -> p (a c)").bitcast(I32), 0)
         nc.vector.memset(ws_plane[:].rearrange("p b a c -> p (b a c)").bitcast(I32), 0)
-        nc.vector.memset(s_raw[64:P, :].bitcast(I32), 0)
         mask_floor = floor[:, 8:9]
         nc.scalar.activation(out=mask_floor, in_=floor[:, 0:1], func=ACT.Abs_reciprocal_sqrt)
 
@@ -92,10 +90,12 @@ def tile_list_ratio_mask_synthesis_kernel(
             nc.sync.dma_start(w4_s[r:P:32].bitcast(I32), w4_scales.rearrange("a (q r) c -> r q a c", r=4)[r].bitcast(I32))
         tab_w.append(kept("tab_w1", [P, T], I32))
         nc.sync.dma_start(tab_w[0][:], tab_words[0].rearrange("p t i -> p (t i)").bitcast(I32))
-        nc.sync.dma_start(w4_raw[:].bitcast(I32), w4_words.rearrange("a p c -> p a c").bitcast(I32))
+        w4_halves = w4_words.rearrange("a p (b c) -> b p a c", b=2)
+        nc.sync.dma_start(w4_raw[0][:].bitcast(I32), w4_halves[0].bitcast(I32))
         nc.sync.dma_start(tab_w[1][:], tab_words[1].rearrange("p t i -> p (t i)").bitcast(I32))
+        nc.sync.dma_start(w4_raw[1][:].bitcast(I32), w4_halves[1].bitcast(I32))
         nc.vector.tensor_copy(out=v_picked[:], in_=tab_s[:].indirect(idx[:]))
-        nc.vector.tensor_copy(
+        nc.gpsimd.tensor_copy(
             out=w4_plane[:].rearrange("p a (b i m) -> p (a b) i m", b=2, i=4), in_=w4_s[:].rearrange("p a (b m i) -> p (a b) i m", b=2, i=4)
         )
         for r in range(4):
@@ -105,6 +105,8 @@ def tile_list_ratio_mask_synthesis_kernel(
             )
 
         def load_ws_scales():
+            s_raw = shared("s_raw", [P, PASS], U8, "w4_s")
+            nc.gpsimd.memset(s_raw[64:P, :].bitcast(I32), 0)
             for a in range(2):
                 nc.sync.dma_start(s_raw[a:64:2, :].bitcast(I32), ws_scales[a].rearrange("q (b c) -> (q b) c", b=2).bitcast(I32))
             nc.vector.tensor_copy(
@@ -140,9 +142,9 @@ def tile_list_ratio_mask_synthesis_kernel(
 
         nc.sync.dma_start(idx2[:], offs2)
         load_rows(noise_all[0], noise, 0)
-        load_ws_scales()
-        load_rows(noise_all[1], noise, 1)
         nc.sync.dma_start(wgt_sb, wgt)
+        load_rows(noise_all[1], noise, 1)
+        load_ws_scales()
         for b in range(2):
             for a in range(2):
                 load_wn(a, b)
@@ -156,14 +158,14 @@ def tile_list_ratio_mask_synthesis_kernel(
         for b in range(2):
             nc.gpsimd.tensor_copy(
                 out=w4_w[b][:].rearrange("p a (i m e) -> p a i m e", i=4, e=2),
-                in_=w4_raw[:, :, 2 * PASS * b : 2 * PASS * (b + 1)].rearrange("p a (m i e) -> p a i m e", i=4, e=2),
+                in_=w4_raw[b][:].rearrange("p a (m i e) -> p a i m e", i=4, e=2),
             )
         gather_words(1, 0)
         gather_words(0, 1)
         gather_words(1, 1)
 
         h = {(b, i): shared("h", [P, S], F32, f"h{b}_{i}") for b in range(2) for i in range(4)}
-        x = [kept("x0", [P, 4, M], F32)[:], late[:, 9 * M : 25 * M].rearrange("p (i w) -> p i w", i=4)[:, :, 0:M]]
+        x = [noise_all[0], late[:, 9 * M : 25 * M].rearrange("p (i w) -> p i w", i=4)[:, :, 0:M]]
         den = [kept(f"den{b}", [P, 4, M], F32) for b in range(2)]
 
         def speech(b, i, j):
@@ -335,23 +337,25 @@ def tile_list_ratio_mask_synthesis_kernel(
         for turn in range(4):
             nc.tensor.matmul_mx(
                 out=idle_bank[:],
-                lhsT=w4_raw[:, 0, 0 : 2 * P].bitcast(E2M1),
-                lhsT_scale=w4_s[:, 0, 0:P],
+                lhsT=w4_raw[0][:, 0, 0 : 2 * P].bitcast(E2M1),
+                lhsT_scale=w4_plane[:, 0, 0:P],
                 rhs=v_w[0][0][:].bitcast(E4M3),
-                rhs_scale=w4_s[:, 0, 0:BANK],
+                rhs_scale=w4_plane[:, 0, 0:BANK],
                 start=True,
                 stop=True,
             )
         on_vector, on_scalar = nc.vector.tensor_copy, nc.scalar.copy
+        first_noise = round_noise(0, on_vector)
+        speech(0, 0, 0)
         for i in range(4):
-            speech(0, i, 0)
-        for i in range(4):
+            if i < 3:
+                speech(0, i + 1, 0)
             speech(0, i, 1)
             pick(0, i)
         for i in range(4):
             for j in range(2):
                 speech(1, i, j)
-        noise_words = [round_noise(a, on_vector) for a in range(2)]
+        noise_words = [first_noise, round_noise(1, on_vector)]
         quantise_noise(0, noise_words[0])
         first_wn = round_wn(0, 0, on_vector)
         quantise_noise(1, noise_words[1])

@@ -1,6 +1,7 @@
 from contextlib import ExitStack
 
 import concourse.mybir as mybir
+from concourse.masks import make_identity
 
 K, H, N, T, S, M = 1024, 1024, 1024, 2048, 1024, 512
 P = 128
@@ -36,6 +37,7 @@ def tile_list_ratio_mask_synthesis_kernel(
     with ExitStack() as ctx:
         keep = ctx.enter_context(tc.tile_pool(name="keep", bufs=1))
         rounded = ctx.enter_context(tc.tile_pool(name="rounded", bufs=4))
+        turned = ctx.enter_context(tc.tile_pool(name="turned", bufs=4))
         psum = ctx.enter_context(tc.psum_pool(name="psum", bufs=1))
 
         def kept(name, shape, dtype):
@@ -77,6 +79,8 @@ def tile_list_ratio_mask_synthesis_kernel(
         nc.vector.memset(floor[:, 0:1], 25.0)
         nc.vector.memset(v_s[:].rearrange("p a c -> p (a c)").bitcast(I32), 0)
         nc.vector.memset(ws_plane[:].rearrange("p b a c -> p (b a c)").bitcast(I32), 0)
+        identity = kept("identity", [P, P], F32)
+        make_identity(nc, identity[:])
         mask_floor = floor[:, 8:9]
         nc.scalar.activation(out=mask_floor, in_=floor[:, 0:1], func=ACT.Abs_reciprocal_sqrt)
 
@@ -208,9 +212,14 @@ def tile_list_ratio_mask_synthesis_kernel(
         def quantise_noise(a, words):
             quantise(noise_q[a][:], noise_s[a][:], words[:].rearrange("p m j -> p (m j)"))
 
-        def round_wn(a, b, copy):
+        def round_wn_plain(a, copy):
+            words = rounded_tile([P, PASS, 4])
+            copy(out=by_words(words[:]), in_=by_rows(wn_raw[a, 0]))
+            return words[:].rearrange("p (i m) j -> p i m j", i=4)
+
+        def round_wn(a, b, *copies):
             words = rounded_tile([P, 4, P, 4])
-            for pair in range(2):
+            for pair, copy in enumerate(copies):
                 slots = slice(2 * pair, 2 * pair + 2)
                 copy(
                     out=words[:, slots, :, :].rearrange("p i m j -> p m j i"),
@@ -241,8 +250,51 @@ def tile_list_ratio_mask_synthesis_kernel(
         z_q = [kept(f"z_q{b}", [P, M], U32) for b in range(2)]
         z_s = [kept(f"z_s{b}", [P, M], U8) for b in range(2)]
 
-        picked = list(x)
-        x[0] = shared("x_squared", [P, 4, M], F32, "v_w1_1")[:]
+        picked = x
+        sums = {}
+
+        def block_cols(u):
+            return slice(P * u, P * (u + 1))
+
+        speech_power = {}
+
+        def turn_speech(u):
+            bank = bank_tile(u, [P, 4, P])
+            for i in range(4):
+                nc.tensor.transpose(bank[:, i, :], x[0][:, i, block_cols(u)], identity[:])
+            speech_power[u] = shared("speech_power", [P, 4, P], F32, f"h0_{u}")
+            nc.scalar.activation(out=speech_power[u][:], in_=bank[:], func=ACT.Square)
+
+        def open_sum(u):
+            sums[u] = bank_tile(4 + u, [P, 4, P])
+            for i in range(4):
+                nc.tensor.matmul(sums[u][:, i, :], speech_power[u][:, i, :], identity[:], is_transpose=True, start=(i == 0), stop=False)
+
+        turned_noise = {}
+
+        def turned_noise_power(u):
+            bank = bank_tile(u, [P, PASS])
+            for a in range(2):
+                nc.tensor.matmul_mx(
+                    out=bank[:],
+                    lhsT=noise_q[a][:, block_cols(u)].bitcast(E4M3),
+                    lhsT_scale=noise_s[a][:, block_cols(u)],
+                    rhs=wn_q[a, 0][:].bitcast(E4M3),
+                    rhs_scale=wn_s[a, 0][:],
+                    start=(a == 0),
+                    stop=(a == 1),
+                )
+            turned_noise[u] = turned.tile([P, 4, P], F32, name="turned_noise", align_bytes=64)
+            nc.scalar.activation(out=turned_noise[u][:], in_=bank[:].rearrange("m (p i) -> m i p", i=4), func=ACT.Square)
+
+        def close_sum(u):
+            for i in range(4):
+                nc.tensor.matmul(sums[u][:, i, :], turned_noise[u][:, i, :], identity[:], is_transpose=True, start=False, stop=(i == 3))
+            nc.scalar.activation(out=den[0][:, :, block_cols(u)], in_=sums[u][:], func=ACT.Abs_reciprocal_sqrt, bias=mask_floor)
+
+        def scale_speech(c):
+            part = den[0][:, :, chunk_cols(c)]
+            nc.vector.tensor_tensor(out=part, in0=x[0][:, :, chunk_cols(c)], in1=part, op=ALU.mult)
 
         def square(b, cols):
             nc.scalar.activation(out=x[b][:, :, cols], in_=picked[b][:, :, cols], func=ACT.Square)
@@ -269,7 +321,7 @@ def tile_list_ratio_mask_synthesis_kernel(
             cols = chunk_cols(c)
             z_words[c, b] = rounded_tile([P, CHUNKS[c], 4])
             nc.vector.tensor_tensor(
-                out=by_words(z_words[c, b][:]), in0=by_rows(x[b][:, :, cols]), in1=by_rows(den[b][:, :, cols]), op=ALU.mult
+                out=by_words(z_words[c, b][:]), in0=by_rows((mix_all[0], x[1])[b][:, :, cols]), in1=by_rows(den[b][:, :, cols]), op=ALU.mult
             )
 
         ws_w = shared("ws_w", [P, 2, N], I32, "h1_3")
@@ -357,55 +409,58 @@ def tile_list_ratio_mask_synthesis_kernel(
                 speech(1, i, j)
         noise_words = [first_noise, round_noise(1, on_vector)]
         quantise_noise(0, noise_words[0])
-        first_wn = round_wn(0, 0, on_vector)
+        first_wn = round_wn_plain(0, on_vector)
         quantise_noise(1, noise_words[1])
-        second_wn = round_wn(1, 0, on_scalar)
+        second_wn = round_wn_plain(1, on_scalar)
         quantise_wn(0, 0, first_wn)
         quantise_wn(1, 0, second_wn)
-        square(0, whole)
-        quantise_wn(0, 1, round_wn(0, 1, on_scalar))
-        quantise_wn(1, 1, round_wn(1, 1, on_scalar))
-        noise_power(0, 0)
+        for u in range(4):
+            turn_speech(u)
+        for u in range(4):
+            open_sum(u)
+        third_wn = round_wn(0, 1, on_scalar, on_scalar)
+        last_wn = round_wn(1, 1, on_vector, on_scalar)
+        quantise_wn(0, 1, third_wn)
+        quantise_wn(1, 1, last_wn)
         for i in range(4):
             pick(1, i)
+        for u in range(4):
+            turned_noise_power(u)
+        for u in range(4):
+            close_sum(u)
+        scale_speech(0)
         noise_power(0, 1)
-        power_sum(0, 0)
-        root(0, 0)
         square(1, chunk_cols(0))
         invert(0, 0)
         power_sum(0, 1)
         root(0, 1)
-        noise_power(1, 0)
+        noise_power(1, 1)
         invert(0, 1)
-        numerator(0, 0)
+        scale_speech(1)
         deal_ws()
         round_z(0, 0)
         numerator(0, 1)
         finish(0, 0)
-        noise_power(1, 1)
         square(1, chunk_cols(1))
-        power_sum(1, 0)
-        root(1, 0)
-        round_z(0, 1)
+        invert(1, 0)
         power_sum(1, 1)
+        round_z(0, 1)
+        scale_speech(2)
         finish(0, 1)
         root(1, 1)
-        invert(1, 0)
-        invert(1, 1)
-        noise_power(2, 0)
         noise_power(2, 1)
+        invert(1, 1)
         square(1, chunk_cols(2))
-        for b in range(2):
-            power_sum(2, b)
-            numerator(1, b)
-        for step in (root, invert):
-            for b in range(2):
-                step(2, b)
+        invert(2, 0)
+        power_sum(2, 1)
+        numerator(1, 1)
+        root(2, 1)
+        invert(2, 1)
         for b in range(2):
             round_z(1, b)
         for b in range(2):
             finish(1, b)
-            numerator(2, b)
+        numerator(2, 1)
         for step in (round_z, finish):
             for b in range(2):
                 step(2, b)

@@ -21,7 +21,7 @@ E2M1 = mybir.dt.float4_e2m1fn_x4
 ACT = mybir.ActivationFunctionType
 ALU = mybir.AluOpType
 
-CHUNKS = [256, 128, 128]
+CHUNKS = [128, 128, 128, 128]
 PICK_TILES = 3
 
 
@@ -133,7 +133,7 @@ def tile_list_ratio_mask_synthesis_kernel(
         noise_all = [rows(M + 4 * M * a, M) for a in range(2)]
         wn_raw = {(a, b): rows(9 * M + 4 * PASS * (2 * b + a), PASS) for a in range(2) for b in range(2)}
         mix_all = [rows(25 * M + 4 * M * b, M) for b in range(2)]
-        y_sb = {(c, g): rows(M + 8 * starts[c] + 4 * g * CHUNKS[c], CHUNKS[c]) for c, g in units}
+        y_sb = {(c, g): rows((5, 7, 10, 14)[c] * M + 4 * g * CHUNKS[c], CHUNKS[c]) for c, g in units}
 
         def load_wn(a, b):
             nc.sync.dma_start(
@@ -426,48 +426,46 @@ def tile_list_ratio_mask_synthesis_kernel(
             pick(1, i)
         for u in range(4):
             turned_noise_power(u)
-        for u in range(4):
-            close_sum(u)
+        close_sum(0)
+        close_sum(1)
+        last = len(CHUNKS) - 1
+
+        def planes(c):
+            store_both(round_y, c)
+            store_both(store_planes, c)
+
         scale_speech(0)
         noise_power(0, 1)
         square(1, chunk_cols(0))
-        invert(0, 0)
         power_sum(0, 1)
-        root(0, 1)
-        noise_power(1, 1)
-        invert(0, 1)
-        scale_speech(1)
+        close_sum(2)
+        close_sum(3)
         deal_ws()
-        round_z(0, 0)
-        numerator(0, 1)
-        finish(0, 0)
-        square(1, chunk_cols(1))
-        invert(1, 0)
-        power_sum(1, 1)
-        round_z(0, 1)
-        scale_speech(2)
-        finish(0, 1)
-        root(1, 1)
-        noise_power(2, 1)
-        invert(1, 1)
-        square(1, chunk_cols(2))
-        invert(2, 0)
-        power_sum(2, 1)
-        numerator(1, 1)
-        root(2, 1)
-        invert(2, 1)
-        for b in range(2):
-            round_z(1, b)
-        for b in range(2):
-            finish(1, b)
-        numerator(2, 1)
-        for step in (round_z, finish):
-            for b in range(2):
-                step(2, b)
         for c in range(len(CHUNKS)):
+            invert(c, 0)
+            if c < last:
+                noise_power(c + 1, 1)
+            root(c, 1)
+            round_z(c, 0)
+            numerator(c, 1)
+            if c < last:
+                square(1, chunk_cols(c + 1))
+            invert(c, 1)
+            finish(c, 0)
+            if c < last:
+                scale_speech(c + 1)
+                power_sum(c + 1, 1)
+            round_z(c, 1)
+            finish(c, 1)
+            if c == 1:
+                store_both(store_y, 0)
+                planes(0)
+            if c == 2:
+                store_y(1, 0)
+        store_y(1, 1)
+        for c in (last - 1, last):
             store_both(store_y, c)
-        for c in range(len(CHUNKS)):
-            store_both(round_y, c)
-            store_both(store_planes, c)
+        for c in range(1, len(CHUNKS)):
+            planes(c)
         for q in range(4):
             (nc.scalar, nc.sync)[q % 2].dma_start(out_2[:, 4 * q : 4 * q + 4, :].bitcast(I32), y_s[32 * q : 32 * q + 8, :].bitcast(I32))

@@ -60,15 +60,15 @@ def tile_list_ratio_mask_synthesis_kernel(
 
         idx = keep.tile([P, S // 16], U16, name="idx")
         idx2 = keep.tile([P, M // 16], U16, name="idx2")
-        tab_s = shared("tab_s", [P, T], U8, "late")
-        w4_s = kept("w4_s", [P, 2, H], U8)
+        tab_s = kept("tab_s", [P, T], U8)
+        w4_s = shared("w4_s", [P, 2, H], U8, "late")
         s_dealt = kept("s_dealt", [P, PASS], U8)
         tab_w = [kept("tab_w0", [P, T], I32)]
-        w4_raw = [kept(f"w4_raw{b}", [P, 2, 2 * PASS], U8) for b in range(2)]
+        w4_raw = [kept("w4_raw0", [P, 2, 2 * PASS], U8), None]
         w4_w = [kept(f"w4_w{b}", [P, 2, 2 * PASS], U8) for b in range(2)]
         w4_plane = kept("w4_plane", [P, 2, H], U8)
         ws_plane = kept("ws_plane", [P, 2, 2, PASS], U8)
-        v_picked = shared("v_picked", [P, S], U8, "ws")
+        v_picked = shared("v_picked", [P, S], U8, "picked")
         v_s = kept("v_s", [P, 2, S], U8)
         v_w = [[shared("v_w", [P, BANK], U32, f"v_w{a}_{j}") for j in range(2)] for a in range(2)]
         floor = kept("floor", [P, 16], F32)
@@ -84,8 +84,12 @@ def tile_list_ratio_mask_synthesis_kernel(
         mask_floor = floor[:, 8:9]
         nc.scalar.activation(out=mask_floor, in_=floor[:, 0:1], func=ACT.Abs_reciprocal_sqrt)
 
-        def gather_words(a, j):
-            nc.vector.tensor_copy(out=v_w[a][j][:], in_=tab_w[a][:].bitcast(U32).indirect(idx[:, 32 * j : 32 * (j + 1)]))
+        def gather_words(a, j, first=0, width=BANK):
+            entry = BANK * j + first
+            nc.vector.tensor_copy(
+                out=v_w[a][j][:, first : first + width],
+                in_=tab_w[a][:].bitcast(U32).indirect(idx[:, entry // 16 : (entry + width) // 16]),
+            )
 
         for a in range(2):
             nc.sync.dma_start(tab_s[a:32:2, :].bitcast(I32), tab_scales[a].rearrange("(q r) t -> r q t", r=4).bitcast(I32))
@@ -97,11 +101,17 @@ def tile_list_ratio_mask_synthesis_kernel(
         w4_halves = w4_words.rearrange("a p (b c) -> b p a c", b=2)
         nc.sync.dma_start(w4_raw[0][:].bitcast(I32), w4_halves[0].bitcast(I32))
         nc.sync.dma_start(tab_w[1][:], tab_words[1].rearrange("p t i -> p (t i)").bitcast(I32))
-        nc.sync.dma_start(w4_raw[1][:].bitcast(I32), w4_halves[1].bitcast(I32))
         nc.vector.tensor_copy(out=v_picked[:], in_=tab_s[:].indirect(idx[:]))
-        nc.gpsimd.tensor_copy(
-            out=w4_plane[:].rearrange("p a (b i m) -> p (a b) i m", b=2, i=4), in_=w4_s[:].rearrange("p a (b m i) -> p (a b) i m", b=2, i=4)
-        )
+
+        def deal_w4_scales(b):
+            half = slice(PASS * b, PASS * (b + 1))
+            nc.gpsimd.tensor_copy(
+                out=w4_plane[:, :, half].rearrange("p a (i m) -> p a i m", i=4),
+                in_=w4_s[:, :, half].rearrange("p a (m i) -> p a i m", i=4),
+            )
+
+        for b in range(2):
+            deal_w4_scales(b)
         for r in range(4):
             nc.sync.dma_start(
                 v_s[r:P:32].rearrange("p a c -> p (a c)").bitcast(I32),
@@ -109,7 +119,7 @@ def tile_list_ratio_mask_synthesis_kernel(
             )
 
         def load_ws_scales():
-            s_raw = shared("s_raw", [P, PASS], U8, "w4_s")
+            s_raw = shared("s_raw", [P, PASS], U8, "tab_s")
             nc.gpsimd.memset(s_raw[64:P, :].bitcast(I32), 0)
             for a in range(2):
                 nc.sync.dma_start(s_raw[a:64:2, :].bitcast(I32), ws_scales[a].rearrange("q (b c) -> (q b) c", b=2).bitcast(I32))
@@ -144,8 +154,10 @@ def tile_list_ratio_mask_synthesis_kernel(
         def load_rows(tile, source, a):
             nc.sync.dma_start(tile, source[PASS * a : PASS * (a + 1), :].rearrange("(p j) m -> p j m", j=4))
 
+        w4_raw[1] = shared("w4_raw1", [P, 2, 2 * PASS], U8, "picked")
         nc.sync.dma_start(idx2[:], offs2)
         load_rows(noise_all[0], noise, 0)
+        nc.sync.dma_start(w4_raw[1][:].bitcast(I32), w4_halves[1].bitcast(I32))
         nc.sync.dma_start(wgt_sb, wgt)
         load_rows(noise_all[1], noise, 1)
         load_ws_scales()
@@ -153,39 +165,45 @@ def tile_list_ratio_mask_synthesis_kernel(
             for a in range(2):
                 load_wn(a, b)
         load_rows(mix_all[0], mix, 0)
-        ws_raw = shared("ws_raw", [P, 2, N], I32, "ws")
+        ws_raw = shared("ws_raw", [P, 2, N], I32, "tab_s")
         nc.sync.dma_start(ws_raw[:], ws_words.rearrange("a p c i -> p a (c i)").bitcast(I32))
         load_rows(mix_all[1], mix, 1)
         place_ws_scales()
 
         gather_words(0, 0)
-        for b in range(2):
+        for i in range(4):
             nc.gpsimd.tensor_copy(
-                out=w4_w[b][:].rearrange("p a (i m e) -> p a i m e", i=4, e=2),
-                in_=w4_raw[b][:].rearrange("p a (m i e) -> p a i m e", i=4, e=2),
+                out=w4_w[0][:].rearrange("p a (i m e) -> p a i m e", i=4, e=2)[:, :, i],
+                in_=w4_raw[0][:].rearrange("p a (m i e) -> p a i m e", i=4, e=2)[:, :, i],
             )
-        gather_words(1, 0)
+        gather_words(1, 0, 0, BANK // 2)
+        gather_words(1, 0, BANK // 2, BANK // 2)
         gather_words(0, 1)
         gather_words(1, 1)
+        nc.vector.tensor_copy(
+            out=w4_w[1][:].bitcast(U16).rearrange("p a (i m) -> p a i m", i=4),
+            in_=w4_raw[1][:].bitcast(U16).rearrange("p a (m i) -> p a i m", i=4),
+        )
 
         h = {(b, i): shared("h", [P, S], F32, f"h{b}_{i}") for b in range(2) for i in range(4)}
         x = [noise_all[0], late[:, 9 * M : 25 * M].rearrange("p (i w) -> p i w", i=4)[:, :, 0:M]]
         den = [kept(f"den{b}", [P, 4, M], F32) for b in range(2)]
 
-        def speech(b, i, j):
+        def speech(number, b, i, j, first=0, width=BANK):
             col = PASS * b + P * i
-            bank = bank_tile(2 * i + j, [P, BANK])
+            entries = slice(BANK * j + first, BANK * j + first + width)
+            bank = bank_tile((number + 6) % 8, [P, width])
             for a in range(2):
                 nc.tensor.matmul_mx(
                     out=bank[:],
                     lhsT=w4_w[b][:, a, 2 * P * i : 2 * P * (i + 1)].bitcast(E2M1),
                     lhsT_scale=w4_plane[:, a, col : col + P],
-                    rhs=v_w[a][j][:].bitcast(E4M3),
-                    rhs_scale=v_s[:, a, BANK * j : BANK * (j + 1)],
+                    rhs=v_w[a][j][:, first : first + width].bitcast(E4M3),
+                    rhs_scale=v_s[:, a, entries],
                     start=(a == 0),
                     stop=(a == 1),
                 )
-            nc.scalar.copy(out=h[b, i][:, BANK * j : BANK * (j + 1)], in_=bank[:])
+            nc.scalar.copy(out=h[b, i][:, entries], in_=bank[:])
 
         def pick(b, i):
             nc.vector.tensor_tensor(out=picked[b][:, i, :], in0=h[b, i][:].indirect(idx2[:]), in1=wgt_sb, op=ALU.mult)
@@ -258,43 +276,43 @@ def tile_list_ratio_mask_synthesis_kernel(
 
         speech_power = {}
 
-        def turn_speech(u):
-            bank = bank_tile(u, [P, 4, P])
+        def turn_speech(u, b=0):
+            bank = bank_tile(u + 2 * b, [P, 4, P])
             for i in range(4):
-                nc.tensor.transpose(bank[:, i, :], x[0][:, i, block_cols(u)], identity[:])
-            speech_power[u] = shared("speech_power", [P, 4, P], F32, f"h0_{u}")
-            nc.scalar.activation(out=speech_power[u][:], in_=bank[:], func=ACT.Square)
+                nc.tensor.transpose(bank[:, i, :], x[b][:, i, block_cols(u)], identity[:])
+            speech_power[u, b] = shared("speech_power", [P, 4, P], F32, f"h0_{u}")
+            nc.scalar.activation(out=speech_power[u, b][:], in_=bank[:], func=ACT.Square)
 
-        def open_sum(u):
-            sums[u] = bank_tile(4 + u, [P, 4, P])
+        def open_sum(u, b=0):
+            sums[u, b] = bank_tile(4 + u, [P, 4, P])
             for i in range(4):
-                nc.tensor.matmul(sums[u][:, i, :], speech_power[u][:, i, :], identity[:], is_transpose=True, start=(i == 0), stop=False)
+                nc.tensor.matmul(sums[u, b][:, i, :], (speech_power, turned_noise)[b][u, b][:, i, :], identity[:], is_transpose=True, start=(i == 0), stop=False)
 
         turned_noise = {}
 
-        def turned_noise_power(u):
+        def turned_noise_power(u, b=0):
             bank = bank_tile(u, [P, PASS])
             for a in range(2):
                 nc.tensor.matmul_mx(
                     out=bank[:],
                     lhsT=noise_q[a][:, block_cols(u)].bitcast(E4M3),
                     lhsT_scale=noise_s[a][:, block_cols(u)],
-                    rhs=wn_q[a, 0][:].bitcast(E4M3),
-                    rhs_scale=wn_s[a, 0][:],
+                    rhs=wn_q[a, b][:].bitcast(E4M3),
+                    rhs_scale=wn_s[a, b][:],
                     start=(a == 0),
                     stop=(a == 1),
                 )
-            turned_noise[u] = turned.tile([P, 4, P], F32, name="turned_noise", align_bytes=64)
-            nc.scalar.activation(out=turned_noise[u][:], in_=bank[:].rearrange("m (p i) -> m i p", i=4), func=ACT.Square)
+            turned_noise[u, b] = turned.tile([P, 4, P], F32, name="turned_noise", align_bytes=64)
+            nc.scalar.activation(out=turned_noise[u, b][:], in_=bank[:].rearrange(("m (p i) -> m i p", "m (i p) -> m i p")[b], i=4), func=ACT.Square)
 
-        def close_sum(u):
+        def close_sum(u, b=0):
             for i in range(4):
-                nc.tensor.matmul(sums[u][:, i, :], turned_noise[u][:, i, :], identity[:], is_transpose=True, start=False, stop=(i == 3))
-            nc.scalar.activation(out=den[0][:, :, block_cols(u)], in_=sums[u][:], func=ACT.Abs_reciprocal_sqrt, bias=mask_floor)
+                nc.tensor.matmul(sums[u, b][:, i, :], (turned_noise, speech_power)[b][u, b][:, i, :], identity[:], is_transpose=True, start=False, stop=(i == 3))
+            nc.scalar.activation(out=den[b][:, :, block_cols(u)], in_=sums[u, b][:], func=ACT.Abs_reciprocal_sqrt, bias=mask_floor)
 
-        def scale_speech(c):
-            part = den[0][:, :, chunk_cols(c)]
-            nc.vector.tensor_tensor(out=part, in0=x[0][:, :, chunk_cols(c)], in1=part, op=ALU.mult)
+        def scale_speech(c, b=0):
+            part = den[b][:, :, chunk_cols(c)]
+            nc.vector.tensor_tensor(out=part, in0=x[b][:, :, chunk_cols(c)], in1=part, op=ALU.mult)
 
         def square(b, cols):
             nc.scalar.activation(out=x[b][:, :, cols], in_=picked[b][:, :, cols], func=ACT.Square)
@@ -321,7 +339,7 @@ def tile_list_ratio_mask_synthesis_kernel(
             cols = chunk_cols(c)
             z_words[c, b] = rounded_tile([P, CHUNKS[c], 4])
             nc.vector.tensor_tensor(
-                out=by_words(z_words[c, b][:]), in0=by_rows((mix_all[0], x[1])[b][:, :, cols]), in1=by_rows(den[b][:, :, cols]), op=ALU.mult
+                out=by_words(z_words[c, b][:]), in0=by_rows((x[1] if b == 1 and c >= 2 else mix_all[b])[:, :, cols]), in1=by_rows(den[b][:, :, cols]), op=ALU.mult
             )
 
         ws_w = shared("ws_w", [P, 2, N], I32, "h1_3")
@@ -385,7 +403,7 @@ def tile_list_ratio_mask_synthesis_kernel(
                 store(c, g)
 
         whole = slice(0, M)
-        idle_bank = bank_tile(7, [P, BANK])
+        idle_bank = bank_tile(5, [P, BANK])
         for turn in range(4):
             nc.tensor.matmul_mx(
                 out=idle_bank[:],
@@ -398,15 +416,17 @@ def tile_list_ratio_mask_synthesis_kernel(
             )
         on_vector, on_scalar = nc.vector.tensor_copy, nc.scalar.copy
         first_noise = round_noise(0, on_vector)
-        speech(0, 0, 0)
+        for quarter in range(2):
+            for i in range(2):
+                speech(2 * quarter + i, 0, i, 0, quarter * BANK // 2, BANK // 2)
+        for i in range(2, 4):
+            speech(2 + i, 0, i, 0)
         for i in range(4):
-            if i < 3:
-                speech(0, i + 1, 0)
-            speech(0, i, 1)
+            speech(6 + i, 0, i, 1)
             pick(0, i)
         for i in range(4):
             for j in range(2):
-                speech(1, i, j)
+                speech(10 + 2 * i + j, 1, i, j)
         noise_words = [first_noise, round_noise(1, on_vector)]
         quantise_noise(0, noise_words[0])
         first_wn = round_wn_plain(0, on_vector)
@@ -419,7 +439,7 @@ def tile_list_ratio_mask_synthesis_kernel(
         for u in range(4):
             open_sum(u)
         third_wn = round_wn(0, 1, on_scalar, on_scalar)
-        last_wn = round_wn(1, 1, on_vector, on_scalar)
+        last_wn = round_wn(1, 1, on_vector, on_vector)
         quantise_wn(0, 1, third_wn)
         quantise_wn(1, 1, last_wn)
         for i in range(4):
@@ -435,35 +455,59 @@ def tile_list_ratio_mask_synthesis_kernel(
             store_both(store_planes, c)
 
         scale_speech(0)
-        noise_power(0, 1)
-        square(1, chunk_cols(0))
-        power_sum(0, 1)
+        scale_speech(1)
         close_sum(2)
         close_sum(3)
+        for u in range(2):
+            turned_noise_power(u, 1)
+        for step in (open_sum, turn_speech):
+            for u in range(2):
+                step(u, 1)
         deal_ws()
-        for c in range(len(CHUNKS)):
-            invert(c, 0)
-            if c < last:
-                noise_power(c + 1, 1)
-            root(c, 1)
-            round_z(c, 0)
-            numerator(c, 1)
-            if c < last:
-                square(1, chunk_cols(c + 1))
-            invert(c, 1)
-            finish(c, 0)
-            if c < last:
-                scale_speech(c + 1)
-                power_sum(c + 1, 1)
-            round_z(c, 1)
-            finish(c, 1)
-            if c == 1:
-                store_both(store_y, 0)
-                planes(0)
-            if c == 2:
-                store_y(1, 0)
+        invert(0, 0)
+        invert(1, 0)
+        for u in range(2):
+            close_sum(u, 1)
+            scale_speech(u, 1)
+        round_z(0, 0)
+        round_z(1, 0)
+        noise_power(2, 1)
+        invert(0, 1)
+        square(1, chunk_cols(2))
+        invert(1, 1)
+        finish(0, 0)
+        round_z(0, 1)
+        power_sum(2, 1)
+        finish(0, 1)
+        scale_speech(2)
+        round_z(1, 1)
+        finish(1, 0)
+        finish(1, 1)
+        invert(2, 0)
+        root(2, 1)
+        store_both(store_y, 0)
+        noise_power(3, 1)
+        invert(2, 1)
+        square(1, chunk_cols(3))
+        numerator(2, 1)
+        scale_speech(3)
+        power_sum(3, 1)
+        round_z(2, 0)
+        round_z(2, 1)
+        finish(2, 0)
+        finish(2, 1)
+        invert(3, 0)
+        store_y(1, 0)
+        root(3, 1)
+        numerator(3, 1)
         store_y(1, 1)
-        for c in (last - 1, last):
+        invert(3, 1)
+        planes(0)
+        round_z(3, 0)
+        round_z(3, 1)
+        finish(3, 0)
+        finish(3, 1)
+        for c in range(2, len(CHUNKS)):
             store_both(store_y, c)
         for c in range(1, len(CHUNKS)):
             planes(c)

@@ -8,6 +8,7 @@ P = 128
 PASS = 512
 BANK = 512
 HALF = M // 2
+CHUNKS = M // P
 FLOPS = 2 * K * H * S + 2 * K * H * M + 2 * H * N * M
 
 F32 = mybir.dt.float32
@@ -21,23 +22,19 @@ E2M1 = mybir.dt.float4_e2m1fn_x4
 ACT = mybir.ActivationFunctionType
 ALU = mybir.AluOpType
 
-CHUNKS = [128, 128, 128, 128]
-PICK_TILES = 3
-
 
 def tile_list_ratio_mask_synthesis_kernel(
     tc, tab_words, tab_scales, offs, w4_words, w4_scales, offs2, wgt, noise, wn, mix, ws_words, ws_scales,
     out_0, out_1, out_2,
 ):
     nc = tc.nc
-    starts = [sum(CHUNKS[:c]) for c in range(len(CHUNKS))]
-    units = [(c, b) for c in range(len(CHUNKS)) for b in range(2)]
-    last_chunk = len(CHUNKS) - 1
+    on_vector, on_scalar = nc.vector.tensor_copy, nc.scalar.copy
+    units = [(c, b) for c in range(CHUNKS) for b in range(2)]
 
     with ExitStack() as ctx:
         keep = ctx.enter_context(tc.tile_pool(name="keep", bufs=1))
         rounded = ctx.enter_context(tc.tile_pool(name="rounded", bufs=4))
-        turned = ctx.enter_context(tc.tile_pool(name="turned", bufs=4))
+        turned = ctx.enter_context(tc.tile_pool(name="turned", bufs=CHUNKS))
         psum = ctx.enter_context(tc.psum_pool(name="psum", bufs=1))
 
         def kept(name, shape, dtype):
@@ -46,17 +43,14 @@ def tile_list_ratio_mask_synthesis_kernel(
         def shared(name, shape, dtype, tag):
             return keep.tile(shape, dtype, name=name, tag=tag, align_bytes=64)
 
-        def rounded_tile(shape):
-            return rounded.tile(shape, BF16, name="rounded", tag="rounded", align_bytes=64)
+        def rounded_tile(width):
+            return rounded.tile([P, width, 4], BF16, name="rounded", tag="rounded", align_bytes=64)
 
         def bank_tile(number, shape):
             return psum.tile(shape, F32, name="bank", tag=f"bank{number}")
 
         def chunk_cols(c):
-            return slice(starts[c], starts[c] + CHUNKS[c])
-
-        def chunk_bank(c, row_pass, slot):
-            return (8 * starts[c] + (4 * row_pass + slot) * CHUNKS[c]) // BANK
+            return slice(P * c, P * (c + 1))
 
         idx = keep.tile([P, S // 16], U16, name="idx")
         idx2 = keep.tile([P, M // 16], U16, name="idx2")
@@ -141,9 +135,9 @@ def tile_list_ratio_mask_synthesis_kernel(
             return late[:, first : first + 4 * width].rearrange("p (j m) -> p j m", j=4)
 
         noise_all = [rows(M + 4 * M * a, M) for a in range(2)]
-        wn_raw = {(a, b): rows(9 * M + 4 * PASS * (2 * b + a), PASS) for a in range(2) for b in range(2)}
+        wn_raw = {(a, b): rows(9 * M + 4 * PASS * (2 * a + b), PASS) for a in range(2) for b in range(2)}
         mix_all = [rows(25 * M + 4 * M * b, M) for b in range(2)]
-        y_sb = {(c, g): rows((5, 7, 10, 14)[c] * M + 4 * g * CHUNKS[c], CHUNKS[c]) for c, g in units}
+        y_sb = {(c, g): rows((5 + 2 * c) * M + 4 * g * P, P) for c, g in units}
 
         def load_wn(a, b):
             nc.sync.dma_start(
@@ -156,14 +150,17 @@ def tile_list_ratio_mask_synthesis_kernel(
 
         w4_raw[1] = shared("w4_raw1", [P, 2, 2 * PASS], U8, "picked")
         nc.sync.dma_start(idx2[:], offs2)
-        load_rows(noise_all[0], noise, 0)
+        for half in range(2):
+            cols = slice(HALF * half, HALF * (half + 1))
+            nc.sync.dma_start(noise_all[0][:, :, cols], noise[0:PASS, cols].rearrange("(p j) m -> p j m", j=4))
         nc.sync.dma_start(w4_raw[1][:].bitcast(I32), w4_halves[1].bitcast(I32))
         nc.sync.dma_start(wgt_sb, wgt)
-        load_rows(noise_all[1], noise, 1)
+        load_wn(0, 0)
         load_ws_scales()
-        for b in range(2):
-            for a in range(2):
-                load_wn(a, b)
+        load_rows(noise_all[1], noise, 1)
+        load_wn(1, 0)
+        for a in range(2):
+            load_wn(a, 1)
         load_rows(mix_all[0], mix, 0)
         ws_raw = shared("ws_raw", [P, 2, N], I32, "tab_s")
         nc.sync.dma_start(ws_raw[:], ws_words.rearrange("a p c i -> p a (c i)").bitcast(I32))
@@ -186,13 +183,13 @@ def tile_list_ratio_mask_synthesis_kernel(
         )
 
         h = {(b, i): shared("h", [P, S], F32, f"h{b}_{i}") for b in range(2) for i in range(4)}
-        x = [noise_all[0], late[:, 9 * M : 25 * M].rearrange("p (i w) -> p i w", i=4)[:, :, 0:M]]
-        den = [kept(f"den{b}", [P, 4, M], F32) for b in range(2)]
+        x = [noise_all[0], rows(20 * M, M)]
+        ratio = [kept(f"ratio{b}", [P, 4, M], F32) for b in range(2)]
 
         def speech(number, b, i, j, first=0, width=BANK):
             col = PASS * b + P * i
             entries = slice(BANK * j + first, BANK * j + first + width)
-            bank = bank_tile((number + 6) % 8, [P, width])
+            bank = bank_tile((number + 2) % 8, [P, width])
             for a in range(2):
                 nc.tensor.matmul_mx(
                     out=bank[:],
@@ -206,7 +203,7 @@ def tile_list_ratio_mask_synthesis_kernel(
             nc.scalar.copy(out=h[b, i][:, entries], in_=bank[:])
 
         def pick(b, i):
-            nc.vector.tensor_tensor(out=picked[b][:, i, :], in0=h[b, i][:].indirect(idx2[:]), in1=wgt_sb, op=ALU.mult)
+            nc.vector.tensor_tensor(out=x[b][:, i, :], in0=h[b, i][:].indirect(idx2[:]), in1=wgt_sb, op=ALU.mult)
 
         noise_q = [kept(f"noise_q{a}", [P, M], U32) for a in range(2)]
         noise_s = [kept(f"noise_s{a}", [P, M], U8) for a in range(2)]
@@ -223,169 +220,103 @@ def tile_list_ratio_mask_synthesis_kernel(
             nc.vector.quantize_mx(out=codes.bitcast(E4M3), scales=scales, in_=words)
 
         def round_noise(a, copy):
-            words = rounded_tile([P, M, 4])
-            copy(out=by_words(words[:]), in_=by_rows(noise_all[a]))
+            words = rounded_tile(M)
+            width = (HALF, M)[a]
+            for first in range(0, M, width):
+                cols = slice(first, first + width)
+                copy(out=by_words(words[:, cols, :]), in_=by_rows(noise_all[a][:, :, cols]))
             return words
 
         def quantise_noise(a, words):
             quantise(noise_q[a][:], noise_s[a][:], words[:].rearrange("p m j -> p (m j)"))
 
-        def round_wn_plain(a, copy):
-            words = rounded_tile([P, PASS, 4])
-            copy(out=by_words(words[:]), in_=by_rows(wn_raw[a, 0]))
-            return words[:].rearrange("p (i m) j -> p i m j", i=4)
-
         def round_wn(a, b, *copies):
-            words = rounded_tile([P, 4, P, 4])
+            words = shared("middle", [P, PASS, 4], BF16, "middle") if a != b else rounded_tile(PASS)
             for pair, copy in enumerate(copies):
                 slots = slice(2 * pair, 2 * pair + 2)
                 copy(
-                    out=words[:, slots, :, :].rearrange("p i m j -> p m j i"),
+                    out=words[:].rearrange("p (i m) j -> p m j i", i=4)[:, :, :, slots],
                     in_=wn_raw[a, b].rearrange("p j (m i) -> p m j i", i=4)[:, :, :, slots],
                 )
             return words
 
         def quantise_wn(a, b, words):
-            quantise(wn_q[a, b][:], wn_s[a, b][:], words[:].rearrange("p i m j -> p (i m j)"))
+            quantise(wn_q[a, b][:], wn_s[a, b][:], words[:].rearrange("p c j -> p (c j)"))
 
-        def noise_power(c, b):
-            per_bank = BANK // CHUNKS[c]
-            for first in range(0, 4, per_bank):
-                bank = bank_tile(chunk_bank(c, b, first), [P, per_bank, CHUNKS[c]])
-                for i in range(first, first + per_bank):
-                    for a in range(2):
-                        nc.tensor.matmul_mx(
-                            out=bank[:, i - first, :],
-                            lhsT=wn_q[a, b][:, P * i : P * (i + 1)].bitcast(E4M3),
-                            lhsT_scale=wn_s[a, b][:, P * i : P * (i + 1)],
-                            rhs=noise_q[a][:, chunk_cols(c)].bitcast(E4M3),
-                            rhs_scale=noise_s[a][:, chunk_cols(c)],
-                            start=(a == 0),
-                            stop=(a == 1),
-                        )
-                nc.scalar.activation(out=den[b][:, first : first + per_bank, chunk_cols(c)], in_=bank[:], func=ACT.Square)
+        noise_banks, noise_power, speech_power, sums = {}, {}, {}, {}
+
+        def noise_pass(c, b, a):
+            if a == 0:
+                noise_banks[c, b] = bank_tile(c, [P, PASS])
+            nc.tensor.matmul_mx(
+                out=noise_banks[c, b][:],
+                lhsT=noise_q[a][:, chunk_cols(c)].bitcast(E4M3),
+                lhsT_scale=noise_s[a][:, chunk_cols(c)],
+                rhs=wn_q[a, b][:].bitcast(E4M3),
+                rhs_scale=wn_s[a, b][:],
+                start=(a == 0),
+                stop=(a == 1),
+            )
+
+        def square_noise(c, b):
+            noise_power[c, b] = turned.tile([P, 4, P], F32, name="noise_power", align_bytes=64)[:]
+            nc.scalar.activation(
+                out=noise_power[c, b], in_=noise_banks[c, b][:].rearrange("m (i p) -> m i p", i=4), func=ACT.Square
+            )
+
+        def square_speech(c, b):
+            bank = bank_tile(c + (4, 0)[b], [P, 4, P])
+            for i in range(4):
+                nc.tensor.transpose(bank[:, i, :], x[b][:, i, chunk_cols(c)], identity[:])
+            if b == 0 and c >= 2:
+                speech_power[c, b] = wn_raw[1, 0][:, c - 2, :].rearrange("p (i m) -> p i m", i=4)
+            else:
+                speech_power[c, b] = shared("speech_power", [P, 4, P], F32, f"h0_{c}")[:]
+            nc.scalar.activation(out=speech_power[c, b], in_=bank[:], func=ACT.Square)
+
+        def add_turned(c, b, term, opens):
+            for i in range(4):
+                nc.tensor.matmul(
+                    sums[c, b][:, i, :], term[:, i, :], identity[:], is_transpose=True,
+                    start=(opens and i == 0), stop=(not opens and i == 3),
+                )
+
+        def open_sum(c, b):
+            sums[c, b] = bank_tile(4 + c, [P, 4, P])
+            add_turned(c, b, (speech_power, noise_power)[b][c, b], True)
+
+        def close_sum(c, b):
+            add_turned(c, b, (noise_power, speech_power)[b][c, b], False)
+            nc.scalar.activation(
+                out=ratio[b][:, :, chunk_cols(c)], in_=sums[c, b][:], func=ACT.Abs_reciprocal_sqrt, bias=mask_floor
+            )
+
+        def scale_speech(c, b):
+            part = ratio[b][:, :, chunk_cols(c)]
+            nc.vector.tensor_tensor(out=part, in0=x[b][:, :, chunk_cols(c)], in1=part, op=ALU.mult)
+
+        mask = {}
+
+        def square_ratio(c, b):
+            part = ratio[b][:, :, chunk_cols(c)]
+            mask[c, b] = shared("mask", [P, 4, P], F32, f"h0_{c}")[:] if b == 0 else part
+            nc.scalar.activation(out=mask[c, b], in_=part, func=ACT.Square)
 
         z_q = [kept(f"z_q{b}", [P, M], U32) for b in range(2)]
         z_s = [kept(f"z_s{b}", [P, M], U8) for b in range(2)]
-
-        picked = x
-        sums = {}
-
-        def block_cols(u):
-            return slice(P * u, P * (u + 1))
-
-        speech_power = {}
-
-        def turn_speech(u, b=0):
-            bank = bank_tile(u + 2 * b, [P, 4, P])
-            for i in range(4):
-                nc.tensor.transpose(bank[:, i, :], x[b][:, i, block_cols(u)], identity[:])
-            speech_power[u, b] = shared("speech_power", [P, 4, P], F32, f"h0_{u}")
-            nc.scalar.activation(out=speech_power[u, b][:], in_=bank[:], func=ACT.Square)
-
-        def open_sum(u, b=0):
-            sums[u, b] = bank_tile(4 + u, [P, 4, P])
-            for i in range(4):
-                nc.tensor.matmul(sums[u, b][:, i, :], (speech_power, turned_noise)[b][u, b][:, i, :], identity[:], is_transpose=True, start=(i == 0), stop=False)
-
-        turned_noise = {}
-
-        def turned_noise_power(u, b=0):
-            bank = bank_tile(u, [P, PASS])
-            for a in range(2):
-                nc.tensor.matmul_mx(
-                    out=bank[:],
-                    lhsT=noise_q[a][:, block_cols(u)].bitcast(E4M3),
-                    lhsT_scale=noise_s[a][:, block_cols(u)],
-                    rhs=wn_q[a, b][:].bitcast(E4M3),
-                    rhs_scale=wn_s[a, b][:],
-                    start=(a == 0),
-                    stop=(a == 1),
-                )
-            turned_noise[u, b] = turned.tile([P, 4, P], F32, name="turned_noise", align_bytes=64)
-            nc.scalar.activation(out=turned_noise[u, b][:], in_=bank[:].rearrange(("m (p i) -> m i p", "m (i p) -> m i p")[b], i=4), func=ACT.Square)
-
-        def close_sum(u, b=0):
-            for i in range(4):
-                nc.tensor.matmul(sums[u, b][:, i, :], (turned_noise, speech_power)[b][u, b][:, i, :], identity[:], is_transpose=True, start=False, stop=(i == 3))
-            nc.scalar.activation(out=den[b][:, :, block_cols(u)], in_=sums[u, b][:], func=ACT.Abs_reciprocal_sqrt, bias=mask_floor)
-
-        def scale_speech(c, b=0):
-            part = den[b][:, :, chunk_cols(c)]
-            nc.vector.tensor_tensor(out=part, in0=x[b][:, :, chunk_cols(c)], in1=part, op=ALU.mult)
-
-        def square(b, cols):
-            nc.scalar.activation(out=x[b][:, :, cols], in_=picked[b][:, :, cols], func=ACT.Square)
-
-        def numerator(c, b):
-            cols = chunk_cols(c)
-            nc.vector.tensor_tensor(out=x[b][:, :, cols], in0=x[b][:, :, cols], in1=mix_all[b][:, :, cols], op=ALU.mult)
-
-        def power_sum(c, b):
-            part = den[b][:, :, chunk_cols(c)]
-            nc.vector.tensor_tensor(out=part, in0=x[b][:, :, chunk_cols(c)], in1=part, op=ALU.add)
-
-        def root(c, b):
-            part = den[b][:, :, chunk_cols(c)]
-            nc.scalar.activation(out=part, in_=part, func=ACT.Abs_reciprocal_sqrt, bias=mask_floor)
-
-        def invert(c, b):
-            part = den[b][:, :, chunk_cols(c)]
-            nc.scalar.activation(out=part, in_=part, func=ACT.Square)
-
         z_words = {}
 
         def round_z(c, b):
-            cols = chunk_cols(c)
-            z_words[c, b] = rounded_tile([P, CHUNKS[c], 4])
+            z_words[c, b] = rounded_tile(P)
             nc.vector.tensor_tensor(
-                out=by_words(z_words[c, b][:]), in0=by_rows((x[1] if b == 1 and c >= 2 else mix_all[b])[:, :, cols]), in1=by_rows(den[b][:, :, cols]), op=ALU.mult
+                out=by_words(z_words[c, b][:]), in0=by_rows(mix_all[b][:, :, chunk_cols(c)]), in1=by_rows(mask[c, b]),
+                op=ALU.mult,
             )
 
         ws_w = shared("ws_w", [P, 2, N], I32, "h1_3")
         y_s = kept("y_s", [P, M], U8)
-        y_q = [kept(f"y_q{c}", [P, 2, width], I32) for c, width in enumerate(CHUNKS)]
-        y_banks = {}
-
-        def synthesis_pass(c, b):
-            per_bank = BANK // CHUNKS[c]
-            for g in range(2):
-                for first in range(0, 4, per_bank):
-                    if b == 0:
-                        y_banks[c, g, first] = bank_tile(chunk_bank(c, g, first), [P, per_bank, CHUNKS[c]])
-                    for t in range(first, first + per_bank):
-                        col = PASS * g + P * t
-                        nc.tensor.matmul_mx(
-                            out=y_banks[c, g, first][:, t - first, :],
-                            lhsT=ws_w[:, b, col : col + P].bitcast(E4M3),
-                            lhsT_scale=ws_plane[:, g, b, P * t : P * (t + 1)],
-                            rhs=z_q[b][:, chunk_cols(c)].bitcast(E4M3),
-                            rhs_scale=z_s[b][:, chunk_cols(c)],
-                            start=(b == 0 and t == first),
-                            stop=(b == 1 and t == first + per_bank - 1),
-                        )
-
-        def store_y(c, g):
-            per_bank = BANK // CHUNKS[c]
-            copy = nc.scalar.copy
-            for first in range(0, 4, per_bank):
-                slots = slice(first, first + per_bank)
-                copy(out=y_sb[c, g][:, slots, :], in_=y_banks[c, g, first][:])
-                nc.sync.dma_start(
-                    out_0[PASS * g : PASS * (g + 1), chunk_cols(c)].rearrange("(p t) m -> p t m", t=4)[:, slots, :],
-                    y_sb[c, g][:, slots, :],
-                )
-
-        y_words = {}
-
-        def round_y(c, g):
-            y_words[c, g] = rounded_tile([P, CHUNKS[c], 4])
-            nc.vector.tensor_copy(out=by_words(y_words[c, g][:]), in_=by_rows(y_sb[c, g]))
-
-        def store_planes(c, g):
-            quantise(y_q[c][:, g, :], y_s[4 * g : P, chunk_cols(c)], y_words[c, g][:].rearrange("p m t -> p (m t)"))
-            if g == 1:
-                nc.sync.dma_start(out_1[:, :, chunk_cols(c), :].rearrange("g p m t -> p g (m t)").bitcast(I32), y_q[c][:])
+        y_q = [kept(f"y_q{half}", [P, 2, HALF], I32) for half in range(2)]
+        y_banks, y_words = {}, {}
 
         def deal_ws():
             nc.vector.tensor_copy(
@@ -393,17 +324,41 @@ def tile_list_ratio_mask_synthesis_kernel(
                 in_=ws_raw[:].rearrange("p b (g m t) -> p (b g) m t", g=2, t=4),
             )
 
-        def finish(c, b):
+        def synthesise(c, b):
             cols = chunk_cols(c)
             quantise(z_q[b][:, cols], z_s[b][:, cols], z_words[c, b][:].rearrange("p m i -> p (m i)"))
-            synthesis_pass(c, b)
-
-        def store_both(store, c):
             for g in range(2):
-                store(c, g)
+                if b == 0:
+                    y_banks[c, g] = bank_tile(2 * c + g, [P, 4, P])
+                for t in range(4):
+                    col = PASS * g + P * t
+                    nc.tensor.matmul_mx(
+                        out=y_banks[c, g][:, t, :],
+                        lhsT=ws_w[:, b, col : col + P].bitcast(E4M3),
+                        lhsT_scale=ws_plane[:, g, b, P * t : P * (t + 1)],
+                        rhs=z_q[b][:, cols].bitcast(E4M3),
+                        rhs_scale=z_s[b][:, cols],
+                        start=(b == 0 and t == 0),
+                        stop=(b == 1 and t == 3),
+                    )
 
-        whole = slice(0, M)
-        idle_bank = bank_tile(5, [P, BANK])
+        def store_y(c, g):
+            nc.scalar.copy(out=y_sb[c, g], in_=y_banks[c, g][:])
+            nc.sync.dma_start(
+                out_0[PASS * g : PASS * (g + 1), chunk_cols(c)].rearrange("(p t) m -> p t m", t=4), y_sb[c, g]
+            )
+
+        def round_y(c, g):
+            y_words[c, g] = rounded_tile(P)
+            nc.vector.tensor_copy(out=by_words(y_words[c, g][:]), in_=by_rows(y_sb[c, g]))
+
+        def quantise_y(c, g):
+            quantise(
+                y_q[c // 2][:, g, chunk_cols(c % 2)], y_s[4 * g : P, chunk_cols(c)],
+                y_words[c, g][:].rearrange("p m t -> p (m t)"),
+            )
+
+        idle_bank = bank_tile(1, [P, BANK])
         for turn in range(4):
             nc.tensor.matmul_mx(
                 out=idle_bank[:],
@@ -414,7 +369,6 @@ def tile_list_ratio_mask_synthesis_kernel(
                 start=True,
                 stop=True,
             )
-        on_vector, on_scalar = nc.vector.tensor_copy, nc.scalar.copy
         first_noise = round_noise(0, on_vector)
         for quarter in range(2):
             for i in range(2):
@@ -427,89 +381,68 @@ def tile_list_ratio_mask_synthesis_kernel(
         for i in range(4):
             for j in range(2):
                 speech(10 + 2 * i + j, 1, i, j)
-        noise_words = [first_noise, round_noise(1, on_vector)]
-        quantise_noise(0, noise_words[0])
-        first_wn = round_wn_plain(0, on_vector)
-        quantise_noise(1, noise_words[1])
-        second_wn = round_wn_plain(1, on_scalar)
+        first_wn = round_wn(0, 0, on_vector, on_vector)
+        quantise_noise(0, first_noise)
+        second_noise = round_noise(1, on_vector)
         quantise_wn(0, 0, first_wn)
+        second_wn = round_wn(1, 0, on_scalar, on_scalar)
+        quantise_noise(1, second_noise)
         quantise_wn(1, 0, second_wn)
-        for u in range(4):
-            turn_speech(u)
-        for u in range(4):
-            open_sum(u)
-        third_wn = round_wn(0, 1, on_scalar, on_scalar)
+        for c in range(CHUNKS):
+            square_speech(c, 0)
+        for c in range(CHUNKS):
+            noise_pass(c, 0, 0)
+        for c in range(2):
+            open_sum(c, 0)
+        third_wn = round_wn(0, 1, on_scalar, on_vector)
         last_wn = round_wn(1, 1, on_vector, on_vector)
         quantise_wn(0, 1, third_wn)
         quantise_wn(1, 1, last_wn)
         for i in range(4):
             pick(1, i)
-        for u in range(4):
-            turned_noise_power(u)
-        close_sum(0)
-        close_sum(1)
-        last = len(CHUNKS) - 1
-
-        def planes(c):
-            store_both(round_y, c)
-            store_both(store_planes, c)
-
-        scale_speech(0)
-        scale_speech(1)
-        close_sum(2)
-        close_sum(3)
-        for u in range(2):
-            turned_noise_power(u, 1)
-        for step in (open_sum, turn_speech):
-            for u in range(2):
-                step(u, 1)
+        for c in range(CHUNKS):
+            noise_pass(c, 0, 1)
+            square_noise(c, 0)
+        for c in range(2, CHUNKS):
+            open_sum(c, 0)
+        for c in range(CHUNKS):
+            close_sum(c, 0)
+        for c in range(CHUNKS):
+            for a in range(2):
+                noise_pass(c, 1, a)
+            square_noise(c, 1)
+        for c in range(CHUNKS):
+            open_sum(c, 1)
+            scale_speech(c, 0)
         deal_ws()
-        invert(0, 0)
-        invert(1, 0)
-        for u in range(2):
-            close_sum(u, 1)
-            scale_speech(u, 1)
-        round_z(0, 0)
-        round_z(1, 0)
-        noise_power(2, 1)
-        invert(0, 1)
-        square(1, chunk_cols(2))
-        invert(1, 1)
-        finish(0, 0)
-        round_z(0, 1)
-        power_sum(2, 1)
-        finish(0, 1)
-        scale_speech(2)
-        round_z(1, 1)
-        finish(1, 0)
-        finish(1, 1)
-        invert(2, 0)
-        root(2, 1)
-        store_both(store_y, 0)
-        noise_power(3, 1)
-        invert(2, 1)
-        square(1, chunk_cols(3))
-        numerator(2, 1)
-        scale_speech(3)
-        power_sum(3, 1)
-        round_z(2, 0)
-        round_z(2, 1)
-        finish(2, 0)
-        finish(2, 1)
-        invert(3, 0)
-        store_y(1, 0)
-        root(3, 1)
-        numerator(3, 1)
-        store_y(1, 1)
-        invert(3, 1)
-        planes(0)
-        round_z(3, 0)
-        round_z(3, 1)
-        finish(3, 0)
-        finish(3, 1)
-        for c in range(2, len(CHUNKS)):
-            store_both(store_y, c)
-        for c in range(1, len(CHUNKS)):
-            planes(c)
+        for c in range(CHUNKS - 1):
+            square_speech(c, 1)
+        for n in range(len(units) + 2):
+            if n < CHUNKS:
+                close_sum(n, 1)
+            if n < len(units):
+                square_ratio(*units[n])
+            if n == 0:
+                square_speech(CHUNKS - 1, 1)
+            if n < CHUNKS:
+                scale_speech(n, 1)
+            if 1 <= n <= len(units):
+                round_z(*units[n - 1])
+            if n >= 2:
+                synthesise(*units[n - 2])
+            if n in (4, 6):
+                store_y(0, n // 2 - 2)
+        for c in range(1, CHUNKS):
+            for g in range(2):
+                store_y(c, g)
+        for c in range(CHUNKS):
+            for step in (round_y, quantise_y):
+                for g in range(2):
+                    step(c, g)
+            if c % 2 == 1:
+                cols = slice(HALF * (c // 2), HALF * (c // 2 + 1))
+                nc.sync.dma_start(out_1[:, :, cols, :].rearrange("g p m t -> p g (m t)").bitcast(I32), y_q[c // 2][:])
         for q in range(4):
-            (nc.scalar, nc.sync)[q % 2].dma_start(out_2[:, 4 * q : 4 * q + 4, :].bitcast(I32), y_s[32 * q : 32 * q + 8, :].bitcast(I32))
+            (nc.scalar, nc.sync)[q % 2].dma_start(
+                out_2[:, 4 * q : 4 * q + 4, :].bitcast(I32), y_s[32 * q : 32 * q + 8, :].bitcast(I32)
+            )

@@ -56,6 +56,7 @@ def tile_list_ratio_mask_synthesis_kernel(
         idx2 = keep.tile([P, M // 16], U16, name="idx2")
         tab_s = kept("tab_s", [P, T], U8)
         w4_s = shared("w4_s", [P, 2, H], U8, "late")
+        s_raw = kept("s_raw", [P, PASS], U8)
         s_dealt = kept("s_dealt", [P, PASS], U8)
         tab_w = [kept("tab_w0", [P, T], I32)]
         w4_raw = [kept("w4_raw0", [P, 2, 2 * PASS], U8), None]
@@ -72,6 +73,7 @@ def tile_list_ratio_mask_synthesis_kernel(
         nc.vector.memset(tab_s[64:P, :].bitcast(I32), 0)
         nc.vector.memset(floor[:, 0:1], 25.0)
         nc.vector.memset(v_s[:].rearrange("p a c -> p (a c)").bitcast(I32), 0)
+        nc.vector.memset(s_raw[64:P, :].bitcast(I32), 0)
         nc.vector.memset(ws_plane[:].rearrange("p b a c -> p (b a c)").bitcast(I32), 0)
         identity = kept("identity", [P, P], F32)
         make_identity(nc, identity[:])
@@ -94,6 +96,7 @@ def tile_list_ratio_mask_synthesis_kernel(
         nc.sync.dma_start(tab_w[0][:], tab_words[0].rearrange("p t i -> p (t i)").bitcast(I32))
         w4_halves = w4_words.rearrange("a p (b c) -> b p a c", b=2)
         nc.sync.dma_start(w4_raw[0][:].bitcast(I32), w4_halves[0].bitcast(I32))
+        nc.sync.dma_start(idx2[:], offs2)
         nc.sync.dma_start(tab_w[1][:], tab_words[1].rearrange("p t i -> p (t i)").bitcast(I32))
         nc.vector.tensor_copy(out=v_picked[:], in_=tab_s[:].indirect(idx[:]))
 
@@ -112,14 +115,8 @@ def tile_list_ratio_mask_synthesis_kernel(
                 v_picked[8 * r : 8 * r + 8, :].bitcast(I32),
             )
 
-        def load_ws_scales():
-            s_raw = shared("s_raw", [P, PASS], U8, "tab_s")
-            nc.gpsimd.memset(s_raw[64:P, :].bitcast(I32), 0)
-            for a in range(2):
-                nc.sync.dma_start(s_raw[a:64:2, :].bitcast(I32), ws_scales[a].rearrange("q (b c) -> (q b) c", b=2).bitcast(I32))
-            nc.vector.tensor_copy(
-                out=s_dealt[:].rearrange("p (i m) -> p i m", i=4), in_=s_raw[:].rearrange("p (m i) -> p i m", i=4)
-            )
+        for a in range(2):
+            nc.sync.dma_start(s_raw[a:64:2, :].bitcast(I32), ws_scales[a].rearrange("q (b c) -> (q b) c", b=2).bitcast(I32))
 
         def place_ws_scales():
             for q in range(4):
@@ -149,23 +146,17 @@ def tile_list_ratio_mask_synthesis_kernel(
             nc.sync.dma_start(tile, source[PASS * a : PASS * (a + 1), :].rearrange("(p j) m -> p j m", j=4))
 
         w4_raw[1] = shared("w4_raw1", [P, 2, 2 * PASS], U8, "picked")
-        nc.sync.dma_start(idx2[:], offs2)
         for half in range(2):
             cols = slice(HALF * half, HALF * (half + 1))
             nc.sync.dma_start(noise_all[0][:, :, cols], noise[0:PASS, cols].rearrange("(p j) m -> p j m", j=4))
         nc.sync.dma_start(w4_raw[1][:].bitcast(I32), w4_halves[1].bitcast(I32))
         nc.sync.dma_start(wgt_sb, wgt)
         load_wn(0, 0)
-        load_ws_scales()
         load_rows(noise_all[1], noise, 1)
         load_wn(1, 0)
         for a in range(2):
             load_wn(a, 1)
         load_rows(mix_all[0], mix, 0)
-        ws_raw = shared("ws_raw", [P, 2, N], I32, "tab_s")
-        nc.sync.dma_start(ws_raw[:], ws_words.rearrange("a p c i -> p a (c i)").bitcast(I32))
-        load_rows(mix_all[1], mix, 1)
-        place_ws_scales()
 
         gather_words(0, 0)
         for i in range(4):
@@ -173,6 +164,9 @@ def tile_list_ratio_mask_synthesis_kernel(
                 out=w4_w[0][:].rearrange("p a (i m e) -> p a i m e", i=4, e=2)[:, :, i],
                 in_=w4_raw[0][:].rearrange("p a (m i e) -> p a i m e", i=4, e=2)[:, :, i],
             )
+        nc.gpsimd.tensor_copy(
+            out=s_dealt[:].rearrange("p (i m) -> p i m", i=4), in_=s_raw[:].rearrange("p (m i) -> p i m", i=4)
+        )
         gather_words(1, 0, 0, BANK // 2)
         gather_words(1, 0, BANK // 2, BANK // 2)
         gather_words(0, 1)
@@ -181,6 +175,10 @@ def tile_list_ratio_mask_synthesis_kernel(
             out=w4_w[1][:].bitcast(U16).rearrange("p a (i m) -> p a i m", i=4),
             in_=w4_raw[1][:].bitcast(U16).rearrange("p a (m i) -> p a i m", i=4),
         )
+        ws_raw = shared("ws_raw", [P, 2, N], I32, "picked")
+        nc.sync.dma_start(ws_raw[:], ws_words.rearrange("a p c i -> p a (c i)").bitcast(I32))
+        load_rows(mix_all[1], mix, 1)
+        place_ws_scales()
 
         h = {(b, i): shared("h", [P, S], F32, f"h{b}_{i}") for b in range(2) for i in range(4)}
         x = [noise_all[0], rows(20 * M, M)]
@@ -247,7 +245,7 @@ def tile_list_ratio_mask_synthesis_kernel(
 
         def noise_pass(c, b, a):
             if a == 0:
-                noise_banks[c, b] = bank_tile(c, [P, PASS])
+                noise_banks[c, b] = bank_tile(c + 4 * b, [P, PASS])
             nc.tensor.matmul_mx(
                 out=noise_banks[c, b][:],
                 lhsT=noise_q[a][:, chunk_cols(c)].bitcast(E4M3),
@@ -265,7 +263,7 @@ def tile_list_ratio_mask_synthesis_kernel(
             )
 
         def square_speech(c, b):
-            bank = bank_tile(c + (4, 0)[b], [P, 4, P])
+            bank = bank_tile(c + 4, [P, 4, P])
             for i in range(4):
                 nc.tensor.transpose(bank[:, i, :], x[b][:, i, chunk_cols(c)], identity[:])
             if b == 0 and c >= 2:
@@ -282,7 +280,7 @@ def tile_list_ratio_mask_synthesis_kernel(
                 )
 
         def open_sum(c, b):
-            sums[c, b] = bank_tile(4 + c, [P, 4, P])
+            sums[c, b] = bank_tile(c + 4 * (1 - b), [P, 4, P])
             add_turned(c, b, (speech_power, noise_power)[b][c, b], True)
 
         def close_sum(c, b):
@@ -344,7 +342,8 @@ def tile_list_ratio_mask_synthesis_kernel(
 
         def store_y(c, g):
             nc.scalar.copy(out=y_sb[c, g], in_=y_banks[c, g][:])
-            nc.sync.dma_start(
+            queue = nc.scalar if (c, g) == units[-1] else nc.sync
+            queue.dma_start(
                 out_0[PASS * g : PASS * (g + 1), chunk_cols(c)].rearrange("(p t) m -> p t m", t=4), y_sb[c, g]
             )
 
@@ -412,14 +411,16 @@ def tile_list_ratio_mask_synthesis_kernel(
                 noise_pass(c, 1, a)
             square_noise(c, 1)
         for c in range(CHUNKS):
-            open_sum(c, 1)
             scale_speech(c, 0)
+        open_sum(0, 1)
         deal_ws()
         for c in range(CHUNKS - 1):
             square_speech(c, 1)
         for n in range(len(units) + 2):
             if n < CHUNKS:
                 close_sum(n, 1)
+            if n + 1 < CHUNKS:
+                open_sum(n + 1, 1)
             if n < len(units):
                 square_ratio(*units[n])
             if n == 0:
@@ -430,11 +431,10 @@ def tile_list_ratio_mask_synthesis_kernel(
                 round_z(*units[n - 1])
             if n >= 2:
                 synthesise(*units[n - 2])
-            if n in (4, 6):
-                store_y(0, n // 2 - 2)
-        for c in range(1, CHUNKS):
-            for g in range(2):
-                store_y(c, g)
+            if n >= 4:
+                store_y(*units[n - 4])
+        for g in range(2):
+            store_y(CHUNKS - 1, g)
         for c in range(CHUNKS):
             for step in (round_y, quantise_y):
                 for g in range(2):

from contextlib import ExitStack

import concourse.mybir as mybir
from concourse.masks import make_identity

K, H, N, T, S, M = 1024, 1024, 1024, 2048, 1024, 512
P = 128
PASS = 512
BANK = 512
HALF = M // 2
CHUNKS = M // P
FLOPS = 2 * K * H * S + 2 * K * H * M + 2 * H * N * M

F32 = mybir.dt.float32
BF16 = mybir.dt.bfloat16
I32 = mybir.dt.int32
U32 = mybir.dt.uint32
U16 = mybir.dt.uint16
U8 = mybir.dt.uint8
E4M3 = mybir.dt.float8_e4m3fn_x4
E2M1 = mybir.dt.float4_e2m1fn_x4
ACT = mybir.ActivationFunctionType
ALU = mybir.AluOpType


def tile_list_ratio_mask_synthesis_kernel(
    tc, tab_words, tab_scales, offs, w4_words, w4_scales, offs2, wgt, noise, wn, mix, ws_words, ws_scales,
    out_0, out_1, out_2,
):
    nc = tc.nc
    on_vector, on_scalar = nc.vector.tensor_copy, nc.scalar.copy
    units = [(c, b) for c in range(CHUNKS) for b in range(2)]

    with ExitStack() as ctx:
        keep = ctx.enter_context(tc.tile_pool(name="keep", bufs=1))
        rounded = ctx.enter_context(tc.tile_pool(name="rounded", bufs=4))
        turned = ctx.enter_context(tc.tile_pool(name="turned", bufs=CHUNKS))
        psum = ctx.enter_context(tc.psum_pool(name="psum", bufs=1))

        def kept(name, shape, dtype):
            return keep.tile(shape, dtype, name=name, align_bytes=64)

        def shared(name, shape, dtype, tag):
            return keep.tile(shape, dtype, name=name, tag=tag, align_bytes=64)

        def rounded_tile(width):
            return rounded.tile([P, width, 4], BF16, name="rounded", tag="rounded", align_bytes=64)

        def bank_tile(number, shape):
            return psum.tile(shape, F32, name="bank", tag=f"bank{number}")

        def chunk_cols(c):
            return slice(P * c, P * (c + 1))

        idx = keep.tile([P, S // 16], U16, name="idx")
        idx2 = keep.tile([P, M // 16], U16, name="idx2")
        tab_s = kept("tab_s", [P, T], U8)
        w4_s = shared("w4_s", [P, 2, H], U8, "late")
        s_raw = kept("s_raw", [P, PASS], U8)
        s_dealt = kept("s_dealt", [P, PASS], U8)
        tab_w = [kept("tab_w0", [P, T], I32)]
        w4_raw = [kept("w4_raw0", [P, 2, 2 * PASS], U8), None]
        w4_w = [kept(f"w4_w{b}", [P, 2, 2 * PASS], U8) for b in range(2)]
        w4_plane = kept("w4_plane", [P, 2, H], U8)
        ws_plane = kept("ws_plane", [P, 2, 2, PASS], U8)
        v_picked = shared("v_picked", [P, S], U8, "picked")
        v_s = kept("v_s", [P, 2, S], U8)
        v_w = [[shared("v_w", [P, BANK], U32, f"v_w{a}_{j}") for j in range(2)] for a in range(2)]
        floor = kept("floor", [P, 16], F32)

        nc.vector.memset(w4_s[:].rearrange("p a c -> p (a c)").bitcast(I32), 0)
        nc.vector.memset(tab_s[32:64, :].bitcast(I32), 0)
        nc.vector.memset(tab_s[64:P, :].bitcast(I32), 0)
        nc.vector.memset(floor[:, 0:1], 25.0)
        nc.vector.memset(v_s[:].rearrange("p a c -> p (a c)").bitcast(I32), 0)
        nc.vector.memset(s_raw[64:P, :].bitcast(I32), 0)
        nc.vector.memset(ws_plane[:].rearrange("p b a c -> p (b a c)").bitcast(I32), 0)
        identity = kept("identity", [P, P], F32)
        make_identity(nc, identity[:])
        mask_floor = floor[:, 8:9]
        nc.scalar.activation(out=mask_floor, in_=floor[:, 0:1], func=ACT.Abs_reciprocal_sqrt)

        def gather_words(a, j, first=0, width=BANK):
            entry = BANK * j + first
            nc.vector.tensor_copy(
                out=v_w[a][j][:, first : first + width],
                in_=tab_w[a][:].bitcast(U32).indirect(idx[:, entry // 16 : (entry + width) // 16]),
            )

        for a in range(2):
            nc.sync.dma_start(tab_s[a:32:2, :].bitcast(I32), tab_scales[a].rearrange("(q r) t -> r q t", r=4).bitcast(I32))
        nc.sync.dma_start(idx[:], offs)
        for r in range(4):
            nc.sync.dma_start(w4_s[r:P:32].bitcast(I32), w4_scales.rearrange("a (q r) c -> r q a c", r=4)[r].bitcast(I32))
        tab_w.append(kept("tab_w1", [P, T], I32))
        nc.sync.dma_start(tab_w[0][:], tab_words[0].rearrange("p t i -> p (t i)").bitcast(I32))
        w4_halves = w4_words.rearrange("a p (b c) -> b p a c", b=2)
        nc.sync.dma_start(w4_raw[0][:].bitcast(I32), w4_halves[0].bitcast(I32))
        nc.sync.dma_start(idx2[:], offs2)
        nc.sync.dma_start(tab_w[1][:], tab_words[1].rearrange("p t i -> p (t i)").bitcast(I32))
        nc.vector.tensor_copy(out=v_picked[:], in_=tab_s[:].indirect(idx[:]))

        def deal_w4_scales(b):
            half = slice(PASS * b, PASS * (b + 1))
            nc.gpsimd.tensor_copy(
                out=w4_plane[:, :, half].rearrange("p a (i m) -> p a i m", i=4),
                in_=w4_s[:, :, half].rearrange("p a (m i) -> p a i m", i=4),
            )

        for b in range(2):
            deal_w4_scales(b)
        for r in range(4):
            nc.sync.dma_start(
                v_s[r:P:32].rearrange("p a c -> p (a c)").bitcast(I32),
                v_picked[8 * r : 8 * r + 8, :].bitcast(I32),
            )

        for a in range(2):
            nc.sync.dma_start(s_raw[a:64:2, :].bitcast(I32), ws_scales[a].rearrange("q (b c) -> (q b) c", b=2).bitcast(I32))

        def place_ws_scales():
            for q in range(4):
                nc.sync.dma_start(
                    ws_plane[32 * q : 32 * q + 4].rearrange("p b a c -> p (b a c)").bitcast(I32),
                    s_dealt[16 * q : 16 * q + 16, :].bitcast(I32),
                )

        late = shared("late", [P, M + 4 * (2 * M + 2 * H + 2 * M)], F32, "late")
        wgt_sb = late[:, 0:M]

        def rows(first, width):
            return late[:, first : first + 4 * width].rearrange("p (j m) -> p j m", j=4)

        noise_all = [rows(M + 4 * M * a, M) for a in range(2)]
        wn_raw = {(a, b): rows(9 * M + 4 * PASS * (2 * a + b), PASS) for a in range(2) for b in range(2)}
        mix_all = [rows(25 * M + 4 * M * b, M) for b in range(2)]
        y_sb = {(c, g): rows((5 + 2 * c) * M + 4 * g * P, P) for c, g in units}

        def load_wn(a, b):
            nc.sync.dma_start(
                wn_raw[a, b],
                wn[PASS * a : PASS * (a + 1), PASS * b : PASS * (b + 1)].rearrange("(p j) c -> p j c", j=4),
            )

        def load_rows(tile, source, a):
            nc.sync.dma_start(tile, source[PASS * a : PASS * (a + 1), :].rearrange("(p j) m -> p j m", j=4))

        w4_raw[1] = shared("w4_raw1", [P, 2, 2 * PASS], U8, "picked")
        for half in range(2):
            cols = slice(HALF * half, HALF * (half + 1))
            nc.sync.dma_start(noise_all[0][:, :, cols], noise[0:PASS, cols].rearrange("(p j) m -> p j m", j=4))
        nc.sync.dma_start(w4_raw[1][:].bitcast(I32), w4_halves[1].bitcast(I32))
        nc.sync.dma_start(wgt_sb, wgt)
        load_wn(0, 0)
        load_rows(noise_all[1], noise, 1)
        load_wn(1, 0)
        for a in range(2):
            load_wn(a, 1)
        load_rows(mix_all[0], mix, 0)

        gather_words(0, 0)
        for i in range(4):
            nc.gpsimd.tensor_copy(
                out=w4_w[0][:].rearrange("p a (i m e) -> p a i m e", i=4, e=2)[:, :, i],
                in_=w4_raw[0][:].rearrange("p a (m i e) -> p a i m e", i=4, e=2)[:, :, i],
            )
        nc.gpsimd.tensor_copy(
            out=s_dealt[:].rearrange("p (i m) -> p i m", i=4), in_=s_raw[:].rearrange("p (m i) -> p i m", i=4)
        )
        gather_words(1, 0, 0, BANK // 2)
        gather_words(1, 0, BANK // 2, BANK // 2)
        gather_words(0, 1)
        gather_words(1, 1)
        nc.vector.tensor_copy(
            out=w4_w[1][:].bitcast(U16).rearrange("p a (i m) -> p a i m", i=4),
            in_=w4_raw[1][:].bitcast(U16).rearrange("p a (m i) -> p a i m", i=4),
        )
        ws_raw = shared("ws_raw", [P, 2, N], I32, "picked")
        nc.sync.dma_start(ws_raw[:], ws_words.rearrange("a p c i -> p a (c i)").bitcast(I32))
        load_rows(mix_all[1], mix, 1)
        place_ws_scales()

        h = {(b, i): shared("h", [P, S], F32, f"h{b}_{i}") for b in range(2) for i in range(4)}
        x = [noise_all[0], rows(20 * M, M)]
        ratio = [kept(f"ratio{b}", [P, 4, M], F32) for b in range(2)]

        def speech(number, b, i, j, first=0, width=BANK):
            col = PASS * b + P * i
            entries = slice(BANK * j + first, BANK * j + first + width)
            bank = bank_tile((number + 2) % 8, [P, width])
            for a in range(2):
                nc.tensor.matmul_mx(
                    out=bank[:],
                    lhsT=w4_w[b][:, a, 2 * P * i : 2 * P * (i + 1)].bitcast(E2M1),
                    lhsT_scale=w4_plane[:, a, col : col + P],
                    rhs=v_w[a][j][:, first : first + width].bitcast(E4M3),
                    rhs_scale=v_s[:, a, entries],
                    start=(a == 0),
                    stop=(a == 1),
                )
            nc.scalar.copy(out=h[b, i][:, entries], in_=bank[:])

        def pick(b, i):
            nc.vector.tensor_tensor(out=x[b][:, i, :], in0=h[b, i][:].indirect(idx2[:]), in1=wgt_sb, op=ALU.mult)

        noise_q = [kept(f"noise_q{a}", [P, M], U32) for a in range(2)]
        noise_s = [kept(f"noise_s{a}", [P, M], U8) for a in range(2)]
        wn_q = {(a, b): kept(f"wn_q{a}_{b}", [P, PASS], U32) for a in range(2) for b in range(2)}
        wn_s = {(a, b): kept(f"wn_s{a}_{b}", [P, PASS], U8) for a in range(2) for b in range(2)}

        def by_rows(tile):
            return tile.rearrange("p j (c e) -> p c j e", e=4)

        def by_words(tile):
            return tile.rearrange("p (c e) j -> p c j e", e=4)

        def quantise(codes, scales, words):
            nc.vector.quantize_mx(out=codes.bitcast(E4M3), scales=scales, in_=words)

        def round_noise(a, copy):
            words = rounded_tile(M)
            width = (HALF, M)[a]
            for first in range(0, M, width):
                cols = slice(first, first + width)
                copy(out=by_words(words[:, cols, :]), in_=by_rows(noise_all[a][:, :, cols]))
            return words

        def quantise_noise(a, words):
            quantise(noise_q[a][:], noise_s[a][:], words[:].rearrange("p m j -> p (m j)"))

        def round_wn(a, b, *copies):
            words = shared("middle", [P, PASS, 4], BF16, "middle") if a != b else rounded_tile(PASS)
            for pair, copy in enumerate(copies):
                slots = slice(2 * pair, 2 * pair + 2)
                copy(
                    out=words[:].rearrange("p (i m) j -> p m j i", i=4)[:, :, :, slots],
                    in_=wn_raw[a, b].rearrange("p j (m i) -> p m j i", i=4)[:, :, :, slots],
                )
            return words

        def quantise_wn(a, b, words):
            quantise(wn_q[a, b][:], wn_s[a, b][:], words[:].rearrange("p c j -> p (c j)"))

        noise_banks, noise_power, speech_power, sums = {}, {}, {}, {}

        def noise_pass(c, b, a):
            if a == 0:
                noise_banks[c, b] = bank_tile(c + 4 * b, [P, PASS])
            nc.tensor.matmul_mx(
                out=noise_banks[c, b][:],
                lhsT=noise_q[a][:, chunk_cols(c)].bitcast(E4M3),
                lhsT_scale=noise_s[a][:, chunk_cols(c)],
                rhs=wn_q[a, b][:].bitcast(E4M3),
                rhs_scale=wn_s[a, b][:],
                start=(a == 0),
                stop=(a == 1),
            )

        def square_noise(c, b):
            noise_power[c, b] = turned.tile([P, 4, P], F32, name="noise_power", align_bytes=64)[:]
            nc.scalar.activation(
                out=noise_power[c, b], in_=noise_banks[c, b][:].rearrange("m (i p) -> m i p", i=4), func=ACT.Square
            )

        def square_speech(c, b):
            bank = bank_tile(c + 4, [P, 4, P])
            for i in range(4):
                nc.tensor.transpose(bank[:, i, :], x[b][:, i, chunk_cols(c)], identity[:])
            if b == 0 and c >= 2:
                speech_power[c, b] = wn_raw[1, 0][:, c - 2, :].rearrange("p (i m) -> p i m", i=4)
            else:
                speech_power[c, b] = shared("speech_power", [P, 4, P], F32, f"h0_{c}")[:]
            nc.scalar.activation(out=speech_power[c, b], in_=bank[:], func=ACT.Square)

        def add_turned(c, b, term, opens):
            for i in range(4):
                nc.tensor.matmul(
                    sums[c, b][:, i, :], term[:, i, :], identity[:], is_transpose=True,
                    start=(opens and i == 0), stop=(not opens and i == 3),
                )

        def open_sum(c, b):
            sums[c, b] = bank_tile(c + 4 * (1 - b), [P, 4, P])
            add_turned(c, b, (speech_power, noise_power)[b][c, b], True)

        def close_sum(c, b):
            add_turned(c, b, (noise_power, speech_power)[b][c, b], False)
            nc.scalar.activation(
                out=ratio[b][:, :, chunk_cols(c)], in_=sums[c, b][:], func=ACT.Abs_reciprocal_sqrt, bias=mask_floor
            )

        def scale_speech(c, b):
            part = ratio[b][:, :, chunk_cols(c)]
            nc.vector.tensor_tensor(out=part, in0=x[b][:, :, chunk_cols(c)], in1=part, op=ALU.mult)

        mask = {}

        def square_ratio(c, b):
            part = ratio[b][:, :, chunk_cols(c)]
            mask[c, b] = shared("mask", [P, 4, P], F32, f"h0_{c}")[:] if b == 0 else part
            nc.scalar.activation(out=mask[c, b], in_=part, func=ACT.Square)

        z_q = [kept(f"z_q{b}", [P, M], U32) for b in range(2)]
        z_s = [kept(f"z_s{b}", [P, M], U8) for b in range(2)]
        z_words = {}

        def round_z(c, b):
            z_words[c, b] = rounded_tile(P)
            nc.vector.tensor_tensor(
                out=by_words(z_words[c, b][:]), in0=by_rows(mix_all[b][:, :, chunk_cols(c)]), in1=by_rows(mask[c, b]),
                op=ALU.mult,
            )

        ws_w = shared("ws_w", [P, 2, N], I32, "h1_3")
        y_s = kept("y_s", [P, M], U8)
        y_q = [kept(f"y_q{half}", [P, 2, HALF], I32) for half in range(2)]
        y_banks, y_words = {}, {}

        def deal_ws():
            nc.vector.tensor_copy(
                out=ws_w[:].rearrange("p b (g t m) -> p (b g) m t", g=2, t=4),
                in_=ws_raw[:].rearrange("p b (g m t) -> p (b g) m t", g=2, t=4),
            )

        def synthesise(c, b):
            cols = chunk_cols(c)
            quantise(z_q[b][:, cols], z_s[b][:, cols], z_words[c, b][:].rearrange("p m i -> p (m i)"))
            for g in range(2):
                if b == 0:
                    y_banks[c, g] = bank_tile(2 * c + g, [P, 4, P])
                for t in range(4):
                    col = PASS * g + P * t
                    nc.tensor.matmul_mx(
                        out=y_banks[c, g][:, t, :],
                        lhsT=ws_w[:, b, col : col + P].bitcast(E4M3),
                        lhsT_scale=ws_plane[:, g, b, P * t : P * (t + 1)],
                        rhs=z_q[b][:, cols].bitcast(E4M3),
                        rhs_scale=z_s[b][:, cols],
                        start=(b == 0 and t == 0),
                        stop=(b == 1 and t == 3),
                    )

        def store_y(c, g):
            nc.scalar.copy(out=y_sb[c, g], in_=y_banks[c, g][:])
            queue = nc.scalar if (c, g) == units[-1] else nc.sync
            queue.dma_start(
                out_0[PASS * g : PASS * (g + 1), chunk_cols(c)].rearrange("(p t) m -> p t m", t=4), y_sb[c, g]
            )

        def round_y(c, g):
            y_words[c, g] = rounded_tile(P)
            nc.vector.tensor_copy(out=by_words(y_words[c, g][:]), in_=by_rows(y_sb[c, g]))

        def quantise_y(c, g):
            quantise(
                y_q[c // 2][:, g, chunk_cols(c % 2)], y_s[4 * g : P, chunk_cols(c)],
                y_words[c, g][:].rearrange("p m t -> p (m t)"),
            )

        idle_bank = bank_tile(1, [P, BANK])
        for turn in range(4):
            nc.tensor.matmul_mx(
                out=idle_bank[:],
                lhsT=w4_raw[0][:, 0, 0 : 2 * P].bitcast(E2M1),
                lhsT_scale=w4_plane[:, 0, 0:P],
                rhs=v_w[0][0][:].bitcast(E4M3),
                rhs_scale=w4_plane[:, 0, 0:BANK],
                start=True,
                stop=True,
            )
        first_noise = round_noise(0, on_vector)
        for quarter in range(2):
            for i in range(2):
                speech(2 * quarter + i, 0, i, 0, quarter * BANK // 2, BANK // 2)
        for i in range(2, 4):
            speech(2 + i, 0, i, 0)
        for i in range(4):
            speech(6 + i, 0, i, 1)
            pick(0, i)
        for i in range(4):
            for j in range(2):
                speech(10 + 2 * i + j, 1, i, j)
        first_wn = round_wn(0, 0, on_vector, on_vector)
        quantise_noise(0, first_noise)
        second_noise = round_noise(1, on_vector)
        quantise_wn(0, 0, first_wn)
        second_wn = round_wn(1, 0, on_scalar, on_scalar)
        quantise_noise(1, second_noise)
        quantise_wn(1, 0, second_wn)
        for c in range(CHUNKS):
            square_speech(c, 0)
        for c in range(CHUNKS):
            noise_pass(c, 0, 0)
        for c in range(2):
            open_sum(c, 0)
        third_wn = round_wn(0, 1, on_scalar, on_vector)
        last_wn = round_wn(1, 1, on_vector, on_vector)
        quantise_wn(0, 1, third_wn)
        quantise_wn(1, 1, last_wn)
        for i in range(4):
            pick(1, i)
        for c in range(CHUNKS):
            noise_pass(c, 0, 1)
            square_noise(c, 0)
        for c in range(2, CHUNKS):
            open_sum(c, 0)
        for c in range(CHUNKS):
            close_sum(c, 0)
        for c in range(CHUNKS):
            for a in range(2):
                noise_pass(c, 1, a)
            square_noise(c, 1)
        for c in range(CHUNKS):
            scale_speech(c, 0)
        open_sum(0, 1)
        deal_ws()
        for c in range(CHUNKS - 1):
            square_speech(c, 1)
        for n in range(len(units) + 2):
            if n < CHUNKS:
                close_sum(n, 1)
            if n + 1 < CHUNKS:
                open_sum(n + 1, 1)
            if n < len(units):
                square_ratio(*units[n])
            if n == 0:
                square_speech(CHUNKS - 1, 1)
            if n < CHUNKS:
                scale_speech(n, 1)
            if 1 <= n <= len(units):
                round_z(*units[n - 1])
            if n >= 2:
                synthesise(*units[n - 2])
            if n >= 4:
                store_y(*units[n - 4])
        for g in range(2):
            store_y(CHUNKS - 1, g)
        for c in range(CHUNKS):
            for step in (round_y, quantise_y):
                for g in range(2):
                    step(c, g)
            if c % 2 == 1:
                cols = slice(HALF * (c // 2), HALF * (c // 2 + 1))
                nc.sync.dma_start(out_1[:, :, cols, :].rearrange("g p m t -> p g (m t)").bitcast(I32), y_q[c // 2][:])
        for q in range(4):
            (nc.scalar, nc.sync)[q % 2].dma_start(
                out_2[:, 4 * q : 4 * q + 4, :].bitcast(I32), y_s[32 * q : 32 * q + 8, :].bitcast(I32)
            )
